import numpy as np
import ml_dtypes


def mxq(x, axis, fmt="e4m3"):
    dtype, down = {"e4m3": (ml_dtypes.float8_e4m3fn, 7), "e5m2": (ml_dtypes.float8_e5m2, 14)}[fmt]
    v = np.moveaxis(np.asarray(x, np.float32).astype(ml_dtypes.bfloat16).astype(np.float64), axis, -1)
    blocks = v.reshape(v.shape[:-1] + (-1, 32))
    amax = np.abs(blocks).max(-1, keepdims=True)
    byte = np.maximum(np.where(amax > 0, np.frexp(amax)[1] - 1 + 127, 0) - down, 1)
    scale = np.exp2(byte - 127.0)
    codes = (blocks / scale).astype(np.float32).astype(dtype).astype(np.float64)
    return np.moveaxis((codes * scale).reshape(v.shape), -1, axis)


WIDE = False


def mx_kscale(k):
    if not WIDE:
        return np.ones(k)
    levels = np.array([10, -10, 5, -5, 0])
    if k % 512:
        return np.exp2(np.random.permutation(np.resize(levels, k // 32))).repeat(32)
    a = np.empty((k // 512, 16))
    for p in range(k // 512):
        a[p, :8] = np.random.permutation(np.resize(levels, 8))
        for g in range(8):
            far = levels[np.abs(levels - a[p, g]) >= 10]
            a[p, g + 8] = far[np.random.randint(len(far))]
    return np.exp2(a.ravel()).repeat(32)


def f64(x):
    return np.asarray(x).astype(np.float64)


def striped(idx):
    return np.tile(idx.reshape(-1, 16).T, (8, 1)).astype(np.uint16)


def unstriped(offs):
    return offs[:16].T.reshape(-1).astype(np.int64)


E2M1 = np.array([0.0, 0.5, 1.0, 1.5, 2.0, 3.0, 4.0, 6.0, -0.0, -0.5, -1.0, -1.5, -2.0, -3.0, -4.0, -6.0])


def pack_weight(w, fmt):
    k, n = w.shape
    w = f64(np.asarray(w, np.float32).astype(ml_dtypes.bfloat16)).reshape(k // 32, 32, n)
    amax = np.abs(w).max(1)
    if fmt == "e4m3":
        byte = np.frexp(amax)[1] - 1 + 127 - 7
    else:
        mant, ex = np.frexp(amax / 6.0)
        byte = np.where(mant > 0.5, ex, ex - 1) + 127
    byte = np.clip(np.where(amax > 0, byte, 1), 1, 254)
    scaled = (w * np.exp2(127.0 - byte)[:, None, :]).reshape(k, n).astype(np.float32)
    by_word = np.ascontiguousarray(scaled.reshape(k // 512, 128, 4, n).transpose(0, 1, 3, 2))
    if fmt == "e4m3":
        words = by_word.astype(ml_dtypes.float8_e4m3fn).view(np.uint8)
    else:
        c = by_word.astype(ml_dtypes.float4_e2m1fn).view(np.uint8) & 0xF
        words = (c[..., 0::2] | (c[..., 1::2] << 4)).reshape(k // 512, 128, 2 * n)
    return np.ascontiguousarray(words), np.ascontiguousarray(byte.astype(np.uint8).reshape(k // 512, 16, n))


def unpack_weight(words, scales, fmt):
    g, _, n = scales.shape
    words = np.ascontiguousarray(words).reshape(g, 128, n, -1)
    if fmt == "e4m3":
        vals = words.view(ml_dtypes.float8_e4m3fn).astype(np.float64)
    else:
        nib = np.empty((g, 128, n, 4), np.uint8)
        nib[..., 0::2] = words & 0xF
        nib[..., 1::2] = words >> 4
        vals = E2M1[nib]
    vals = vals * np.repeat(np.exp2(scales.astype(np.float64) - 127.0), 8, axis=1)[..., None]
    return vals.transpose(0, 1, 3, 2).reshape(g * 512, n)


def gelu(v):
    return 0.5 * v * (1.0 + np.tanh(np.sqrt(2.0 / np.pi) * (v + 0.044715 * v**3)))


K, K2, H, N, T, T2, S = 1024, 512, 1024, 512, 4096, 2048, 1024

def setup_inputs():
    n = np.random.standard_normal
    s = mx_kscale(K)[:, None]
    s2 = mx_kscale(K2)[:, None]
    u = mx_kscale(H)[:, None]
    tab_words, tab_scales = pack_weight(n((K, T)) * s, "e4m3")
    tab2_words, tab2_scales = pack_weight(n((K2, T2)) * s2, "e4m3")
    wd_words, wd_scales = pack_weight(n((K, H)) / np.sqrt(K) / s * u.T, "e2m1")
    wc_words, wc_scales = pack_weight(n((H, N)) / np.sqrt(H) / u, "e4m3")
    return {
        "tab_words": tab_words, "tab_scales": tab_scales,
        "tab2_words": tab2_words, "tab2_scales": tab2_scales,
        "offs": striped(np.random.permutation(T)[:S]),
        "offs2": striped(np.random.permutation(T2)[:S]),
        "wd_words": wd_words, "wd_scales": wd_scales,
        "ws": (n((K2, H)) / np.sqrt(K2) / s2 * u.T).astype(np.float32),
        "safety": (0.5 * np.exp(0.3 * n(H)) * u[:, 0]).astype(np.float32),
        "wc_words": wc_words, "wc_scales": wc_scales,
        "base": (0.5 * n(N)).astype(np.float32),
    }

def reference(tab_words, tab_scales, tab2_words, tab2_scales, offs, offs2,
              wd_words, wd_scales, ws, safety, wc_words, wc_scales, base):
    v = unpack_weight(tab_words, tab_scales, "e4m3")[:, unstriped(offs)]
    v2 = unpack_weight(tab2_words, tab2_scales, "e4m3")[:, unstriped(offs2)]
    wd = unpack_weight(wd_words, wd_scales, "e2m1")
    wc = unpack_weight(wc_words, wc_scales, "e4m3")
    demand = wd.T @ v
    stock = mxq(f64(ws), 0, "e4m3").T @ v2
    h = np.maximum(demand - stock + f64(safety)[:, None], 0.0)
    y = wc.T @ mxq(h, 0, "e4m3")
    return y + f64(base)[:, None]

@@ -1,0 +1,272 @@
+from contextlib import ExitStack
+
+import concourse.mybir as mybir
+
+K, K2, H, N, T, T2, S = 1024, 512, 1024, 512, 4096, 2048, 1024
+FLOPS = 2 * S * (K * H + K2 * H + H * N)
+
+F32 = mybir.dt.float32
+BF16 = mybir.dt.bfloat16
+I32 = mybir.dt.int32
+U32 = mybir.dt.uint32
+U16 = mybir.dt.uint16
+U8 = mybir.dt.uint8
+FP8X4 = mybir.dt.float8_e4m3fn_x4
+FP4X4 = mybir.dt.float4_e2m1fn_x4
+ALU = mybir.AluOpType
+ACT = mybir.ActivationFunctionType
+
+P = 128
+PACK = 4
+K_PASS = P * PACK
+HALF = 512
+LIST_ROWS = 16
+QUADS = 4
+STOCK_ROW = 4
+COST_ROW = 8
+
+
+def tile_list_supplier_shortage_cost_kernel(
+    tc, tab_words, tab_scales, tab2_words, tab2_scales, offs, offs2,
+    wd_words, wd_scales, ws, safety, wc_words, wc_scales, base, out,
+):
+    nc = tc.nc
+    with ExitStack() as ctx:
+        keep = ctx.enter_context(tc.tile_pool(name="keep", bufs=1))
+        ring = ctx.enter_context(tc.tile_pool(name="ring", bufs=4))
+        outs = ctx.enter_context(tc.tile_pool(name="outs", bufs=8))
+        psum = ctx.enter_context(tc.psum_pool(name="psum", bufs=8))
+
+        def held(name, shape, dtype):
+            return keep.tile(shape, dtype, name=name, align_bytes=256)
+
+        idx = keep.tile([P, S // LIST_ROWS], U16, name="idx")
+        idx2 = keep.tile([P, S // LIST_ROWS], U16, name="idx2")
+        v_table = [held("v_table%d" % g, [P, T], I32) for g in range(2)]
+        v2_table = held("v2_table", [P, T2], I32)
+        v_scale_table = held("v_scale_table", [P, T // 4], I32)
+        v2_scale_table = held("v2_scale_table", [P, T2 // 4], I32)
+        wd_raw = held("wd_raw", [P, 2, H // 2], I32)
+        wd_scale_raw = held("wd_scale_raw", [P, 2, H // 4], I32)
+        wc_codes = held("wc_codes", [P, 2, N], I32)
+        wc_planes = held("wc_planes", [P, 2, N // 4], I32)
+        v_planes = [held("v_plane%d" % g, [P, S // 4], I32) for g in range(2)]
+        ws_raw = [held("ws_raw%d" % a, [P, PACK, K_PASS], F32) for a in range(2)]
+        safety_sb = held("safety_sb", [P, 2, PACK], F32)
+        base_sb = held("base_sb", [P, N // P], F32)
+        warm = held("warm", [P, 2], F32)
+
+        nc.vector.memset(v_scale_table[:], 0)
+        nc.vector.memset(wd_scale_raw[:], 0)
+        nc.vector.memset(v2_scale_table[:], 0)
+        for g in range(2):
+            nc.vector.memset(v_planes[g][:], 0)
+        nc.vector.memset(wc_planes[:], 0)
+
+        def words(ap):
+            return ap.rearrange("p t i -> p (t i)").bitcast(I32)
+
+        def ws_half(a):
+            return ws[:, a * K_PASS : (a + 1) * K_PASS].rearrange("(p j) c -> p j c", j=PACK)
+
+        nc.sync.dma_start(idx[:], offs)
+        nc.sync.dma_start(wd_raw[:], wd_words.bitcast(I32).rearrange("g p w -> p g w"))
+        nc.gpsimd.dma_start(v_table[0][:], words(tab_words[0]))
+        nc.gpsimd.dma_start(ws_raw[0][:], ws_half(0))
+        nc.gpsimd.dma_start(v_table[1][:], words(tab_words[1]))
+        nc.gpsimd.dma_start(v2_table[:], words(tab2_words[0]))
+        nc.gpsimd.dma_start(ws_raw[1][:], ws_half(1))
+        nc.gpsimd.dma_start(wc_codes[:], wc_words.rearrange("a p c i -> p a (c i)").bitcast(I32))
+        nc.sync.dma_start(v_scale_table[0:P:4, :], tab_scales.bitcast(I32).rearrange("g q w -> (g q) w"))
+        nc.sync.dma_start(idx2[:], offs2)
+        for q in range(QUADS):
+            nc.sync.dma_start(
+                wd_scale_raw[32 * q : 32 * q + 4, :, :],
+                wd_scales[:, 4 * q : 4 * q + 4, :].bitcast(I32).rearrange("g r w -> r g w"),
+            )
+        for q in range(QUADS):
+            nc.scalar.dma_start(
+                v2_scale_table[32 * q + STOCK_ROW : 32 * q + STOCK_ROW + 4, :],
+                tab2_scales[0, 4 * q : 4 * q + 4, :].bitcast(I32),
+            )
+        nc.scalar.dma_start(safety_sb[:], safety.rearrange("(a p t) -> p a t", a=2, t=PACK))
+        with nc.allow_non_contiguous_dma(reason="one value of base for each partition"):
+            nc.scalar.dma_start(base_sb[:], base.rearrange("(i p) -> p i", p=P))
+        for q in range(QUADS):
+            nc.scalar.dma_start(
+                wc_planes[32 * q + COST_ROW : 32 * q + COST_ROW + 4, :, :],
+                wc_scales[:, 4 * q : 4 * q + 4, :].bitcast(I32).rearrange("a r w -> r a w"),
+            )
+
+        v_scale_picked = held("v_scale_picked", [P, S], U8)
+        nc.vector.tensor_copy(v_scale_picked[:], v_scale_table[:].bitcast(U8).indirect(idx[:]))
+        for g in range(2):
+            for r in range(4):
+                first = 64 * g + 4 * r
+                nc.sync.dma_start(
+                    v_planes[g][r:P:32, :],
+                    v_scale_picked[first : 64 * g + 64 : 16, :].bitcast(I32),
+                )
+
+        wd_codes = held("wd_codes", [P, 4, PACK, P], U16)
+        nc.vector.tensor_copy(
+            wd_codes[:],
+            wd_raw[:].bitcast(U16).rearrange("p g (a m t) -> p (g a) t m", a=2, t=PACK),
+        )
+        wd_planes = held("wd_planes", [P, 4, PACK, P], U8)
+        nc.vector.tensor_copy(
+            wd_planes[:],
+            wd_scale_raw[:].bitcast(U8).rearrange("p g (a m t) -> p (g a) t m", a=2, t=PACK),
+        )
+
+        ws_codes = [held("ws_codes%d" % a, [P, K_PASS], U32) for a in range(2)]
+        ws_planes = [held("ws_plane%d" % a, [P, K_PASS], U8) for a in range(2)]
+        ws_bf = [held("ws_bf%d" % a, [P, PACK, P, PACK], BF16) for a in range(2)]
+
+        def ws_views(a):
+            return (
+                ws_bf[a][:].rearrange("p t m j -> p m t j"),
+                ws_raw[a][:].rearrange("p j (m t) -> p m t j", t=PACK),
+            )
+
+        def quantize_ws(a):
+            nc.vector.quantize_mx(
+                out=ws_codes[a][:].bitcast(FP8X4),
+                scales=ws_planes[a][:],
+                in_=ws_bf[a][:].rearrange("p t m j -> p (t m j)"),
+            )
+
+        def list_cols(h):
+            return slice(h * HALF // LIST_ROWS, (h + 1) * HALF // LIST_ROWS)
+
+        v_codes = [[held("v_codes%d_%d" % (g, h), [P, HALF], U32) for h in range(2)] for g in range(2)]
+        v2_codes = [held("v2_codes%d" % h, [P, HALF], U32) for h in range(2)]
+        v2_plane = held("v2_plane", [P, S], U8)
+
+        def gather_v(g, h):
+            nc.vector.tensor_copy(v_codes[g][h][:], v_table[g][:].bitcast(U32).indirect(idx[:, list_cols(h)]))
+
+        def gather_v2(h):
+            nc.vector.tensor_copy(v2_codes[h][:], v2_table[:].bitcast(U32).indirect(idx2[:, list_cols(h)]))
+
+        def demand_pass(acc, g, a, t, h):
+            nc.tensor.matmul_mx(
+                out=acc[:],
+                lhsT=wd_codes[:, 2 * g + a, t, :].bitcast(U8).bitcast(FP4X4),
+                lhsT_scale=wd_planes[:, 2 * g + a, t, :],
+                rhs=v_codes[g][h][:].bitcast(FP8X4),
+                rhs_scale=v_planes[g][:].bitcast(U8)[:, h * HALF : (h + 1) * HALF],
+                start=(g == 0),
+                stop=False,
+            )
+
+        def stock_pass(acc, a, t, h):
+            nc.tensor.matmul_mx(
+                out=acc[:],
+                lhsT=ws_codes[a][:, t * P : (t + 1) * P].bitcast(FP8X4),
+                lhsT_scale=ws_planes[a][:, t * P : (t + 1) * P],
+                rhs=v2_codes[h][:].bitcast(FP8X4),
+                rhs_scale=v2_plane[STOCK_ROW:P, h * HALF : (h + 1) * HALF],
+                start=False,
+                stop=True,
+            )
+
+        def new_acc():
+            return psum.tile([P, HALF], F32, name="acc")
+
+        def new_rows():
+            return ring.tile([P, PACK, HALF], BF16, name="h_rows", align_bytes=256)
+
+        def shortage(rows, acc, a, t):
+            nc.scalar.activation(rows[:, t, :], acc[:], ACT.Relu, bias=safety_sb[:, a, t : t + 1])
+
+        h_codes = [[held("h_codes%d_%d" % (a, h), [P, HALF], U32) for h in range(2)] for a in range(2)]
+        h_planes = [[held("h_plane%d_%d" % (a, h), [P, HALF], U8) for h in range(2)] for a in range(2)]
+
+        def quantize_h(rows, a, h):
+            grouped = ring.tile([P, HALF, PACK], BF16, name="h_grouped", align_bytes=256)
+            nc.vector.tensor_copy(
+                grouped[:].rearrange("p (c i) t -> p c t i", i=4),
+                rows[:].rearrange("p t (c i) -> p c t i", i=4),
+            )
+            nc.vector.quantize_mx(
+                out=h_codes[a][h][:].bitcast(FP8X4),
+                scales=h_planes[a][h][:],
+                in_=grouped[:].rearrange("p c t -> p (c t)"),
+            )
+
+        def cost_pass(acc, a, i, h):
+            nc.tensor.matmul_mx(
+                out=acc[:],
+                lhsT=wc_codes[:, a, i * P : (i + 1) * P].bitcast(FP8X4),
+                lhsT_scale=wc_planes[COST_ROW:P, a, :].bitcast(U8)[:, i * P : (i + 1) * P],
+                rhs=h_codes[a][h][:].bitcast(FP8X4),
+                rhs_scale=h_planes[a][h][:],
+                start=(a == 0),
+                stop=(a == 1),
+            )
+
+        def emit(acc, i, h, on_vector):
+            result = outs.tile([P, HALF], F32, name="result")
+            if on_vector:
+                nc.vector.tensor_scalar(result[:], acc[:], base_sb[:, i : i + 1], None, ALU.add)
+            else:
+                nc.scalar.activation(result[:], acc[:], ACT.Identity, bias=base_sb[:, i : i + 1])
+            nc.sync.dma_start(out[i * P : (i + 1) * P, h * HALF : (h + 1) * HALF], result[:])
+
+        nc.vector.memset(warm[:, 0:1], 0.0)
+        nc.scalar.activation(warm[:, 1:2], warm[:, 0:1], ACT.Relu)
+        accs = [[new_acc() for t in range(PACK)] for h in range(2)]
+        for h in range(2):
+            gather_v(0, h)
+            for t in range(PACK):
+                demand_pass(accs[h][t], 0, 0, t, h)
+        dst, src = ws_views(0)
+        nc.scalar.activation(dst, src, ACT.Copy, scale=-1.0)
+        nc.vector.tensor_copy(v2_plane[:], v2_scale_table[:].bitcast(U8).indirect(idx2[:]))
+        quantize_ws(0)
+        for h in range(2):
+            gather_v(1, h)
+            for t in range(PACK):
+                demand_pass(accs[h][t], 1, 0, t, h)
+        rows0 = [new_rows() for h in range(2)]
+        for h in range(2):
+            gather_v2(h)
+            for t in range(PACK):
+                stock_pass(accs[h][t], 0, t, h)
+                shortage(rows0[h], accs[h][t], 0, t)
+        dst, src = ws_views(1)
+        nc.vector.tensor_scalar(dst, src, -1.0, None, ALU.mult)
+        quantize_ws(1)
+        quantize_h(rows0[0], 0, 0)
+
+        accs10 = [new_acc() for t in range(PACK)]
+        for t in range(PACK):
+            for g in range(2):
+                demand_pass(accs10[t], g, 1, t, 0)
+        quantize_h(rows0[1], 0, 1)
+        rows10 = new_rows()
+        for t in range(PACK):
+            stock_pass(accs10[t], 1, t, 0)
+            shortage(rows10, accs10[t], 1, t)
+        quantize_h(rows10, 1, 0)
+        rows11 = new_rows()
+        for t in range(PACK):
+            acc = new_acc()
+            for g in range(2):
+                demand_pass(acc, g, 1, t, 1)
+            stock_pass(acc, 1, t, 1)
+            shortage(rows11, acc, 1, t)
+        quantize_h(rows11, 1, 1)
+
+        for i in range(N // P):
+            acc = new_acc()
+            for a in range(2):
+                cost_pass(acc, a, i, 0)
+            emit(acc, i, 0, False)
+        accs = [new_acc() for i in range(N // P)]
+        for i in range(N // P):
+            cost_pass(accs[i], 0, i, 1)
+        for i in range(N // P):
+            cost_pass(accs[i], 1, i, 1)
+            emit(accs[i], i, 1, i % 2 == 1)

@@ -22,8 +22,11 @@ K_PASS = P * PACK
 HALF = 512
 LIST_ROWS = 16
 QUADS = 4
+TOP = 96
+TOP2 = 112
 STOCK_ROW = 4
 COST_ROW = 8
+KIB = 1024
 
 
 def tile_list_supplier_shortage_cost_kernel(
@@ -33,35 +36,31 @@ def tile_list_supplier_shortage_cost_kernel(
     nc = tc.nc
     with ExitStack() as ctx:
         keep = ctx.enter_context(tc.tile_pool(name="keep", bufs=1))
+        placed = ctx.enter_context(tc.tile_pool(name="placed", bufs=1))
         ring = ctx.enter_context(tc.tile_pool(name="ring", bufs=4))
         outs = ctx.enter_context(tc.tile_pool(name="outs", bufs=8))
-        psum = ctx.enter_context(tc.psum_pool(name="psum", bufs=8))
+        psum = ctx.enter_context(tc.psum_pool(name="psum", bufs=1))
 
         def held(name, shape, dtype):
             return keep.tile(shape, dtype, name=name, align_bytes=256)
 
+        def at(kib, name, shape, dtype):
+            return placed.tile(shape, dtype, name=name, align_bytes=256, offset=kib * KIB)
+
         idx = keep.tile([P, S // LIST_ROWS], U16, name="idx")
         idx2 = keep.tile([P, S // LIST_ROWS], U16, name="idx2")
-        v_table = [held("v_table%d" % g, [P, T], I32) for g in range(2)]
-        v2_table = held("v2_table", [P, T2], I32)
         v_scale_table = held("v_scale_table", [P, T // 4], I32)
-        v2_scale_table = held("v2_scale_table", [P, T2 // 4], I32)
-        wd_raw = held("wd_raw", [P, 2, H // 2], I32)
-        wd_scale_raw = held("wd_scale_raw", [P, 2, H // 4], I32)
-        wc_codes = held("wc_codes", [P, 2, N], I32)
-        wc_planes = held("wc_planes", [P, 2, N // 4], I32)
-        v_planes = [held("v_plane%d" % g, [P, S // 4], I32) for g in range(2)]
-        ws_raw = [held("ws_raw%d" % a, [P, PACK, K_PASS], F32) for a in range(2)]
-        safety_sb = held("safety_sb", [P, 2, PACK], F32)
-        base_sb = held("base_sb", [P, N // P], F32)
+        wd_scale_raw = held("wd_scale_raw", [P, H // 4], I32)
+        v2_table = held("v2_table", [P, T2], I32)
+        v2_scale_picked = held("v2_scale_picked", [P, S], U8)
+        planes = held("planes", [P, 2, (S + H) // 4], I32)
+        v2_plane = held("v2_plane", [P, S // 4], I32)
         warm = held("warm", [P, 2], F32)
 
-        nc.vector.memset(v_scale_table[:], 0)
-        nc.vector.memset(wd_scale_raw[:], 0)
-        nc.vector.memset(v2_scale_table[:], 0)
-        for g in range(2):
-            nc.vector.memset(v_planes[g][:], 0)
-        nc.vector.memset(wc_planes[:], 0)
+        v2_scale_table = at(0, "v2_scale_table", [P, T2 // 4], I32)
+        v_scale_picked = at(31, "v_scale_picked", [P, 2 * S], U8)
+        stage_bytes = at(33, "stage", [P, 4 * KIB], I32)
+        stage = stage_bytes[:, : (S + H) // 4]
 
         def words(ap):
             return ap.rearrange("p t i -> p (t i)").bitcast(I32)
@@ -69,55 +68,77 @@ def tile_list_supplier_shortage_cost_kernel(
         def ws_half(a):
             return ws[:, a * K_PASS : (a + 1) * K_PASS].rearrange("(p j) c -> p j c", j=PACK)
 
-        nc.sync.dma_start(idx[:], offs)
-        nc.sync.dma_start(wd_raw[:], wd_words.bitcast(I32).rearrange("g p w -> p g w"))
-        nc.gpsimd.dma_start(v_table[0][:], words(tab_words[0]))
-        nc.gpsimd.dma_start(ws_raw[0][:], ws_half(0))
-        nc.gpsimd.dma_start(v_table[1][:], words(tab_words[1]))
-        nc.gpsimd.dma_start(v2_table[:], words(tab2_words[0]))
-        nc.gpsimd.dma_start(ws_raw[1][:], ws_half(1))
-        nc.gpsimd.dma_start(wc_codes[:], wc_words.rearrange("a p c i -> p a (c i)").bitcast(I32))
-        nc.sync.dma_start(v_scale_table[0:P:4, :], tab_scales.bitcast(I32).rearrange("g q w -> (g q) w"))
+        def wd_half(a):
+            return wd_words.bitcast(I32)[:, :, a * 256 : (a + 1) * 256].rearrange("g p w -> p g w")
+
+        wd_raw0 = held("wd_raw0", [P, 2, K_PASS // 2], I32)
+        ws_raw0 = held("ws_raw0", [P, PACK, K_PASS], F32)
+
         nc.sync.dma_start(idx2[:], offs2)
+        nc.sync.dma_start(v2_scale_table[TOP2:P, :], tab2_scales[0].bitcast(I32))
+        nc.sync.dma_start(idx[:], offs)
+        nc.sync.dma_start(v_scale_table[TOP:P, :], tab_scales.bitcast(I32).rearrange("g q w -> q g w"))
+        nc.sync.dma_start(wd_scale_raw[TOP:P, :], wd_scales.bitcast(I32).rearrange("g q w -> q g w"))
+        nc.sync.dma_start(wd_raw0[:], wd_half(0))
+        nc.sync.dma_start(v2_table[:], words(tab2_words[0]))
+        nc.sync.dma_start(ws_raw0[:], ws_half(0))
+
+        nc.vector.memset(warm[:, 0:1], 0.0)
+        nc.scalar.activation(warm[:, 1:2], warm[:, 0:1], ACT.Relu)
+        nc.vector.memset(v2_scale_table[0:TOP, :], 0)
+        nc.vector.memset(v2_scale_table[TOP:TOP2, :], 0)
+        nc.vector.memset(v2_plane[:], 0)
+        nc.vector.memset(v_scale_table[0:TOP, :], 0)
+        nc.vector.memset(wd_scale_raw[0:TOP, :], 0)
+        nc.vector.memset(planes[:], 0)
+
+        nc.vector.tensor_copy(v2_scale_picked[:], v2_scale_table[:].bitcast(U8).indirect(idx2[:]))
         for q in range(QUADS):
             nc.sync.dma_start(
-                wd_scale_raw[32 * q : 32 * q + 4, :, :],
-                wd_scales[:, 4 * q : 4 * q + 4, :].bitcast(I32).rearrange("g r w -> r g w"),
+                v2_plane[32 * q + STOCK_ROW : 32 * q + STOCK_ROW + 4, :],
+                v2_scale_picked[TOP2 + 4 * q : TOP2 + 4 * q + 4, :].bitcast(I32),
             )
+        v_table = [at(0, "v_table0", [P, T], I32), at(16, "v_table1", [P, T], I32)]
+        nc.sync.dma_start(v_table[0][:], words(tab_words[0]))
+
+        nc.vector.tensor_copy(v_scale_picked[:, :S], v_scale_table[:].bitcast(U8).indirect(idx[:]))
+        nc.vector.tensor_copy(
+            stage[:, S // 4 :].bitcast(U8).rearrange("p (a t m) -> p a t m", a=2, t=PACK),
+            wd_scale_raw[:].bitcast(U8).rearrange("p (a m t) -> p a t m", a=2, t=PACK),
+        )
+        nc.vector.tensor_copy(stage[:, : S // 4], v_scale_picked[:, :S].bitcast(I32))
         for q in range(QUADS):
-            nc.scalar.dma_start(
-                v2_scale_table[32 * q + STOCK_ROW : 32 * q + STOCK_ROW + 4, :],
-                tab2_scales[0, 4 * q : 4 * q + 4, :].bitcast(I32),
-            )
-        nc.scalar.dma_start(safety_sb[:], safety.rearrange("(a p t) -> p a t", a=2, t=PACK))
+            nc.sync.dma_start(planes[32 * q : 32 * q + 4, :, :], stage[TOP + 8 * q : TOP + 8 * q + 8, :])
+        nc.sync.dma_start(v_table[1][:], words(tab_words[1]))
+        safety_sb = at(32, "safety_sb", [P, 2, PACK], F32)
+        nc.sync.dma_start(safety_sb[:], safety.rearrange("(a p t) -> p a t", a=2, t=PACK))
+
+        wd_raw1 = at(33, "wd_raw1", [P, 2, K_PASS // 2], I32)
+        ws_raw1 = at(35, "ws_raw1", [P, PACK, K_PASS], F32)
+        wc_codes = at(43, "wc_codes", [P, 2, N], I32)
+        wc_planes = at(47, "wc_planes", [P, 2, N // 4], I32)
+        base_sb = at(48, "base_sb", [P, N // P], F32)
+        wd_raw = [wd_raw0, wd_raw1]
+        ws_raw = [ws_raw0, ws_raw1]
+        nc.sync.dma_start(wd_raw1[:], wd_half(1))
+        nc.sync.dma_start(ws_raw1[:], ws_half(1))
+        nc.sync.dma_start(wc_codes[:], wc_words.rearrange("a p c i -> p a (c i)").bitcast(I32))
         with nc.allow_non_contiguous_dma(reason="one value of base for each partition"):
-            nc.scalar.dma_start(base_sb[:], base.rearrange("(i p) -> p i", p=P))
+            nc.sync.dma_start(base_sb[:], base.rearrange("(i p) -> p i", p=P))
+        nc.gpsimd.memset(wc_planes[:], 0)
         for q in range(QUADS):
-            nc.scalar.dma_start(
+            nc.sync.dma_start(
                 wc_planes[32 * q + COST_ROW : 32 * q + COST_ROW + 4, :, :],
                 wc_scales[:, 4 * q : 4 * q + 4, :].bitcast(I32).rearrange("a r w -> r a w"),
             )
 
-        v_scale_picked = held("v_scale_picked", [P, S], U8)
-        nc.vector.tensor_copy(v_scale_picked[:], v_scale_table[:].bitcast(U8).indirect(idx[:]))
-        for g in range(2):
-            for r in range(4):
-                first = 64 * g + 4 * r
-                nc.sync.dma_start(
-                    v_planes[g][r:P:32, :],
-                    v_scale_picked[first : 64 * g + 64 : 16, :].bitcast(I32),
-                )
+        wd_codes = [held("wd_codes%d" % a, [P, 2, PACK, P], U16) for a in range(2)]
 
-        wd_codes = held("wd_codes", [P, 4, PACK, P], U16)
-        nc.vector.tensor_copy(
-            wd_codes[:],
-            wd_raw[:].bitcast(U16).rearrange("p g (a m t) -> p (g a) t m", a=2, t=PACK),
-        )
-        wd_planes = held("wd_planes", [P, 4, PACK, P], U8)
-        nc.vector.tensor_copy(
-            wd_planes[:],
-            wd_scale_raw[:].bitcast(U8).rearrange("p g (a m t) -> p (g a) t m", a=2, t=PACK),
-        )
+        def sort_wd(a):
+            nc.vector.tensor_copy(
+                wd_codes[a][:],
+                wd_raw[a][:].bitcast(U16).rearrange("p g (m t) -> p g t m", t=PACK),
+            )
 
         ws_codes = [held("ws_codes%d" % a, [P, K_PASS], U32) for a in range(2)]
         ws_planes = [held("ws_plane%d" % a, [P, K_PASS], U8) for a in range(2)]
@@ -141,7 +162,6 @@ def tile_list_supplier_shortage_cost_kernel(
 
         v_codes = [[held("v_codes%d_%d" % (g, h), [P, HALF], U32) for h in range(2)] for g in range(2)]
         v2_codes = [held("v2_codes%d" % h, [P, HALF], U32) for h in range(2)]
-        v2_plane = held("v2_plane", [P, S], U8)
 
         def gather_v(g, h):
             nc.vector.tensor_copy(v_codes[g][h][:], v_table[g][:].bitcast(U32).indirect(idx[:, list_cols(h)]))
@@ -149,30 +169,33 @@ def tile_list_supplier_shortage_cost_kernel(
         def gather_v2(h):
             nc.vector.tensor_copy(v2_codes[h][:], v2_table[:].bitcast(U32).indirect(idx2[:, list_cols(h)]))
 
-        def demand_pass(acc, g, a, t, h):
+        plane_bytes = planes[:].bitcast(U8)
+
+        def demand_pass(acc, g, a, t, h, start, stop):
+            first = S + (a * PACK + t) * P
             nc.tensor.matmul_mx(
                 out=acc[:],
-                lhsT=wd_codes[:, 2 * g + a, t, :].bitcast(U8).bitcast(FP4X4),
-                lhsT_scale=wd_planes[:, 2 * g + a, t, :],
+                lhsT=wd_codes[a][:, g, t, :].bitcast(U8).bitcast(FP4X4),
+                lhsT_scale=plane_bytes[:, g, first : first + P],
                 rhs=v_codes[g][h][:].bitcast(FP8X4),
-                rhs_scale=v_planes[g][:].bitcast(U8)[:, h * HALF : (h + 1) * HALF],
-                start=(g == 0),
-                stop=False,
+                rhs_scale=plane_bytes[:, g, h * HALF : (h + 1) * HALF],
+                start=start,
+                stop=stop,
             )
 
-        def stock_pass(acc, a, t, h):
+        def stock_pass(acc, a, t, h, start, stop):
             nc.tensor.matmul_mx(
                 out=acc[:],
                 lhsT=ws_codes[a][:, t * P : (t + 1) * P].bitcast(FP8X4),
                 lhsT_scale=ws_planes[a][:, t * P : (t + 1) * P],
                 rhs=v2_codes[h][:].bitcast(FP8X4),
-                rhs_scale=v2_plane[STOCK_ROW:P, h * HALF : (h + 1) * HALF],
-                start=False,
-                stop=True,
+                rhs_scale=v2_plane[STOCK_ROW:P, :].bitcast(U8)[:, h * HALF : (h + 1) * HALF],
+                start=start,
+                stop=stop,
             )
 
-        def new_acc():
-            return psum.tile([P, HALF], F32, name="acc")
+        def bank(h, t):
+            return psum.tile([P, HALF], F32, name="bank%d" % (PACK * h + t))
 
         def new_rows():
             return ring.tile([P, PACK, HALF], BF16, name="h_rows", align_bytes=256)
@@ -214,59 +237,53 @@ def tile_list_supplier_shortage_cost_kernel(
                 nc.scalar.activation(result[:], acc[:], ACT.Identity, bias=base_sb[:, i : i + 1])
             nc.sync.dma_start(out[i * P : (i + 1) * P, h * HALF : (h + 1) * HALF], result[:])
 
-        nc.vector.memset(warm[:, 0:1], 0.0)
-        nc.scalar.activation(warm[:, 1:2], warm[:, 0:1], ACT.Relu)
-        accs = [[new_acc() for t in range(PACK)] for h in range(2)]
+        sort_wd(0)
+        dst, src = ws_views(0)
+        nc.scalar.activation(dst, src, ACT.Copy, scale=-1.0)
+        for h in range(2):
+            gather_v2(h)
+        quantize_ws(0)
+        accs = [[bank(h, t) for t in range(PACK)] for h in range(2)]
+        for h in range(2):
+            for t in range(PACK):
+                stock_pass(accs[h][t], 0, t, h, True, False)
         for h in range(2):
             gather_v(0, h)
             for t in range(PACK):
-                demand_pass(accs[h][t], 0, 0, t, h)
-        dst, src = ws_views(0)
-        nc.scalar.activation(dst, src, ACT.Copy, scale=-1.0)
-        nc.vector.tensor_copy(v2_plane[:], v2_scale_table[:].bitcast(U8).indirect(idx2[:]))
-        quantize_ws(0)
+                demand_pass(accs[h][t], 0, 0, t, h, False, False)
+        rows = [[new_rows() for h in range(2)] for a in range(2)]
         for h in range(2):
             gather_v(1, h)
             for t in range(PACK):
-                demand_pass(accs[h][t], 1, 0, t, h)
-        rows0 = [new_rows() for h in range(2)]
-        for h in range(2):
-            gather_v2(h)
-            for t in range(PACK):
-                stock_pass(accs[h][t], 0, t, h)
-                shortage(rows0[h], accs[h][t], 0, t)
+                demand_pass(accs[h][t], 1, 0, t, h, False, True)
+                shortage(rows[0][h], accs[h][t], 0, t)
+
+        sort_wd(1)
         dst, src = ws_views(1)
         nc.vector.tensor_scalar(dst, src, -1.0, None, ALU.mult)
         quantize_ws(1)
-        quantize_h(rows0[0], 0, 0)
-
-        accs10 = [new_acc() for t in range(PACK)]
+        accs = [bank(0, t) for t in range(PACK)]
         for t in range(PACK):
             for g in range(2):
-                demand_pass(accs10[t], g, 1, t, 0)
-        quantize_h(rows0[1], 0, 1)
-        rows10 = new_rows()
+                demand_pass(accs[t], g, 1, t, 0, g == 0, False)
         for t in range(PACK):
-            stock_pass(accs10[t], 1, t, 0)
-            shortage(rows10, accs10[t], 1, t)
-        quantize_h(rows10, 1, 0)
-        rows11 = new_rows()
+            stock_pass(accs[t], 1, t, 0, False, True)
+            shortage(rows[1][0], accs[t], 1, t)
+        quantize_h(rows[0][0], 0, 0)
+        quantize_h(rows[0][1], 0, 1)
         for t in range(PACK):
-            acc = new_acc()
+            acc = bank(1, t)
             for g in range(2):
-                demand_pass(acc, g, 1, t, 1)
-            stock_pass(acc, 1, t, 1)
-            shortage(rows11, acc, 1, t)
-        quantize_h(rows11, 1, 1)
+                demand_pass(acc, g, 1, t, 1, g == 0, False)
+            stock_pass(acc, 1, t, 1, False, True)
+            shortage(rows[1][1], acc, 1, t)
+        quantize_h(rows[1][0], 1, 0)
+        quantize_h(rows[1][1], 1, 1)
 
-        for i in range(N // P):
-            acc = new_acc()
-            for a in range(2):
-                cost_pass(acc, a, i, 0)
-            emit(acc, i, 0, False)
-        accs = [new_acc() for i in range(N // P)]
-        for i in range(N // P):
-            cost_pass(accs[i], 0, i, 1)
-        for i in range(N // P):
-            cost_pass(accs[i], 1, i, 1)
-            emit(accs[i], i, 1, i % 2 == 1)
+        for h in range(2):
+            accs = [bank(h, i) for i in range(N // P)]
+            for i in range(N // P):
+                cost_pass(accs[i], 0, i, h)
+            for i in range(N // P):
+                cost_pass(accs[i], 1, i, h)
+                emit(accs[i], i, h, h == 1 and i % 2 == 1)

@@ -52,15 +52,14 @@ def tile_list_supplier_shortage_cost_kernel(
         v_scale_table = held("v_scale_table", [P, T // 4], I32)
         wd_scale_raw = held("wd_scale_raw", [P, H // 4], I32)
         v2_table = held("v2_table", [P, T2], I32)
-        v2_scale_picked = held("v2_scale_picked", [P, S], U8)
+        stage = held("stage", [P, (S + H) // 4], I32)
         planes = held("planes", [P, 2, (S + H) // 4], I32)
         v2_plane = held("v2_plane", [P, S // 4], I32)
         warm = held("warm", [P, 2], F32)
 
-        v2_scale_table = at(0, "v2_scale_table", [P, T2 // 4], I32)
-        v_scale_picked = at(31, "v_scale_picked", [P, 2 * S], U8)
-        stage_bytes = at(33, "stage", [P, 4 * KIB], I32)
-        stage = stage_bytes[:, : (S + H) // 4]
+        v_scale_picked = at(0, "v_scale_picked", [P, S], U8)
+        v2_scale_table = at(31, "v2_scale_table", [P, T2 // 4], I32)
+        v2_scale_picked = at(33, "v2_scale_picked", [P, 16 * KIB], U8)
 
         def words(ap):
             return ap.rearrange("p t i -> p (t i)").bitcast(I32)
@@ -72,43 +71,44 @@ def tile_list_supplier_shortage_cost_kernel(
             return wd_words.bitcast(I32)[:, :, a * 256 : (a + 1) * 256].rearrange("g p w -> p g w")
 
         wd_raw0 = held("wd_raw0", [P, 2, K_PASS // 2], I32)
-        ws_raw0 = held("ws_raw0", [P, PACK, K_PASS], F32)
+        v_table0 = at(65, "v_table0", [P, T], I32)
 
-        nc.sync.dma_start(idx2[:], offs2)
-        nc.sync.dma_start(v2_scale_table[TOP2:P, :], tab2_scales[0].bitcast(I32))
-        nc.sync.dma_start(idx[:], offs)
-        nc.sync.dma_start(v_scale_table[TOP:P, :], tab_scales.bitcast(I32).rearrange("g q w -> q g w"))
-        nc.sync.dma_start(wd_scale_raw[TOP:P, :], wd_scales.bitcast(I32).rearrange("g q w -> q g w"))
         nc.sync.dma_start(wd_raw0[:], wd_half(0))
+        nc.sync.dma_start(v_scale_table[TOP:P, :], tab_scales.bitcast(I32).rearrange("g q w -> q g w"))
+        nc.sync.dma_start(idx[:], offs)
+        nc.sync.dma_start(wd_scale_raw[TOP:P, :], wd_scales.bitcast(I32).rearrange("g q w -> q g w"))
         nc.sync.dma_start(v2_table[:], words(tab2_words[0]))
-        nc.sync.dma_start(ws_raw0[:], ws_half(0))
+        nc.sync.dma_start(v2_scale_table[TOP2:P, :], tab2_scales[0].bitcast(I32))
+        nc.sync.dma_start(idx2[:], offs2)
+        nc.sync.dma_start(v_table0[:], words(tab_words[0]))
 
         nc.vector.memset(warm[:, 0:1], 0.0)
         nc.scalar.activation(warm[:, 1:2], warm[:, 0:1], ACT.Relu)
-        nc.vector.memset(v2_scale_table[0:TOP, :], 0)
-        nc.vector.memset(v2_scale_table[TOP:TOP2, :], 0)
-        nc.vector.memset(v2_plane[:], 0)
         nc.vector.memset(v_scale_table[0:TOP, :], 0)
         nc.vector.memset(wd_scale_raw[0:TOP, :], 0)
         nc.vector.memset(planes[:], 0)
+        nc.vector.memset(v2_scale_table[0:TOP, :], 0)
+        nc.vector.memset(v2_scale_table[TOP:TOP2, :], 0)
+        nc.vector.memset(v2_plane[:], 0)
 
-        nc.vector.tensor_copy(v2_scale_picked[:], v2_scale_table[:].bitcast(U8).indirect(idx2[:]))
-        for q in range(QUADS):
-            nc.sync.dma_start(
-                v2_plane[32 * q + STOCK_ROW : 32 * q + STOCK_ROW + 4, :],
-                v2_scale_picked[TOP2 + 4 * q : TOP2 + 4 * q + 4, :].bitcast(I32),
-            )
-        v_table = [at(0, "v_table0", [P, T], I32), at(16, "v_table1", [P, T], I32)]
-        nc.sync.dma_start(v_table[0][:], words(tab_words[0]))
-
-        nc.vector.tensor_copy(v_scale_picked[:, :S], v_scale_table[:].bitcast(U8).indirect(idx[:]))
+        nc.vector.tensor_copy(v_scale_picked[:], v_scale_table[:].bitcast(U8).indirect(idx[:]))
         nc.vector.tensor_copy(
             stage[:, S // 4 :].bitcast(U8).rearrange("p (a t m) -> p a t m", a=2, t=PACK),
             wd_scale_raw[:].bitcast(U8).rearrange("p (a m t) -> p a t m", a=2, t=PACK),
         )
-        nc.vector.tensor_copy(stage[:, : S // 4], v_scale_picked[:, :S].bitcast(I32))
+        nc.vector.tensor_copy(stage[:, : S // 4], v_scale_picked[:].bitcast(I32))
         for q in range(QUADS):
             nc.sync.dma_start(planes[32 * q : 32 * q + 4, :, :], stage[TOP + 8 * q : TOP + 8 * q + 8, :])
+        ws_raw0 = at(0, "ws_raw0", [P, PACK, K_PASS], F32)
+        nc.sync.dma_start(ws_raw0[:], ws_half(0))
+
+        nc.vector.tensor_copy(v2_scale_picked[:, :S], v2_scale_table[:].bitcast(U8).indirect(idx2[:]))
+        for q in range(QUADS):
+            nc.sync.dma_start(
+                v2_plane[32 * q + STOCK_ROW : 32 * q + STOCK_ROW + 4, :],
+                v2_scale_picked[TOP2 + 4 * q : TOP2 + 4 * q + 4, :S].bitcast(I32),
+            )
+        v_table = [v_table0, at(16, "v_table1", [P, T], I32)]
         nc.sync.dma_start(v_table[1][:], words(tab_words[1]))
         safety_sb = at(32, "safety_sb", [P, 2, PACK], F32)
         nc.sync.dma_start(safety_sb[:], safety.rearrange("(a p t) -> p a t", a=2, t=PACK))
@@ -142,7 +142,7 @@ def tile_list_supplier_shortage_cost_kernel(
 
         ws_codes = [held("ws_codes%d" % a, [P, K_PASS], U32) for a in range(2)]
         ws_planes = [held("ws_plane%d" % a, [P, K_PASS], U8) for a in range(2)]
-        ws_bf = [held("ws_bf%d" % a, [P, PACK, P, PACK], BF16) for a in range(2)]
+        ws_bf = [held("ws_bf0", [P, PACK, P, PACK], BF16), at(49, "ws_bf1", [P, PACK, P, PACK], BF16)]
 
         def ws_views(a):
             return (
@@ -161,7 +161,7 @@ def tile_list_supplier_shortage_cost_kernel(
             return slice(h * HALF // LIST_ROWS, (h + 1) * HALF // LIST_ROWS)
 
         v_codes = [[held("v_codes%d_%d" % (g, h), [P, HALF], U32) for h in range(2)] for g in range(2)]
-        v2_codes = [held("v2_codes%d" % h, [P, HALF], U32) for h in range(2)]
+        v2_codes = [at(65 + 2 * h, "v2_codes%d" % h, [P, HALF], U32) for h in range(2)]
 
         def gather_v(g, h):
             nc.vector.tensor_copy(v_codes[g][h][:], v_table[g][:].bitcast(U32).indirect(idx[:, list_cols(h)]))
@@ -206,12 +206,15 @@ def tile_list_supplier_shortage_cost_kernel(
         h_codes = [[held("h_codes%d_%d" % (a, h), [P, HALF], U32) for h in range(2)] for a in range(2)]
         h_planes = [[held("h_plane%d_%d" % (a, h), [P, HALF], U8) for h in range(2)] for a in range(2)]
 
-        def quantize_h(rows, a, h):
-            grouped = ring.tile([P, HALF, PACK], BF16, name="h_grouped", align_bytes=256)
+        def interleave(rows, a, h):
+            grouped = at(49 + 4 * (2 * a + h), "h_grouped%d_%d" % (a, h), [P, HALF, PACK], BF16)
             nc.vector.tensor_copy(
                 grouped[:].rearrange("p (c i) t -> p c t i", i=4),
                 rows[:].rearrange("p t (c i) -> p c t i", i=4),
             )
+            return grouped
+
+        def quantize_h(grouped, a, h):
             nc.vector.quantize_mx(
                 out=h_codes[a][h][:].bitcast(FP8X4),
                 scales=h_planes[a][h][:],
@@ -240,17 +243,17 @@ def tile_list_supplier_shortage_cost_kernel(
         sort_wd(0)
         dst, src = ws_views(0)
         nc.scalar.activation(dst, src, ACT.Copy, scale=-1.0)
-        for h in range(2):
-            gather_v2(h)
-        quantize_ws(0)
         accs = [[bank(h, t) for t in range(PACK)] for h in range(2)]
-        for h in range(2):
-            for t in range(PACK):
-                stock_pass(accs[h][t], 0, t, h, True, False)
         for h in range(2):
             gather_v(0, h)
             for t in range(PACK):
-                demand_pass(accs[h][t], 0, 0, t, h, False, False)
+                demand_pass(accs[h][t], 0, 0, t, h, True, False)
+        for h in range(2):
+            gather_v2(h)
+        quantize_ws(0)
+        for h in range(2):
+            for t in range(PACK):
+                stock_pass(accs[h][t], 0, t, h, False, False)
         rows = [[new_rows() for h in range(2)] for a in range(2)]
         for h in range(2):
             gather_v(1, h)
@@ -269,16 +272,17 @@ def tile_list_supplier_shortage_cost_kernel(
         for t in range(PACK):
             stock_pass(accs[t], 1, t, 0, False, True)
             shortage(rows[1][0], accs[t], 1, t)
-        quantize_h(rows[0][0], 0, 0)
-        quantize_h(rows[0][1], 0, 1)
+        grouped = [interleave(rows[0][h], 0, h) for h in range(2)]
+        for h in range(2):
+            quantize_h(grouped[h], 0, h)
         for t in range(PACK):
             acc = bank(1, t)
             for g in range(2):
                 demand_pass(acc, g, 1, t, 1, g == 0, False)
             stock_pass(acc, 1, t, 1, False, True)
             shortage(rows[1][1], acc, 1, t)
-        quantize_h(rows[1][0], 1, 0)
-        quantize_h(rows[1][1], 1, 1)
+        for h in range(2):
+            quantize_h(interleave(rows[1][h], 1, h), 1, h)
 
         for h in range(2):
             accs = [bank(h, i) for i in range(N // P)]

@@ -21,7 +21,6 @@ PACK = 4
 K_PASS = P * PACK
 HALF = 512
 LIST_ROWS = 16
-QUADS = 4
 TOP = 96
 TOP2 = 112
 STOCK_ROW = 4
@@ -45,7 +44,7 @@ def tile_list_supplier_shortage_cost_kernel(
             return keep.tile(shape, dtype, name=name, align_bytes=256)
 
         def at(kib, name, shape, dtype):
-            return placed.tile(shape, dtype, name=name, align_bytes=256, offset=kib * KIB)
+            return placed.tile(shape, dtype, name=name, align_bytes=256, offset=int(kib * KIB))
 
         idx = keep.tile([P, S // LIST_ROWS], U16, name="idx")
         idx2 = keep.tile([P, S // LIST_ROWS], U16, name="idx2")
@@ -53,13 +52,13 @@ def tile_list_supplier_shortage_cost_kernel(
         wd_scale_raw = held("wd_scale_raw", [P, H // 4], I32)
         v2_table = held("v2_table", [P, T2], I32)
         stage = held("stage", [P, (S + H) // 4], I32)
-        planes = held("planes", [P, 2, (S + H) // 4], I32)
+        plane0 = held("plane0", [P, (S + H) // 4], I32)
         v2_plane = held("v2_plane", [P, S // 4], I32)
         warm = held("warm", [P, 2], F32)
 
         v_scale_picked = at(0, "v_scale_picked", [P, S], U8)
         v2_scale_table = at(31, "v2_scale_table", [P, T2 // 4], I32)
-        v2_scale_picked = at(33, "v2_scale_picked", [P, 16 * KIB], U8)
+        v2_scale_picked = at(35, "v2_scale_picked", [P, 16 * KIB], U8)
 
         def words(ap):
             return ap.rearrange("p t i -> p (t i)").bitcast(I32)
@@ -71,12 +70,12 @@ def tile_list_supplier_shortage_cost_kernel(
             return wd_words.bitcast(I32)[:, :, a * 256 : (a + 1) * 256].rearrange("g p w -> p g w")
 
         wd_raw0 = held("wd_raw0", [P, 2, K_PASS // 2], I32)
-        v_table0 = at(65, "v_table0", [P, T], I32)
+        v_table0 = at(67, "v_table0", [P, T], I32)
 
         nc.sync.dma_start(wd_raw0[:], wd_half(0))
-        nc.sync.dma_start(v_scale_table[TOP:P, :], tab_scales.bitcast(I32).rearrange("g q w -> q g w"))
+        nc.sync.dma_start(v_scale_table[TOP:P, :], tab_scales.bitcast(I32).rearrange("g q w -> (g q) w"))
         nc.sync.dma_start(idx[:], offs)
-        nc.sync.dma_start(wd_scale_raw[TOP:P, :], wd_scales.bitcast(I32).rearrange("g q w -> q g w"))
+        nc.sync.dma_start(wd_scale_raw[TOP:P, :], wd_scales.bitcast(I32).rearrange("g q w -> (g q) w"))
         nc.sync.dma_start(v2_table[:], words(tab2_words[0]))
         nc.sync.dma_start(v2_scale_table[TOP2:P, :], tab2_scales[0].bitcast(I32))
         nc.sync.dma_start(idx2[:], offs2)
@@ -86,7 +85,7 @@ def tile_list_supplier_shortage_cost_kernel(
         nc.scalar.activation(warm[:, 1:2], warm[:, 0:1], ACT.Relu)
         nc.vector.memset(v_scale_table[0:TOP, :], 0)
         nc.vector.memset(wd_scale_raw[0:TOP, :], 0)
-        nc.vector.memset(planes[:], 0)
+        nc.vector.memset(plane0[:], 0)
         nc.vector.memset(v2_scale_table[0:TOP, :], 0)
         nc.vector.memset(v2_scale_table[TOP:TOP2, :], 0)
         nc.vector.memset(v2_plane[:], 0)
@@ -97,27 +96,36 @@ def tile_list_supplier_shortage_cost_kernel(
             wd_scale_raw[:].bitcast(U8).rearrange("p (a m t) -> p a t m", a=2, t=PACK),
         )
         nc.vector.tensor_copy(stage[:, : S // 4], v_scale_picked[:].bitcast(I32))
-        for q in range(QUADS):
-            nc.sync.dma_start(planes[32 * q : 32 * q + 4, :, :], stage[TOP + 8 * q : TOP + 8 * q + 8, :])
+
+        def move_plane(plane, g):
+            first = TOP + 16 * g
+            for r in range(4):
+                nc.sync.dma_start(plane[r:P:32, :], stage[first + r : first + 16 : 4, :])
+
+        move_plane(plane0, 0)
         ws_raw0 = at(0, "ws_raw0", [P, PACK, K_PASS], F32)
         nc.sync.dma_start(ws_raw0[:], ws_half(0))
 
         nc.vector.tensor_copy(v2_scale_picked[:, :S], v2_scale_table[:].bitcast(U8).indirect(idx2[:]))
-        for q in range(QUADS):
+        for r in range(4):
             nc.sync.dma_start(
-                v2_plane[32 * q + STOCK_ROW : 32 * q + STOCK_ROW + 4, :],
-                v2_scale_picked[TOP2 + 4 * q : TOP2 + 4 * q + 4, :S].bitcast(I32),
+                v2_plane[STOCK_ROW + r : P : 32, :],
+                v2_scale_picked[TOP2 + r : P : 4, :S].bitcast(I32),
             )
         v_table = [v_table0, at(16, "v_table1", [P, T], I32)]
         nc.sync.dma_start(v_table[1][:], words(tab_words[1]))
         safety_sb = at(32, "safety_sb", [P, 2, PACK], F32)
         nc.sync.dma_start(safety_sb[:], safety.rearrange("(a p t) -> p a t", a=2, t=PACK))
 
-        wd_raw1 = at(33, "wd_raw1", [P, 2, K_PASS // 2], I32)
-        ws_raw1 = at(35, "ws_raw1", [P, PACK, K_PASS], F32)
-        wc_codes = at(43, "wc_codes", [P, 2, N], I32)
-        wc_planes = at(47, "wc_planes", [P, 2, N // 4], I32)
-        base_sb = at(48, "base_sb", [P, N // P], F32)
+        plane1 = at(32.5, "plane1", [P, (S + H) // 4], I32)
+        nc.vector.memset(plane1[:], 0)
+        move_plane(plane1, 1)
+
+        wd_raw1 = at(35, "wd_raw1", [P, 2, K_PASS // 2], I32)
+        ws_raw1 = at(37, "ws_raw1", [P, PACK, K_PASS], F32)
+        wc_codes = at(45, "wc_codes", [P, 2, N], I32)
+        wc_planes = at(49, "wc_planes", [P, 2, N // 4], I32)
+        base_sb = at(50, "base_sb", [P, N // P], F32)
         wd_raw = [wd_raw0, wd_raw1]
         ws_raw = [ws_raw0, ws_raw1]
         nc.sync.dma_start(wd_raw1[:], wd_half(1))
@@ -126,10 +134,10 @@ def tile_list_supplier_shortage_cost_kernel(
         with nc.allow_non_contiguous_dma(reason="one value of base for each partition"):
             nc.sync.dma_start(base_sb[:], base.rearrange("(i p) -> p i", p=P))
         nc.gpsimd.memset(wc_planes[:], 0)
-        for q in range(QUADS):
+        for r in range(4):
             nc.sync.dma_start(
-                wc_planes[32 * q + COST_ROW : 32 * q + COST_ROW + 4, :, :],
-                wc_scales[:, 4 * q : 4 * q + 4, :].bitcast(I32).rearrange("a r w -> r a w"),
+                wc_planes[COST_ROW + r : P : 32, :, :],
+                wc_scales[:, r:16:4, :].bitcast(I32).rearrange("a q w -> q a w"),
             )
 
         wd_codes = [held("wd_codes%d" % a, [P, 2, PACK, P], U16) for a in range(2)]
@@ -142,7 +150,7 @@ def tile_list_supplier_shortage_cost_kernel(
 
         ws_codes = [held("ws_codes%d" % a, [P, K_PASS], U32) for a in range(2)]
         ws_planes = [held("ws_plane%d" % a, [P, K_PASS], U8) for a in range(2)]
-        ws_bf = [held("ws_bf0", [P, PACK, P, PACK], BF16), at(49, "ws_bf1", [P, PACK, P, PACK], BF16)]
+        ws_bf = [held("ws_bf0", [P, PACK, P, PACK], BF16), at(51, "ws_bf1", [P, PACK, P, PACK], BF16)]
 
         def ws_views(a):
             return (
@@ -161,7 +169,7 @@ def tile_list_supplier_shortage_cost_kernel(
             return slice(h * HALF // LIST_ROWS, (h + 1) * HALF // LIST_ROWS)
 
         v_codes = [[held("v_codes%d_%d" % (g, h), [P, HALF], U32) for h in range(2)] for g in range(2)]
-        v2_codes = [at(65 + 2 * h, "v2_codes%d" % h, [P, HALF], U32) for h in range(2)]
+        v2_codes = [at(67 + 2 * h, "v2_codes%d" % h, [P, HALF], U32) for h in range(2)]
 
         def gather_v(g, h):
             nc.vector.tensor_copy(v_codes[g][h][:], v_table[g][:].bitcast(U32).indirect(idx[:, list_cols(h)]))
@@ -169,16 +177,16 @@ def tile_list_supplier_shortage_cost_kernel(
         def gather_v2(h):
             nc.vector.tensor_copy(v2_codes[h][:], v2_table[:].bitcast(U32).indirect(idx2[:, list_cols(h)]))
 
-        plane_bytes = planes[:].bitcast(U8)
+        plane_bytes = [plane0[:].bitcast(U8), plane1[:].bitcast(U8)]
 
         def demand_pass(acc, g, a, t, h, start, stop):
             first = S + (a * PACK + t) * P
             nc.tensor.matmul_mx(
                 out=acc[:],
                 lhsT=wd_codes[a][:, g, t, :].bitcast(U8).bitcast(FP4X4),
-                lhsT_scale=plane_bytes[:, g, first : first + P],
+                lhsT_scale=plane_bytes[g][:, first : first + P],
                 rhs=v_codes[g][h][:].bitcast(FP8X4),
-                rhs_scale=plane_bytes[:, g, h * HALF : (h + 1) * HALF],
+                rhs_scale=plane_bytes[g][:, h * HALF : (h + 1) * HALF],
                 start=start,
                 stop=stop,
             )
@@ -207,7 +215,7 @@ def tile_list_supplier_shortage_cost_kernel(
         h_planes = [[held("h_plane%d_%d" % (a, h), [P, HALF], U8) for h in range(2)] for a in range(2)]
 
         def interleave(rows, a, h):
-            grouped = at(49 + 4 * (2 * a + h), "h_grouped%d_%d" % (a, h), [P, HALF, PACK], BF16)
+            grouped = at(51 + 4 * (2 * a + h), "h_grouped%d_%d" % (a, h), [P, HALF, PACK], BF16)
             nc.vector.tensor_copy(
                 grouped[:].rearrange("p (c i) t -> p c t i", i=4),
                 rows[:].rearrange("p t (c i) -> p c t i", i=4),

@@ -50,7 +50,6 @@ def tile_list_supplier_shortage_cost_kernel(
         idx2 = keep.tile([P, S // LIST_ROWS], U16, name="idx2")
         v_scale_table = held("v_scale_table", [P, T // 4], I32)
         wd_scale_raw = held("wd_scale_raw", [P, H // 4], I32)
-        v2_table = held("v2_table", [P, T2], I32)
         stage = held("stage", [P, (S + H) // 4], I32)
         plane0 = held("plane0", [P, (S + H) // 4], I32)
         v2_plane = held("v2_plane", [P, S // 4], I32)
@@ -76,7 +75,8 @@ def tile_list_supplier_shortage_cost_kernel(
         nc.sync.dma_start(v_scale_table[TOP:P, :], tab_scales.bitcast(I32).rearrange("g q w -> (g q) w"))
         nc.sync.dma_start(idx[:], offs)
         nc.sync.dma_start(wd_scale_raw[TOP:P, :], wd_scales.bitcast(I32).rearrange("g q w -> (g q) w"))
-        nc.sync.dma_start(v2_table[:], words(tab2_words[0]))
+        ws_raw0 = held("ws_raw0", [P, PACK, K_PASS], F32)
+        nc.sync.dma_start(ws_raw0[:], ws_half(0))
         nc.sync.dma_start(v2_scale_table[TOP2:P, :], tab2_scales[0].bitcast(I32))
         nc.sync.dma_start(idx2[:], offs2)
         nc.sync.dma_start(v_table0[:], words(tab_words[0]))
@@ -103,17 +103,18 @@ def tile_list_supplier_shortage_cost_kernel(
                 nc.sync.dma_start(plane[r:P:32, :], stage[first + r : first + 16 : 4, :])
 
         move_plane(plane0, 0)
-        ws_raw0 = at(0, "ws_raw0", [P, PACK, K_PASS], F32)
-        nc.sync.dma_start(ws_raw0[:], ws_half(0))
+        v2_table = at(0, "v2_table", [P, T2], I32)
+        nc.sync.dma_start(v2_table[:], words(tab2_words[0]))
 
         nc.vector.tensor_copy(v2_scale_picked[:, :S], v2_scale_table[:].bitcast(U8).indirect(idx2[:]))
+        v_table = [v_table0, at(16, "v_table1", [P, T], I32)]
+        nc.sync.dma_start(v_table[1][:, : T // 2], words(tab_words[1])[:, : T // 2])
         for r in range(4):
             nc.sync.dma_start(
                 v2_plane[STOCK_ROW + r : P : 32, :],
                 v2_scale_picked[TOP2 + r : P : 4, :S].bitcast(I32),
             )
-        v_table = [v_table0, at(16, "v_table1", [P, T], I32)]
-        nc.sync.dma_start(v_table[1][:], words(tab_words[1]))
+        nc.sync.dma_start(v_table[1][:, T // 2 :], words(tab_words[1])[:, T // 2 :])
         safety_sb = at(32, "safety_sb", [P, 2, PACK], F32)
         nc.sync.dma_start(safety_sb[:], safety.rearrange("(a p t) -> p a t", a=2, t=PACK))
 
@@ -214,30 +215,34 @@ def tile_list_supplier_shortage_cost_kernel(
         h_codes = [[held("h_codes%d_%d" % (a, h), [P, HALF], U32) for h in range(2)] for a in range(2)]
         h_planes = [[held("h_plane%d_%d" % (a, h), [P, HALF], U8) for h in range(2)] for a in range(2)]
 
-        def interleave(rows, a, h):
-            grouped = at(51 + 4 * (2 * a + h), "h_grouped%d_%d" % (a, h), [P, HALF, PACK], BF16)
+        grouped = [
+            [at(51 + 4 * (2 * a + h), "h_grouped%d_%d" % (a, h), [P, HALF * PACK], BF16) for h in range(2)]
+            for a in range(2)
+        ]
+        everything = slice(0, HALF)
+
+        def interleave(rows, a, h, cols):
             nc.vector.tensor_copy(
-                grouped[:].rearrange("p (c i) t -> p c t i", i=4),
-                rows[:].rearrange("p t (c i) -> p c t i", i=4),
+                grouped[a][h][:, PACK * cols.start : PACK * cols.stop].rearrange("p (c i t) -> p c t i", i=4, t=PACK),
+                rows[:, :, cols].rearrange("p t (c i) -> p c t i", i=4),
             )
-            return grouped
 
-        def quantize_h(grouped, a, h):
+        def quantize_h(a, h, cols):
             nc.vector.quantize_mx(
-                out=h_codes[a][h][:].bitcast(FP8X4),
-                scales=h_planes[a][h][:],
-                in_=grouped[:].rearrange("p c t -> p (c t)"),
+                out=h_codes[a][h][:, cols].bitcast(FP8X4),
+                scales=h_planes[a][h][:, cols],
+                in_=grouped[a][h][:, PACK * cols.start : PACK * cols.stop],
             )
 
-        def cost_pass(acc, a, i, h):
+        def cost_pass(acc, a, i, h, cols, stop):
             nc.tensor.matmul_mx(
-                out=acc[:],
+                out=acc[:, cols],
                 lhsT=wc_codes[:, a, i * P : (i + 1) * P].bitcast(FP8X4),
                 lhsT_scale=wc_planes[COST_ROW:P, a, :].bitcast(U8)[:, i * P : (i + 1) * P],
-                rhs=h_codes[a][h][:].bitcast(FP8X4),
-                rhs_scale=h_planes[a][h][:],
+                rhs=h_codes[a][h][:, cols].bitcast(FP8X4),
+                rhs_scale=h_planes[a][h][:, cols],
                 start=(a == 0),
-                stop=(a == 1),
+                stop=stop,
             )
 
         def emit(acc, i, h, on_vector):
@@ -251,6 +256,7 @@ def tile_list_supplier_shortage_cost_kernel(
         sort_wd(0)
         dst, src = ws_views(0)
         nc.scalar.activation(dst, src, ACT.Copy, scale=-1.0)
+        quantize_ws(0)
         accs = [[bank(h, t) for t in range(PACK)] for h in range(2)]
         for h in range(2):
             gather_v(0, h)
@@ -258,7 +264,6 @@ def tile_list_supplier_shortage_cost_kernel(
                 demand_pass(accs[h][t], 0, 0, t, h, True, False)
         for h in range(2):
             gather_v2(h)
-        quantize_ws(0)
         for h in range(2):
             for t in range(PACK):
                 stock_pass(accs[h][t], 0, t, h, False, False)
@@ -280,22 +285,34 @@ def tile_list_supplier_shortage_cost_kernel(
         for t in range(PACK):
             stock_pass(accs[t], 1, t, 0, False, True)
             shortage(rows[1][0], accs[t], 1, t)
-        grouped = [interleave(rows[0][h], 0, h) for h in range(2)]
-        for h in range(2):
-            quantize_h(grouped[h], 0, h)
+        interleave(rows[0][0], 0, 0, everything)
+        interleave(rows[0][1], 0, 1, everything)
+        quantize_h(0, 0, everything)
+        interleave(rows[1][0], 1, 0, everything)
+        quantize_h(1, 0, everything)
+        quantize_h(0, 1, everything)
         for t in range(PACK):
             acc = bank(1, t)
             for g in range(2):
                 demand_pass(acc, g, 1, t, 1, g == 0, False)
             stock_pass(acc, 1, t, 1, False, True)
             shortage(rows[1][1], acc, 1, t)
-        for h in range(2):
-            quantize_h(interleave(rows[1][h], 1, h), 1, h)
+        quarters = [slice(0, HALF // 2), slice(HALF // 2, HALF)]
+        for cols in quarters:
+            interleave(rows[1][1], 1, 1, cols)
+        for cols in quarters:
+            quantize_h(1, 1, cols)
 
-        for h in range(2):
-            accs = [bank(h, i) for i in range(N // P)]
-            for i in range(N // P):
-                cost_pass(accs[i], 0, i, h)
-            for i in range(N // P):
-                cost_pass(accs[i], 1, i, h)
-                emit(accs[i], i, h, h == 1 and i % 2 == 1)
+        for i in range(N // P):
+            acc = bank(0, i)
+            for a in range(2):
+                cost_pass(acc, a, i, 0, everything, a == 1)
+            emit(acc, i, 0, False)
+        accs = [bank(1, i) for i in range(N // P)]
+        for i in range(N // P):
+            cost_pass(accs[i], 0, i, 1, everything, False)
+        for i in range(N // P):
+            cost_pass(accs[i], 1, i, 1, quarters[0], False)
+        for i in range(N // P):
+            cost_pass(accs[i], 1, i, 1, quarters[1], True)
+            emit(accs[i], i, 1, i % 2 == 1)

@@ -43,6 +43,9 @@ def tile_list_supplier_shortage_cost_kernel(
         def held(name, shape, dtype):
             return keep.tile(shape, dtype, name=name, align_bytes=256)
 
+        def shifted(name, width, dtype, lead):
+            return keep.tile([P, lead + width], dtype, name=name, align_bytes=256)[:, lead:]
+
         def at(kib, name, shape, dtype):
             return placed.tile(shape, dtype, name=name, align_bytes=256, offset=int(kib * KIB))
 
@@ -51,8 +54,8 @@ def tile_list_supplier_shortage_cost_kernel(
         v_scale_table = held("v_scale_table", [P, T // 4], I32)
         wd_scale_raw = held("wd_scale_raw", [P, H // 4], I32)
         stage = held("stage", [P, (S + H) // 4], I32)
-        plane0 = held("plane0", [P, (S + H) // 4], I32)
-        v2_plane = held("v2_plane", [P, S // 4], I32)
+        plane0 = shifted("plane0", (S + H) // 4, I32, 16)
+        v2_plane = shifted("v2_plane", S // 4, I32, 16)
         warm = held("warm", [P, 2], F32)
 
         v_scale_picked = at(0, "v_scale_picked", [P, S], U8)
@@ -71,9 +74,9 @@ def tile_list_supplier_shortage_cost_kernel(
         wd_raw0 = held("wd_raw0", [P, 2, K_PASS // 2], I32)
         v_table0 = at(67, "v_table0", [P, T], I32)
 
-        nc.sync.dma_start(wd_raw0[:], wd_half(0))
         nc.sync.dma_start(v_scale_table[TOP:P, :], tab_scales.bitcast(I32).rearrange("g q w -> (g q) w"))
         nc.sync.dma_start(idx[:], offs)
+        nc.sync.dma_start(wd_raw0[:], wd_half(0))
         nc.sync.dma_start(wd_scale_raw[TOP:P, :], wd_scales.bitcast(I32).rearrange("g q w -> (g q) w"))
         ws_raw0 = held("ws_raw0", [P, PACK, K_PASS], F32)
         nc.sync.dma_start(ws_raw0[:], ws_half(0))
@@ -118,15 +121,15 @@ def tile_list_supplier_shortage_cost_kernel(
         safety_sb = at(32, "safety_sb", [P, 2, PACK], F32)
         nc.sync.dma_start(safety_sb[:], safety.rearrange("(a p t) -> p a t", a=2, t=PACK))
 
-        plane1 = at(32.5, "plane1", [P, (S + H) // 4], I32)
+        plane1 = at(32.5, "plane1", [P, 16 + (S + H) // 4], I32)[:, 16:]
         nc.vector.memset(plane1[:], 0)
         move_plane(plane1, 1)
 
         wd_raw1 = at(35, "wd_raw1", [P, 2, K_PASS // 2], I32)
         ws_raw1 = at(37, "ws_raw1", [P, PACK, K_PASS], F32)
-        wc_codes = at(45, "wc_codes", [P, 2, N], I32)
-        wc_planes = at(49, "wc_planes", [P, 2, N // 4], I32)
-        base_sb = at(50, "base_sb", [P, N // P], F32)
+        wc_codes = at(45, "wc_codes", [P, 32 + 2 * N], I32)[:, 32:].rearrange("p (a n) -> p a n", a=2)
+        wc_planes = at(49.25, "wc_planes", [P, 2, N // 4], I32)
+        base_sb = at(50.5, "base_sb", [P, N // P], F32)
         wd_raw = [wd_raw0, wd_raw1]
         ws_raw = [ws_raw0, ws_raw1]
         nc.sync.dma_start(wd_raw1[:], wd_half(1))
@@ -141,7 +144,10 @@ def tile_list_supplier_shortage_cost_kernel(
                 wc_scales[:, r:16:4, :].bitcast(I32).rearrange("a q w -> q a w"),
             )
 
-        wd_codes = [held("wd_codes%d" % a, [P, 2, PACK, P], U16) for a in range(2)]
+        wd_codes = [
+            shifted("wd_codes%d" % a, 2 * K_PASS, U16, 64).rearrange("p (g t m) -> p g t m", g=2, t=PACK)
+            for a in range(2)
+        ]
 
         def sort_wd(a):
             nc.vector.tensor_copy(
@@ -149,7 +155,7 @@ def tile_list_supplier_shortage_cost_kernel(
                 wd_raw[a][:].bitcast(U16).rearrange("p g (m t) -> p g t m", t=PACK),
             )
 
-        ws_codes = [held("ws_codes%d" % a, [P, K_PASS], U32) for a in range(2)]
+        ws_codes = [at(71, "ws_codes0", [P, 32 + K_PASS], U32)[:, 32:], shifted("ws_codes1", K_PASS, U32, 32)]
         ws_planes = [held("ws_plane%d" % a, [P, K_PASS], U8) for a in range(2)]
         ws_bf = [held("ws_bf0", [P, PACK, P, PACK], BF16), at(51, "ws_bf1", [P, PACK, P, PACK], BF16)]
 
@@ -213,7 +219,7 @@ def tile_list_supplier_shortage_cost_kernel(
             nc.scalar.activation(rows[:, t, :], acc[:], ACT.Relu, bias=safety_sb[:, a, t : t + 1])
 
         h_codes = [[held("h_codes%d_%d" % (a, h), [P, HALF], U32) for h in range(2)] for a in range(2)]
-        h_planes = [[held("h_plane%d_%d" % (a, h), [P, HALF], U8) for h in range(2)] for a in range(2)]
+        h_planes = [[shifted("h_plane%d_%d" % (a, h), HALF, U8, 64) for h in range(2)] for a in range(2)]
 
         grouped = [
             [at(51 + 4 * (2 * a + h), "h_grouped%d_%d" % (a, h), [P, HALF * PACK], BF16) for h in range(2)]
@@ -256,7 +262,6 @@ def tile_list_supplier_shortage_cost_kernel(
         sort_wd(0)
         dst, src = ws_views(0)
         nc.scalar.activation(dst, src, ACT.Copy, scale=-1.0)
-        quantize_ws(0)
         accs = [[bank(h, t) for t in range(PACK)] for h in range(2)]
         for h in range(2):
             gather_v(0, h)
@@ -264,6 +269,8 @@ def tile_list_supplier_shortage_cost_kernel(
                 demand_pass(accs[h][t], 0, 0, t, h, True, False)
         for h in range(2):
             gather_v2(h)
+            if h == 0:
+                quantize_ws(0)
         for h in range(2):
             for t in range(PACK):
                 stock_pass(accs[h][t], 0, t, h, False, False)

@@ -219,13 +219,17 @@ def tile_list_supplier_shortage_cost_kernel(
             nc.scalar.activation(rows[:, t, :], acc[:], ACT.Relu, bias=safety_sb[:, a, t : t + 1])
 
         h_codes = [[held("h_codes%d_%d" % (a, h), [P, HALF], U32) for h in range(2)] for a in range(2)]
+        rows10 = at(83, "h_rows10", [P, PACK, HALF], BF16)
+        h_codes[0][1] = at(83, "h_codes_late", [P, HALF], U32)
         h_planes = [[shifted("h_plane%d_%d" % (a, h), HALF, U8, 64) for h in range(2)] for a in range(2)]
 
         grouped = [
             [at(51 + 4 * (2 * a + h), "h_grouped%d_%d" % (a, h), [P, HALF * PACK], BF16) for h in range(2)]
             for a in range(2)
         ]
+        grouped[0][0] = at(37, "h_grouped_first", [P, HALF * PACK], BF16)
         everything = slice(0, HALF)
+        quarters = [slice(0, HALF // 2), slice(HALF // 2, HALF)]
 
         def interleave(rows, a, h, cols):
             nc.vector.tensor_copy(
@@ -274,7 +278,7 @@ def tile_list_supplier_shortage_cost_kernel(
         for h in range(2):
             for t in range(PACK):
                 stock_pass(accs[h][t], 0, t, h, False, False)
-        rows = [[new_rows() for h in range(2)] for a in range(2)]
+        rows = [[new_rows(), new_rows()], [rows10, new_rows()]]
         for h in range(2):
             gather_v(1, h)
             for t in range(PACK):
@@ -284,6 +288,7 @@ def tile_list_supplier_shortage_cost_kernel(
         sort_wd(1)
         dst, src = ws_views(1)
         nc.vector.tensor_scalar(dst, src, -1.0, None, ALU.mult)
+        interleave(rows[0][0], 0, 0, slice(0, P))
         quantize_ws(1)
         accs = [bank(0, t) for t in range(PACK)]
         for t in range(PACK):
@@ -292,11 +297,13 @@ def tile_list_supplier_shortage_cost_kernel(
         for t in range(PACK):
             stock_pass(accs[t], 1, t, 0, False, True)
             shortage(rows[1][0], accs[t], 1, t)
-        interleave(rows[0][0], 0, 0, everything)
+        interleave(rows[0][0], 0, 0, slice(P, HALF))
         interleave(rows[0][1], 0, 1, everything)
         quantize_h(0, 0, everything)
-        interleave(rows[1][0], 1, 0, everything)
-        quantize_h(1, 0, everything)
+        for cols in quarters:
+            interleave(rows[1][0], 1, 0, cols)
+        for cols in quarters:
+            quantize_h(1, 0, cols)
         quantize_h(0, 1, everything)
         for t in range(PACK):
             acc = bank(1, t)
@@ -304,7 +311,6 @@ def tile_list_supplier_shortage_cost_kernel(
                 demand_pass(acc, g, 1, t, 1, g == 0, False)
             stock_pass(acc, 1, t, 1, False, True)
             shortage(rows[1][1], acc, 1, t)
-        quarters = [slice(0, HALF // 2), slice(HALF // 2, HALF)]
         for cols in quarters:
             interleave(rows[1][1], 1, 1, cols)
         for cols in quarters:

@@ -37,7 +37,7 @@ def tile_list_supplier_shortage_cost_kernel(
         keep = ctx.enter_context(tc.tile_pool(name="keep", bufs=1))
         placed = ctx.enter_context(tc.tile_pool(name="placed", bufs=1))
         ring = ctx.enter_context(tc.tile_pool(name="ring", bufs=4))
-        outs = ctx.enter_context(tc.tile_pool(name="outs", bufs=8))
+        outs = ctx.enter_context(tc.tile_pool(name="outs", bufs=12))
         psum = ctx.enter_context(tc.psum_pool(name="psum", bufs=1))
 
         def held(name, shape, dtype):
@@ -227,7 +227,6 @@ def tile_list_supplier_shortage_cost_kernel(
             [at(51 + 4 * (2 * a + h), "h_grouped%d_%d" % (a, h), [P, HALF * PACK], BF16) for h in range(2)]
             for a in range(2)
         ]
-        grouped[0][0] = at(37, "h_grouped_first", [P, HALF * PACK], BF16)
         everything = slice(0, HALF)
         quarters = [slice(0, HALF // 2), slice(HALF // 2, HALF)]
 
@@ -244,24 +243,24 @@ def tile_list_supplier_shortage_cost_kernel(
                 in_=grouped[a][h][:, PACK * cols.start : PACK * cols.stop],
             )
 
-        def cost_pass(acc, a, i, h, cols, stop):
+        def cost_pass(acc, a, i, h, cols, start, stop):
             nc.tensor.matmul_mx(
-                out=acc[:, cols],
+                out=acc,
                 lhsT=wc_codes[:, a, i * P : (i + 1) * P].bitcast(FP8X4),
                 lhsT_scale=wc_planes[COST_ROW:P, a, :].bitcast(U8)[:, i * P : (i + 1) * P],
                 rhs=h_codes[a][h][:, cols].bitcast(FP8X4),
                 rhs_scale=h_planes[a][h][:, cols],
-                start=(a == 0),
+                start=start,
                 stop=stop,
             )
 
-        def emit(acc, i, h, on_vector):
-            result = outs.tile([P, HALF], F32, name="result")
+        def emit(acc, i, h, cols, on_vector):
+            result = outs.tile([P, cols.stop - cols.start], F32, name="result")
             if on_vector:
-                nc.vector.tensor_scalar(result[:], acc[:], base_sb[:, i : i + 1], None, ALU.add)
+                nc.vector.tensor_scalar(result[:], acc, base_sb[:, i : i + 1], None, ALU.add)
             else:
-                nc.scalar.activation(result[:], acc[:], ACT.Identity, bias=base_sb[:, i : i + 1])
-            nc.sync.dma_start(out[i * P : (i + 1) * P, h * HALF : (h + 1) * HALF], result[:])
+                nc.scalar.activation(result[:], acc, ACT.Identity, bias=base_sb[:, i : i + 1])
+            nc.sync.dma_start(out[i * P : (i + 1) * P, h * HALF + cols.start : h * HALF + cols.stop], result[:])
 
         sort_wd(0)
         dst, src = ws_views(0)
@@ -288,7 +287,6 @@ def tile_list_supplier_shortage_cost_kernel(
         sort_wd(1)
         dst, src = ws_views(1)
         nc.vector.tensor_scalar(dst, src, -1.0, None, ALU.mult)
-        interleave(rows[0][0], 0, 0, slice(0, P))
         quantize_ws(1)
         accs = [bank(0, t) for t in range(PACK)]
         for t in range(PACK):
@@ -297,7 +295,7 @@ def tile_list_supplier_shortage_cost_kernel(
         for t in range(PACK):
             stock_pass(accs[t], 1, t, 0, False, True)
             shortage(rows[1][0], accs[t], 1, t)
-        interleave(rows[0][0], 0, 0, slice(P, HALF))
+        interleave(rows[0][0], 0, 0, everything)
         interleave(rows[0][1], 0, 1, everything)
         quantize_h(0, 0, everything)
         for cols in quarters:
@@ -319,13 +317,14 @@ def tile_list_supplier_shortage_cost_kernel(
         for i in range(N // P):
             acc = bank(0, i)
             for a in range(2):
-                cost_pass(acc, a, i, 0, everything, a == 1)
-            emit(acc, i, 0, False)
-        accs = [bank(1, i) for i in range(N // P)]
-        for i in range(N // P):
-            cost_pass(accs[i], 0, i, 1, everything, False)
-        for i in range(N // P):
-            cost_pass(accs[i], 1, i, 1, quarters[0], False)
-        for i in range(N // P):
-            cost_pass(accs[i], 1, i, 1, quarters[1], True)
-            emit(accs[i], i, 1, i % 2 == 1)
+                cost_pass(acc[:], a, i, 0, everything, a == 0, a == 1)
+            emit(acc[:], i, 0, everything, False)
+        accs = [bank(1, b) for b in range(PACK)]
+        for b in range(PACK):
+            for e in range(2):
+                cost_pass(accs[b][:, quarters[e]], 0, 2 * (b % 2) + e, 1, quarters[b // 2], e == 0, False)
+        for b in range(PACK):
+            for e in range(2):
+                cost_pass(accs[b][:, quarters[e]], 1, 2 * (b % 2) + e, 1, quarters[b // 2], False, e == 1)
+            for e in range(2):
+                emit(accs[b][:, quarters[e]], 2 * (b % 2) + e, 1, quarters[b // 2], b % 2 == 1)

@@ -37,7 +37,7 @@ def tile_list_supplier_shortage_cost_kernel(
         keep = ctx.enter_context(tc.tile_pool(name="keep", bufs=1))
         placed = ctx.enter_context(tc.tile_pool(name="placed", bufs=1))
         ring = ctx.enter_context(tc.tile_pool(name="ring", bufs=4))
-        outs = ctx.enter_context(tc.tile_pool(name="outs", bufs=12))
+        outs = ctx.enter_context(tc.tile_pool(name="outs", bufs=8))
         psum = ctx.enter_context(tc.psum_pool(name="psum", bufs=1))
 
         def held(name, shape, dtype):
@@ -254,13 +254,11 @@ def tile_list_supplier_shortage_cost_kernel(
                 stop=stop,
             )
 
-        def emit(acc, i, h, cols, on_vector):
-            result = outs.tile([P, cols.stop - cols.start], F32, name="result")
+        def add_base(result, acc, i, on_vector):
             if on_vector:
-                nc.vector.tensor_scalar(result[:], acc, base_sb[:, i : i + 1], None, ALU.add)
+                nc.vector.tensor_scalar(result, acc, base_sb[:, i : i + 1], None, ALU.add)
             else:
-                nc.scalar.activation(result[:], acc, ACT.Identity, bias=base_sb[:, i : i + 1])
-            nc.sync.dma_start(out[i * P : (i + 1) * P, h * HALF + cols.start : h * HALF + cols.stop], result[:])
+                nc.scalar.activation(result, acc, ACT.Identity, bias=base_sb[:, i : i + 1])
 
         sort_wd(0)
         dst, src = ws_views(0)
@@ -318,7 +316,9 @@ def tile_list_supplier_shortage_cost_kernel(
             acc = bank(0, i)
             for a in range(2):
                 cost_pass(acc[:], a, i, 0, everything, a == 0, a == 1)
-            emit(acc[:], i, 0, everything, False)
+            result = outs.tile([P, HALF], F32, name="result")
+            add_base(result[:], acc[:], i, False)
+            nc.sync.dma_start(out[i * P : (i + 1) * P, :HALF], result[:])
         accs = [bank(1, b) for b in range(PACK)]
         for b in range(PACK):
             for e in range(2):
@@ -326,5 +326,12 @@ def tile_list_supplier_shortage_cost_kernel(
         for b in range(PACK):
             for e in range(2):
                 cost_pass(accs[b][:, quarters[e]], 1, 2 * (b % 2) + e, 1, quarters[b // 2], False, e == 1)
+            result = outs.tile([P, HALF], F32, name="result")
             for e in range(2):
-                emit(accs[b][:, quarters[e]], 2 * (b % 2) + e, 1, quarters[b // 2], b % 2 == 1)
+                add_base(result[:, quarters[e]], accs[b][:, quarters[e]], 2 * (b % 2) + e, b % 2 == 1)
+            first_row = 2 * (b % 2) * P
+            cols = quarters[b // 2]
+            nc.sync.dma_start(
+                out[first_row : first_row + 2 * P, HALF + cols.start : HALF + cols.stop].rearrange("(e p) c -> p e c", e=2),
+                result[:].rearrange("p (e c) -> p e c", e=2),
+            )

@@ -215,18 +215,21 @@ def tile_list_supplier_shortage_cost_kernel(
         def new_rows():
             return ring.tile([P, PACK, HALF], BF16, name="h_rows", align_bytes=256)
 
-        def shortage(rows, acc, a, t):
-            nc.scalar.activation(rows[:, t, :], acc[:], ACT.Relu, bias=safety_sb[:, a, t : t + 1])
+        def shortage(rows, acc, a, t, on_vector=False):
+            if on_vector:
+                nc.vector.tensor_scalar(rows[:, t, :], acc[:], safety_sb[:, a, t : t + 1], 0.0, ALU.add, ALU.max)
+            else:
+                nc.scalar.activation(rows[:, t, :], acc[:], ACT.Relu, bias=safety_sb[:, a, t : t + 1])
 
         h_codes = [[held("h_codes%d_%d" % (a, h), [P, HALF], U32) for h in range(2)] for a in range(2)]
         rows10 = at(83, "h_rows10", [P, PACK, HALF], BF16)
-        h_codes[0][1] = at(83, "h_codes_late", [P, HALF], U32)
         h_planes = [[shifted("h_plane%d_%d" % (a, h), HALF, U8, 64) for h in range(2)] for a in range(2)]
 
         grouped = [
             [at(51 + 4 * (2 * a + h), "h_grouped%d_%d" % (a, h), [P, HALF * PACK], BF16) for h in range(2)]
             for a in range(2)
         ]
+        grouped[0][1] = at(83, "h_grouped_late", [P, HALF * PACK], BF16)
         everything = slice(0, HALF)
         quarters = [slice(0, HALF // 2), slice(HALF // 2, HALF)]
 
@@ -292,15 +295,18 @@ def tile_list_supplier_shortage_cost_kernel(
                 demand_pass(accs[t], g, 1, t, 0, g == 0, False)
         for t in range(PACK):
             stock_pass(accs[t], 1, t, 0, False, True)
-            shortage(rows[1][0], accs[t], 1, t)
-        interleave(rows[0][0], 0, 0, everything)
-        interleave(rows[0][1], 0, 1, everything)
+            if t == PACK - 1:
+                interleave(rows[0][0], 0, 0, everything)
+            shortage(rows[1][0], accs[t], 1, t, t == PACK - 1)
         quantize_h(0, 0, everything)
         for cols in quarters:
             interleave(rows[1][0], 1, 0, cols)
         for cols in quarters:
             quantize_h(1, 0, cols)
-        quantize_h(0, 1, everything)
+        for cols in quarters:
+            interleave(rows[0][1], 0, 1, cols)
+        for cols in quarters:
+            quantize_h(0, 1, cols)
         for t in range(PACK):
             acc = bank(1, t)
             for g in range(2):

@@ -126,14 +126,14 @@ def tile_list_supplier_shortage_cost_kernel(
         move_plane(plane1, 1)
 
         wd_raw1 = at(35, "wd_raw1", [P, 2, K_PASS // 2], I32)
-        ws_raw1 = at(37, "ws_raw1", [P, PACK, K_PASS], F32)
+        ws_raw1 = [at(37 + 4 * c, "ws_raw1_%d" % c, [P, PACK, K_PASS // 2], F32) for c in range(2)]
         wc_codes = at(45, "wc_codes", [P, 32 + 2 * N], I32)[:, 32:].rearrange("p (a n) -> p a n", a=2)
         wc_planes = at(49.25, "wc_planes", [P, 2, N // 4], I32)
         base_sb = at(50.5, "base_sb", [P, N // P], F32)
         wd_raw = [wd_raw0, wd_raw1]
-        ws_raw = [ws_raw0, ws_raw1]
         nc.sync.dma_start(wd_raw1[:], wd_half(1))
-        nc.sync.dma_start(ws_raw1[:], ws_half(1))
+        for c in range(2):
+            nc.sync.dma_start(ws_raw1[c][:], ws_half(1)[:, :, c * 256 : (c + 1) * 256])
         nc.sync.dma_start(wc_codes[:], wc_words.rearrange("a p c i -> p a (c i)").bitcast(I32))
         with nc.allow_non_contiguous_dma(reason="one value of base for each partition"):
             nc.sync.dma_start(base_sb[:], base.rearrange("(i p) -> p i", p=P))
@@ -159,10 +159,10 @@ def tile_list_supplier_shortage_cost_kernel(
         ws_planes = [held("ws_plane%d" % a, [P, K_PASS], U8) for a in range(2)]
         ws_bf = [held("ws_bf0", [P, PACK, P, PACK], BF16), at(51, "ws_bf1", [P, PACK, P, PACK], BF16)]
 
-        def ws_views(a):
+        def ws_views(a, raw, places):
             return (
-                ws_bf[a][:].rearrange("p t m j -> p m t j"),
-                ws_raw[a][:].rearrange("p j (m t) -> p m t j", t=PACK),
+                ws_bf[a][:, :, places, :].rearrange("p t m j -> p m t j"),
+                raw[:].rearrange("p j (m t) -> p m t j", t=PACK),
             )
 
         def quantize_ws(a):
@@ -264,7 +264,7 @@ def tile_list_supplier_shortage_cost_kernel(
                 nc.scalar.activation(result, acc, ACT.Identity, bias=base_sb[:, i : i + 1])
 
         sort_wd(0)
-        dst, src = ws_views(0)
+        dst, src = ws_views(0, ws_raw0, slice(0, P))
         nc.scalar.activation(dst, src, ACT.Copy, scale=-1.0)
         accs = [[bank(h, t) for t in range(PACK)] for h in range(2)]
         for h in range(2):
@@ -286,8 +286,9 @@ def tile_list_supplier_shortage_cost_kernel(
                 shortage(rows[0][h], accs[h][t], 0, t)
 
         sort_wd(1)
-        dst, src = ws_views(1)
-        nc.vector.tensor_scalar(dst, src, -1.0, None, ALU.mult)
+        for c in range(2):
+            dst, src = ws_views(1, ws_raw1[c], slice(c * P // 2, (c + 1) * P // 2))
+            nc.vector.tensor_scalar(dst, src, -1.0, None, ALU.mult)
         quantize_ws(1)
         accs = [bank(0, t) for t in range(PACK)]
         for t in range(PACK):

@@ -223,19 +223,26 @@ def tile_list_supplier_shortage_cost_kernel(
 
         h_codes = [[held("h_codes%d_%d" % (a, h), [P, HALF], U32) for h in range(2)] for a in range(2)]
         rows10 = at(83, "h_rows10", [P, PACK, HALF], BF16)
+        h_codes[0][1] = at(83, "h_codes_late", [P, HALF], U32)
         h_planes = [[shifted("h_plane%d_%d" % (a, h), HALF, U8, 64) for h in range(2)] for a in range(2)]
 
         grouped = [
             [at(51 + 4 * (2 * a + h), "h_grouped%d_%d" % (a, h), [P, HALF * PACK], BF16) for h in range(2)]
             for a in range(2)
         ]
-        grouped[0][1] = at(83, "h_grouped_late", [P, HALF * PACK], BF16)
         everything = slice(0, HALF)
         quarters = [slice(0, HALF // 2), slice(HALF // 2, HALF)]
 
+        late_half = at(85, "h_grouped_late", [P, HALF // 2 * PACK], BF16)
+
+        def grouped_cols(a, h, cols):
+            if (a, h, cols) == (0, 1, quarters[1]):
+                return late_half[:]
+            return grouped[a][h][:, PACK * cols.start : PACK * cols.stop]
+
         def interleave(rows, a, h, cols):
             nc.vector.tensor_copy(
-                grouped[a][h][:, PACK * cols.start : PACK * cols.stop].rearrange("p (c i t) -> p c t i", i=4, t=PACK),
+                grouped_cols(a, h, cols).rearrange("p (c i t) -> p c t i", i=4, t=PACK),
                 rows[:, :, cols].rearrange("p t (c i) -> p c t i", i=4),
             )
 
@@ -243,7 +250,7 @@ def tile_list_supplier_shortage_cost_kernel(
             nc.vector.quantize_mx(
                 out=h_codes[a][h][:, cols].bitcast(FP8X4),
                 scales=h_planes[a][h][:, cols],
-                in_=grouped[a][h][:, PACK * cols.start : PACK * cols.stop],
+                in_=grouped_cols(a, h, cols),
             )
 
         def cost_pass(acc, a, i, h, cols, start, stop):
@@ -299,13 +306,13 @@ def tile_list_supplier_shortage_cost_kernel(
             if t == PACK - 1:
                 interleave(rows[0][0], 0, 0, everything)
             shortage(rows[1][0], accs[t], 1, t, t == PACK - 1)
+        interleave(rows[0][1], 0, 1, quarters[0])
         quantize_h(0, 0, everything)
         for cols in quarters:
             interleave(rows[1][0], 1, 0, cols)
         for cols in quarters:
             quantize_h(1, 0, cols)
-        for cols in quarters:
-            interleave(rows[0][1], 0, 1, cols)
+        interleave(rows[0][1], 0, 1, quarters[1])
         for cols in quarters:
             quantize_h(0, 1, cols)
         for t in range(PACK):
@@ -334,11 +341,14 @@ def tile_list_supplier_shortage_cost_kernel(
             for e in range(2):
                 cost_pass(accs[b][:, quarters[e]], 1, 2 * (b % 2) + e, 1, quarters[b // 2], False, e == 1)
             result = outs.tile([P, HALF], F32, name="result")
-            for e in range(2):
-                add_base(result[:, quarters[e]], accs[b][:, quarters[e]], 2 * (b % 2) + e, b % 2 == 1)
             first_row = 2 * (b % 2) * P
             cols = quarters[b // 2]
-            nc.sync.dma_start(
-                out[first_row : first_row + 2 * P, HALF + cols.start : HALF + cols.stop].rearrange("(e p) c -> p e c", e=2),
-                result[:].rearrange("p (e c) -> p e c", e=2),
-            )
+            target = out[first_row : first_row + 2 * P, HALF + cols.start : HALF + cols.stop]
+            for e in range(2):
+                add_base(result[:, quarters[e]], accs[b][:, quarters[e]], 2 * (b % 2) + e, b % 2 == 1)
+                if b == 0:
+                    nc.sync.dma_start(target[e * P : (e + 1) * P, :], result[:, quarters[e]])
+            if b > 0:
+                nc.sync.dma_start(
+                    target.rearrange("(e p) c -> p e c", e=2), result[:].rearrange("p (e c) -> p e c", e=2)
+                )

@@ -20,12 +20,18 @@ P = 128
 PACK = 4
 K_PASS = P * PACK
 HALF = 512
+PART = HALF // 2
 LIST_ROWS = 16
+BLOCKS = 16
+QUADRANT = 32
 TOP = 96
 TOP2 = 112
 STOCK_ROW = 4
 COST_ROW = 8
 KIB = 1024
+
+PLANE_LEAD = 64
+STATIONARY_LEAD = 128
 
 
 def tile_list_supplier_shortage_cost_kernel(
@@ -36,7 +42,7 @@ def tile_list_supplier_shortage_cost_kernel(
     with ExitStack() as ctx:
         keep = ctx.enter_context(tc.tile_pool(name="keep", bufs=1))
         placed = ctx.enter_context(tc.tile_pool(name="placed", bufs=1))
-        ring = ctx.enter_context(tc.tile_pool(name="ring", bufs=4))
+        ring = ctx.enter_context(tc.tile_pool(name="ring", bufs=3))
         outs = ctx.enter_context(tc.tile_pool(name="outs", bufs=8))
         psum = ctx.enter_context(tc.psum_pool(name="psum", bufs=1))
 
@@ -54,8 +60,8 @@ def tile_list_supplier_shortage_cost_kernel(
         v_scale_table = held("v_scale_table", [P, T // 4], I32)
         wd_scale_raw = held("wd_scale_raw", [P, H // 4], I32)
         stage = held("stage", [P, (S + H) // 4], I32)
-        plane0 = shifted("plane0", (S + H) // 4, I32, 16)
-        v2_plane = shifted("v2_plane", S // 4, I32, 16)
+        plane0 = shifted("plane0", (S + H) // 4, I32, PLANE_LEAD // 4)
+        v2_plane = shifted("v2_plane", S // 4, I32, PLANE_LEAD // 4)
         warm = held("warm", [P, 2], F32)
 
         v_scale_picked = at(0, "v_scale_picked", [P, S], U8)
@@ -69,7 +75,8 @@ def tile_list_supplier_shortage_cost_kernel(
             return ws[:, a * K_PASS : (a + 1) * K_PASS].rearrange("(p j) c -> p j c", j=PACK)
 
         def wd_half(a):
-            return wd_words.bitcast(I32)[:, :, a * 256 : (a + 1) * 256].rearrange("g p w -> p g w")
+            pairs = K_PASS // 2
+            return wd_words.bitcast(I32)[:, :, a * pairs : (a + 1) * pairs].rearrange("g p w -> p g w")
 
         wd_raw0 = held("wd_raw0", [P, 2, K_PASS // 2], I32)
         v_table0 = at(67, "v_table0", [P, T], I32)
@@ -95,15 +102,15 @@ def tile_list_supplier_shortage_cost_kernel(
 
         nc.vector.tensor_copy(v_scale_picked[:], v_scale_table[:].bitcast(U8).indirect(idx[:]))
         nc.vector.tensor_copy(
-            stage[:, S // 4 :].bitcast(U8).rearrange("p (a t m) -> p a t m", a=2, t=PACK),
-            wd_scale_raw[:].bitcast(U8).rearrange("p (a m t) -> p a t m", a=2, t=PACK),
+            stage[:, S // 4 :].bitcast(U8).rearrange("p (a t x) -> p a t x", a=2, t=PACK),
+            wd_scale_raw[:].bitcast(U8).rearrange("p (a x t) -> p a t x", a=2, t=PACK),
         )
         nc.vector.tensor_copy(stage[:, : S // 4], v_scale_picked[:].bitcast(I32))
 
         def move_plane(plane, g):
-            first = TOP + 16 * g
+            first = TOP + BLOCKS * g
             for r in range(4):
-                nc.sync.dma_start(plane[r:P:32, :], stage[first + r : first + 16 : 4, :])
+                nc.sync.dma_start(plane[r:P:QUADRANT, :], stage[first + r : first + BLOCKS : 4, :])
 
         move_plane(plane0, 0)
         v2_table = at(0, "v2_table", [P, T2], I32)
@@ -114,62 +121,68 @@ def tile_list_supplier_shortage_cost_kernel(
         nc.sync.dma_start(v_table[1][:, : T // 2], words(tab_words[1])[:, : T // 2])
         for r in range(4):
             nc.sync.dma_start(
-                v2_plane[STOCK_ROW + r : P : 32, :],
+                v2_plane[STOCK_ROW + r : P : QUADRANT, :],
                 v2_scale_picked[TOP2 + r : P : 4, :S].bitcast(I32),
             )
         nc.sync.dma_start(v_table[1][:, T // 2 :], words(tab_words[1])[:, T // 2 :])
         safety_sb = at(32, "safety_sb", [P, 2, PACK], F32)
         nc.sync.dma_start(safety_sb[:], safety.rearrange("(a p t) -> p a t", a=2, t=PACK))
 
-        plane1 = at(32.5, "plane1", [P, 16 + (S + H) // 4], I32)[:, 16:]
+        plane1 = at(32.5, "plane1", [P, (PLANE_LEAD + S + H) // 4], I32)[:, PLANE_LEAD // 4 :]
         nc.vector.memset(plane1[:], 0)
         move_plane(plane1, 1)
 
         wd_raw1 = at(35, "wd_raw1", [P, 2, K_PASS // 2], I32)
         ws_raw1 = [at(37 + 4 * c, "ws_raw1_%d" % c, [P, PACK, K_PASS // 2], F32) for c in range(2)]
-        wc_codes = at(45, "wc_codes", [P, 32 + 2 * N], I32)[:, 32:].rearrange("p (a n) -> p a n", a=2)
+        wc_codes = at(45, "wc_codes", [P, STATIONARY_LEAD // 4 + 2 * N], I32)[:, STATIONARY_LEAD // 4 :]
+        wc_codes = wc_codes.rearrange("p (a n) -> p a n", a=2)
         wc_planes = at(49.25, "wc_planes", [P, 2, N // 4], I32)
         base_sb = at(50.5, "base_sb", [P, N // P], F32)
         wd_raw = [wd_raw0, wd_raw1]
         nc.sync.dma_start(wd_raw1[:], wd_half(1))
         for c in range(2):
-            nc.sync.dma_start(ws_raw1[c][:], ws_half(1)[:, :, c * 256 : (c + 1) * 256])
+            nc.sync.dma_start(ws_raw1[c][:], ws_half(1)[:, :, c * K_PASS // 2 : (c + 1) * K_PASS // 2])
         nc.sync.dma_start(wc_codes[:], wc_words.rearrange("a p c i -> p a (c i)").bitcast(I32))
         with nc.allow_non_contiguous_dma(reason="one value of base for each partition"):
             nc.sync.dma_start(base_sb[:], base.rearrange("(i p) -> p i", p=P))
         nc.gpsimd.memset(wc_planes[:], 0)
         for r in range(4):
             nc.sync.dma_start(
-                wc_planes[COST_ROW + r : P : 32, :, :],
-                wc_scales[:, r:16:4, :].bitcast(I32).rearrange("a q w -> q a w"),
+                wc_planes[COST_ROW + r : P : QUADRANT, :, :],
+                wc_scales[:, r:BLOCKS:4, :].bitcast(I32).rearrange("a q w -> q a w"),
             )
 
         wd_codes = [
-            shifted("wd_codes%d" % a, 2 * K_PASS, U16, 64).rearrange("p (g t m) -> p g t m", g=2, t=PACK)
+            shifted("wd_codes%d" % a, 2 * K_PASS, U16, STATIONARY_LEAD // 2).rearrange(
+                "p (g t x) -> p g t x", g=2, t=PACK
+            )
             for a in range(2)
         ]
 
         def sort_wd(a):
             nc.vector.tensor_copy(
                 wd_codes[a][:],
-                wd_raw[a][:].bitcast(U16).rearrange("p g (m t) -> p g t m", t=PACK),
+                wd_raw[a][:].bitcast(U16).rearrange("p g (x t) -> p g t x", t=PACK),
             )
 
-        ws_codes = [at(71, "ws_codes0", [P, 32 + K_PASS], U32)[:, 32:], shifted("ws_codes1", K_PASS, U32, 32)]
+        ws_codes = [
+            at(71, "ws_codes0", [P, STATIONARY_LEAD // 4 + K_PASS], U32)[:, STATIONARY_LEAD // 4 :],
+            shifted("ws_codes1", K_PASS, U32, STATIONARY_LEAD // 4),
+        ]
         ws_planes = [held("ws_plane%d" % a, [P, K_PASS], U8) for a in range(2)]
         ws_bf = [held("ws_bf0", [P, PACK, P, PACK], BF16), at(51, "ws_bf1", [P, PACK, P, PACK], BF16)]
 
-        def ws_views(a, raw, places):
+        def ws_views(a, raw, xs):
             return (
-                ws_bf[a][:, :, places, :].rearrange("p t m j -> p m t j"),
-                raw[:].rearrange("p j (m t) -> p m t j", t=PACK),
+                ws_bf[a][:, :, xs, :].rearrange("p t x j -> p x t j"),
+                raw[:].rearrange("p j (x t) -> p x t j", t=PACK),
             )
 
         def quantize_ws(a):
             nc.vector.quantize_mx(
                 out=ws_codes[a][:].bitcast(FP8X4),
                 scales=ws_planes[a][:],
-                in_=ws_bf[a][:].rearrange("p t m j -> p (t m j)"),
+                in_=ws_bf[a][:].rearrange("p t x j -> p (t x j)"),
             )
 
         def list_cols(h):
@@ -209,41 +222,43 @@ def tile_list_supplier_shortage_cost_kernel(
                 stop=stop,
             )
 
-        def bank(h, t):
-            return psum.tile([P, HALF], F32, name="bank%d" % (PACK * h + t))
+        def bank(h, b):
+            return psum.tile([P, HALF], F32, name="bank%d" % (PACK * h + b))
 
         def new_rows():
             return ring.tile([P, PACK, HALF], BF16, name="h_rows", align_bytes=256)
 
-        def shortage(rows, acc, a, t, on_vector=False):
+        def shortage(a, h, t, acc, on_vector=False):
+            bias = safety_sb[:, a, t : t + 1]
             if on_vector:
-                nc.vector.tensor_scalar(rows[:, t, :], acc[:], safety_sb[:, a, t : t + 1], 0.0, ALU.add, ALU.max)
+                nc.vector.tensor_scalar(rows[a][h][:, t, :], acc[:], bias, 0.0, ALU.add, ALU.max)
             else:
-                nc.scalar.activation(rows[:, t, :], acc[:], ACT.Relu, bias=safety_sb[:, a, t : t + 1])
+                nc.scalar.activation(rows[a][h][:, t, :], acc[:], ACT.Relu, bias=bias)
 
-        h_codes = [[held("h_codes%d_%d" % (a, h), [P, HALF], U32) for h in range(2)] for a in range(2)]
-        rows10 = at(83, "h_rows10", [P, PACK, HALF], BF16)
-        h_codes[0][1] = at(83, "h_codes_late", [P, HALF], U32)
-        h_planes = [[shifted("h_plane%d_%d" % (a, h), HALF, U8, 64) for h in range(2)] for a in range(2)]
-
-        grouped = [
-            [at(51 + 4 * (2 * a + h), "h_grouped%d_%d" % (a, h), [P, HALF * PACK], BF16) for h in range(2)]
-            for a in range(2)
+        rows = [[new_rows(), new_rows()], [at(83, "h_rows1_0", [P, PACK, HALF], BF16), new_rows()]]
+        h_codes = [
+            [held("h_codes0_0", [P, HALF], U32), at(83, "h_codes0_1", [P, HALF], U32)],
+            [held("h_codes1_0", [P, HALF], U32), held("h_codes1_1", [P, HALF], U32)],
         ]
-        everything = slice(0, HALF)
-        quarters = [slice(0, HALF // 2), slice(HALF // 2, HALF)]
+        h_planes = [[shifted("h_plane%d_%d" % (a, h), HALF, U8, PLANE_LEAD) for h in range(2)] for a in range(2)]
 
-        late_half = at(85, "h_grouped_late", [P, HALF // 2 * PACK], BF16)
+        whole = slice(0, HALF)
+        parts = [slice(0, PART), slice(PART, HALF)]
+        grouped = {
+            (a, h): at(51 + 4 * (2 * a + h), "h_grouped%d_%d" % (a, h), [P, HALF * PACK], BF16)
+            for a, h in ((0, 0), (1, 0), (1, 1))
+        }
+        grouped_01 = [at(kib, "h_grouped0_1_at%d" % kib, [P, PART * PACK], BF16) for kib in (55, 85)]
 
         def grouped_cols(a, h, cols):
-            if (a, h, cols) == (0, 1, quarters[1]):
-                return late_half[:]
-            return grouped[a][h][:, PACK * cols.start : PACK * cols.stop]
+            if (a, h) == (0, 1):
+                return grouped_01[cols.start // PART][:]
+            return grouped[a, h][:, PACK * cols.start : PACK * cols.stop]
 
-        def interleave(rows, a, h, cols):
+        def interleave(a, h, cols):
             nc.vector.tensor_copy(
                 grouped_cols(a, h, cols).rearrange("p (c i t) -> p c t i", i=4, t=PACK),
-                rows[:, :, cols].rearrange("p t (c i) -> p c t i", i=4),
+                rows[a][h][:, :, cols].rearrange("p t (c i) -> p c t i", i=4),
             )
 
         def quantize_h(a, h, cols):
@@ -278,19 +293,17 @@ def tile_list_supplier_shortage_cost_kernel(
             gather_v(0, h)
             for t in range(PACK):
                 demand_pass(accs[h][t], 0, 0, t, h, True, False)
-        for h in range(2):
-            gather_v2(h)
-            if h == 0:
-                quantize_ws(0)
+        gather_v2(0)
+        quantize_ws(0)
+        gather_v2(1)
         for h in range(2):
             for t in range(PACK):
                 stock_pass(accs[h][t], 0, t, h, False, False)
-        rows = [[new_rows(), new_rows()], [rows10, new_rows()]]
         for h in range(2):
             gather_v(1, h)
             for t in range(PACK):
                 demand_pass(accs[h][t], 1, 0, t, h, False, True)
-                shortage(rows[0][h], accs[h][t], 0, t)
+                shortage(0, h, t, accs[h][t])
 
         sort_wd(1)
         for c in range(2):
@@ -301,53 +314,57 @@ def tile_list_supplier_shortage_cost_kernel(
         for t in range(PACK):
             for g in range(2):
                 demand_pass(accs[t], g, 1, t, 0, g == 0, False)
-        for t in range(PACK):
+        last = PACK - 1
+        for t in range(last):
             stock_pass(accs[t], 1, t, 0, False, True)
-            if t == PACK - 1:
-                interleave(rows[0][0], 0, 0, everything)
-            shortage(rows[1][0], accs[t], 1, t, t == PACK - 1)
-        interleave(rows[0][1], 0, 1, quarters[0])
-        quantize_h(0, 0, everything)
-        for cols in quarters:
-            interleave(rows[1][0], 1, 0, cols)
-        for cols in quarters:
+            shortage(1, 0, t, accs[t])
+        stock_pass(accs[last], 1, last, 0, False, True)
+        interleave(0, 0, whole)
+        shortage(1, 0, last, accs[last], on_vector=True)
+        interleave(0, 1, parts[0])
+        quantize_h(0, 0, whole)
+        for cols in parts:
+            interleave(1, 0, cols)
+        for cols in parts:
             quantize_h(1, 0, cols)
-        interleave(rows[0][1], 0, 1, quarters[1])
-        for cols in quarters:
+        interleave(0, 1, parts[1])
+        for cols in parts:
             quantize_h(0, 1, cols)
+
         for t in range(PACK):
             acc = bank(1, t)
             for g in range(2):
                 demand_pass(acc, g, 1, t, 1, g == 0, False)
             stock_pass(acc, 1, t, 1, False, True)
-            shortage(rows[1][1], acc, 1, t)
-        for cols in quarters:
-            interleave(rows[1][1], 1, 1, cols)
-        for cols in quarters:
+            shortage(1, 1, t, acc)
+        for cols in parts:
+            interleave(1, 1, cols)
+        for cols in parts:
             quantize_h(1, 1, cols)
 
         for i in range(N // P):
             acc = bank(0, i)
             for a in range(2):
-                cost_pass(acc[:], a, i, 0, everything, a == 0, a == 1)
+                cost_pass(acc[:], a, i, 0, whole, a == 0, a == 1)
             result = outs.tile([P, HALF], F32, name="result")
             add_base(result[:], acc[:], i, False)
             nc.sync.dma_start(out[i * P : (i + 1) * P, :HALF], result[:])
+
         accs = [bank(1, b) for b in range(PACK)]
         for b in range(PACK):
             for e in range(2):
-                cost_pass(accs[b][:, quarters[e]], 0, 2 * (b % 2) + e, 1, quarters[b // 2], e == 0, False)
+                cost_pass(accs[b][:, parts[e]], 0, 2 * (b % 2) + e, 1, parts[b // 2], e == 0, False)
         for b in range(PACK):
             for e in range(2):
-                cost_pass(accs[b][:, quarters[e]], 1, 2 * (b % 2) + e, 1, quarters[b // 2], False, e == 1)
+                cost_pass(accs[b][:, parts[e]], 1, 2 * (b % 2) + e, 1, parts[b // 2], False, e == 1)
             result = outs.tile([P, HALF], F32, name="result")
             first_row = 2 * (b % 2) * P
-            cols = quarters[b // 2]
+            cols = parts[b // 2]
             target = out[first_row : first_row + 2 * P, HALF + cols.start : HALF + cols.stop]
             for e in range(2):
-                add_base(result[:, quarters[e]], accs[b][:, quarters[e]], 2 * (b % 2) + e, b % 2 == 1)
+                add_base(result[:, parts[e]], accs[b][:, parts[e]], 2 * (b % 2) + e, b % 2 == 1)
                 if b == 0:
-                    nc.sync.dma_start(target[e * P : (e + 1) * P, :], result[:, quarters[e]])
+                    nc.sync.dma_start(target[e * P : (e + 1) * P, :], result[:, parts[e]])
             if b > 0:
                 nc.sync.dma_start(
                     target.rearrange("(e p) c -> p e c", e=2), result[:].rearrange("p (e c) -> p e c", e=2)

@@ -24,8 +24,8 @@ PART = HALF // 2
 LIST_ROWS = 16
 BLOCKS = 16
 QUADRANT = 32
-TOP = 96
-TOP2 = 112
+SPREAD = 4
+SPREAD2 = 8
 STOCK_ROW = 4
 COST_ROW = 8
 KIB = 1024
@@ -81,23 +81,23 @@ def tile_list_supplier_shortage_cost_kernel(
         wd_raw0 = held("wd_raw0", [P, 2, K_PASS // 2], I32)
         v_table0 = at(67, "v_table0", [P, T], I32)
 
-        nc.sync.dma_start(v_scale_table[TOP:P, :], tab_scales.bitcast(I32).rearrange("g q w -> (g q) w"))
-        nc.sync.dma_start(idx[:], offs)
-        nc.sync.dma_start(wd_raw0[:], wd_half(0))
-        nc.sync.dma_start(wd_scale_raw[TOP:P, :], wd_scales.bitcast(I32).rearrange("g q w -> (g q) w"))
+        nc.vector.memset(v_scale_table[:], 0)
+        nc.vector.memset(wd_scale_raw[:], 0)
+        nc.vector.memset(v2_scale_table[:], 0)
         ws_raw0 = held("ws_raw0", [P, PACK, K_PASS], F32)
-        nc.sync.dma_start(ws_raw0[:], ws_half(0))
-        nc.sync.dma_start(v2_scale_table[TOP2:P, :], tab2_scales[0].bitcast(I32))
+        nc.sync.dma_start(ws_raw0[:, :2, :], ws_half(0)[:, :2, :])
+        nc.sync.dma_start(v_scale_table[0:P:SPREAD, :], tab_scales.bitcast(I32).rearrange("g q w -> (g q) w"))
+        nc.sync.dma_start(idx[:], offs)
+        nc.sync.dma_start(wd_scale_raw[0:P:SPREAD, :], wd_scales.bitcast(I32).rearrange("g q w -> (g q) w"))
+        nc.sync.dma_start(wd_raw0[:], wd_half(0))
+        nc.sync.dma_start(ws_raw0[:, 2:, :], ws_half(0)[:, 2:, :])
+        nc.sync.dma_start(v2_scale_table[4:P:SPREAD2, :], tab2_scales[0].bitcast(I32))
         nc.sync.dma_start(idx2[:], offs2)
         nc.sync.dma_start(v_table0[:], words(tab_words[0]))
 
         nc.vector.memset(warm[:, 0:1], 0.0)
         nc.scalar.activation(warm[:, 1:2], warm[:, 0:1], ACT.Relu)
-        nc.vector.memset(v_scale_table[0:TOP, :], 0)
-        nc.vector.memset(wd_scale_raw[0:TOP, :], 0)
         nc.vector.memset(plane0[:], 0)
-        nc.vector.memset(v2_scale_table[0:TOP, :], 0)
-        nc.vector.memset(v2_scale_table[TOP:TOP2, :], 0)
         nc.vector.memset(v2_plane[:], 0)
 
         nc.vector.tensor_copy(v_scale_picked[:], v_scale_table[:].bitcast(U8).indirect(idx[:]))
@@ -108,9 +108,9 @@ def tile_list_supplier_shortage_cost_kernel(
         nc.vector.tensor_copy(stage[:, : S // 4], v_scale_picked[:].bitcast(I32))
 
         def move_plane(plane, g):
-            first = TOP + BLOCKS * g
             for r in range(4):
-                nc.sync.dma_start(plane[r:P:QUADRANT, :], stage[first + r : first + BLOCKS : 4, :])
+                first = SPREAD * (BLOCKS * g + r)
+                nc.sync.dma_start(plane[r:P:QUADRANT, :], stage[first : SPREAD * BLOCKS * (g + 1) : 4 * SPREAD, :])
 
         move_plane(plane0, 0)
         v2_table = at(0, "v2_table", [P, T2], I32)
@@ -122,7 +122,7 @@ def tile_list_supplier_shortage_cost_kernel(
         for r in range(4):
             nc.sync.dma_start(
                 v2_plane[STOCK_ROW + r : P : QUADRANT, :],
-                v2_scale_picked[TOP2 + r : P : 4, :S].bitcast(I32),
+                v2_scale_picked[4 + SPREAD2 * r : P : QUADRANT, :S].bitcast(I32),
             )
         nc.sync.dma_start(v_table[1][:, T // 2 :], words(tab_words[1])[:, T // 2 :])
         safety_sb = at(32, "safety_sb", [P, 2, PACK], F32)
@@ -352,11 +352,10 @@ def tile_list_supplier_shortage_cost_kernel(
 
         accs = [bank(1, b) for b in range(PACK)]
         for b in range(PACK):
-            for e in range(2):
-                cost_pass(accs[b][:, parts[e]], 0, 2 * (b % 2) + e, 1, parts[b // 2], e == 0, False)
-        for b in range(PACK):
-            for e in range(2):
-                cost_pass(accs[b][:, parts[e]], 1, 2 * (b % 2) + e, 1, parts[b // 2], False, e == 1)
+            for a in range(2):
+                for e in range(2):
+                    first, final = (a, e) == (0, 0), (a, e) == (1, 1)
+                    cost_pass(accs[b][:, parts[e]], a, 2 * (b % 2) + e, 1, parts[b // 2], first, final)
             result = outs.tile([P, HALF], F32, name="result")
             first_row = 2 * (b % 2) * P
             cols = parts[b // 2]

@@ -64,7 +64,7 @@ def tile_list_supplier_shortage_cost_kernel(
         v2_plane = shifted("v2_plane", S // 4, I32, PLANE_LEAD // 4)
         warm = held("warm", [P, 2], F32)
 
-        v_scale_picked = at(0, "v_scale_picked", [P, S], U8)
+        v_scale_picked = at(8, "v_scale_picked", [P, S], U8)
         v2_scale_table = at(31, "v2_scale_table", [P, T2 // 4], I32)
         v2_scale_picked = at(35, "v2_scale_picked", [P, 16 * KIB], U8)
 
@@ -94,6 +94,8 @@ def tile_list_supplier_shortage_cost_kernel(
         nc.sync.dma_start(v2_scale_table[4:P:SPREAD2, :], tab2_scales[0].bitcast(I32))
         nc.sync.dma_start(idx2[:], offs2)
         nc.sync.dma_start(v_table0[:], words(tab_words[0]))
+        v2_table = at(0, "v2_table", [P, T2], I32)
+        nc.sync.dma_start(v2_table[:], words(tab2_words[0]))
 
         nc.vector.memset(warm[:, 0:1], 0.0)
         nc.scalar.activation(warm[:, 1:2], warm[:, 0:1], ACT.Relu)
@@ -113,11 +115,9 @@ def tile_list_supplier_shortage_cost_kernel(
                 nc.sync.dma_start(plane[r:P:QUADRANT, :], stage[first : SPREAD * BLOCKS * (g + 1) : 4 * SPREAD, :])
 
         move_plane(plane0, 0)
-        v2_table = at(0, "v2_table", [P, T2], I32)
-        nc.sync.dma_start(v2_table[:], words(tab2_words[0]))
 
         nc.vector.tensor_copy(v2_scale_picked[:, :S], v2_scale_table[:].bitcast(U8).indirect(idx2[:]))
-        v_table = [v_table0, at(16, "v_table1", [P, T], I32)]
+        v_table = [v_table0, at(8, "v_table1", [P, T], I32)]
         nc.sync.dma_start(v_table[1][:, : T // 2], words(tab_words[1])[:, : T // 2])
         for r in range(4):
             nc.sync.dma_start(

@@ -25,7 +25,7 @@ LIST_ROWS = 16
 BLOCKS = 16
 QUADRANT = 32
 SPREAD = 4
-SPREAD2 = 8
+SPREAD2 = 7
 STOCK_ROW = 4
 COST_ROW = 8
 KIB = 1024
@@ -58,9 +58,10 @@ def tile_list_supplier_shortage_cost_kernel(
         idx = keep.tile([P, S // LIST_ROWS], U16, name="idx")
         idx2 = keep.tile([P, S // LIST_ROWS], U16, name="idx2")
         v_scale_table = held("v_scale_table", [P, T // 4], I32)
-        wd_scale_raw = held("wd_scale_raw", [P, H // 4], I32)
-        stage = held("stage", [P, (S + H) // 4], I32)
-        plane0 = shifted("plane0", (S + H) // 4, I32, PLANE_LEAD // 4)
+        wd_scale_raw = held("wd_scale_raw", [P, K_PASS // 4], I32)
+        wd_scale_late = held("wd_scale_late", [P, 2, K_PASS // 4], I32)
+        stage = [held("stage%d" % g, [P, (S + (1 + 2 * g) * K_PASS) // 4], I32) for g in range(2)]
+        plane0 = shifted("plane0", (S + K_PASS) // 4, I32, PLANE_LEAD // 4)
         v2_plane = shifted("v2_plane", S // 4, I32, PLANE_LEAD // 4)
         warm = held("warm", [P, 2], F32)
 
@@ -83,16 +84,22 @@ def tile_list_supplier_shortage_cost_kernel(
 
         nc.vector.memset(v_scale_table[:], 0)
         nc.vector.memset(wd_scale_raw[:], 0)
+        nc.vector.memset(wd_scale_late[:], 0)
         nc.vector.memset(v2_scale_table[:], 0)
         ws_raw0 = held("ws_raw0", [P, PACK, K_PASS], F32)
         nc.sync.dma_start(ws_raw0[:, :2, :], ws_half(0)[:, :2, :])
         nc.sync.dma_start(v_scale_table[0:P:SPREAD, :], tab_scales.bitcast(I32).rearrange("g q w -> (g q) w"))
         nc.sync.dma_start(idx[:], offs)
-        nc.sync.dma_start(wd_scale_raw[0:P:SPREAD, :], wd_scales.bitcast(I32).rearrange("g q w -> (g q) w"))
+        wd_scale_words = wd_scales.bitcast(I32)
+        nc.sync.dma_start(wd_scale_raw[0:P:SPREAD, :], wd_scale_words.rearrange("g q w -> (g q) w")[:, : K_PASS // 4])
         nc.sync.dma_start(wd_raw0[:], wd_half(0))
         nc.sync.dma_start(ws_raw0[:, 2:, :], ws_half(0)[:, 2:, :])
-        nc.sync.dma_start(v2_scale_table[4:P:SPREAD2, :], tab2_scales[0].bitcast(I32))
+        nc.sync.dma_start(v2_scale_table[4 : 4 + SPREAD2 * BLOCKS : SPREAD2, :], tab2_scales[0].bitcast(I32))
         nc.sync.dma_start(idx2[:], offs2)
+        nc.sync.dma_start(
+            wd_scale_late[SPREAD * BLOCKS : P : SPREAD, :, :],
+            wd_scale_words[:, :, K_PASS // 4 :].rearrange("g q w -> q g w"),
+        )
         nc.sync.dma_start(v_table0[:], words(tab_words[0]))
         v2_table = at(0, "v2_table", [P, T2], I32)
         nc.sync.dma_start(v2_table[:], words(tab2_words[0]))
@@ -104,15 +111,15 @@ def tile_list_supplier_shortage_cost_kernel(
 
         nc.vector.tensor_copy(v_scale_picked[:], v_scale_table[:].bitcast(U8).indirect(idx[:]))
         nc.vector.tensor_copy(
-            stage[:, S // 4 :].bitcast(U8).rearrange("p (a t x) -> p a t x", a=2, t=PACK),
-            wd_scale_raw[:].bitcast(U8).rearrange("p (a x t) -> p a t x", a=2, t=PACK),
+            stage[0][:, S // 4 :].bitcast(U8).rearrange("p (t x) -> p t x", t=PACK),
+            wd_scale_raw[:].bitcast(U8).rearrange("p (x t) -> p t x", t=PACK),
         )
-        nc.vector.tensor_copy(stage[:, : S // 4], v_scale_picked[:].bitcast(I32))
+        nc.vector.tensor_copy(stage[0][:, : S // 4], v_scale_picked[:].bitcast(I32))
 
         def move_plane(plane, g):
             for r in range(4):
                 first = SPREAD * (BLOCKS * g + r)
-                nc.sync.dma_start(plane[r:P:QUADRANT, :], stage[first : SPREAD * BLOCKS * (g + 1) : 4 * SPREAD, :])
+                nc.sync.dma_start(plane[r:P:QUADRANT, :], stage[g][first : SPREAD * BLOCKS * (g + 1) : 4 * SPREAD, :])
 
         move_plane(plane0, 0)
 
@@ -122,13 +129,18 @@ def tile_list_supplier_shortage_cost_kernel(
         for r in range(4):
             nc.sync.dma_start(
                 v2_plane[STOCK_ROW + r : P : QUADRANT, :],
-                v2_scale_picked[4 + SPREAD2 * r : P : QUADRANT, :S].bitcast(I32),
+                v2_scale_picked[4 + SPREAD2 * r : 4 + SPREAD2 * BLOCKS : 4 * SPREAD2, :S].bitcast(I32),
             )
         nc.sync.dma_start(v_table[1][:, T // 2 :], words(tab_words[1])[:, T // 2 :])
-        safety_sb = at(32, "safety_sb", [P, 2, PACK], F32)
+        safety_sb = at(31, "safety_sb", [P, 2, PACK], F32)
         nc.sync.dma_start(safety_sb[:], safety.rearrange("(a p t) -> p a t", a=2, t=PACK))
 
-        plane1 = at(32.5, "plane1", [P, (PLANE_LEAD + S + H) // 4], I32)[:, PLANE_LEAD // 4 :]
+        nc.vector.tensor_copy(stage[1][:, : (S + K_PASS) // 4], stage[0][:])
+        nc.vector.tensor_copy(
+            stage[1][:, (S + K_PASS) // 4 :].bitcast(U8).rearrange("p (g t x) -> p g t x", g=2, t=PACK),
+            wd_scale_late[:].bitcast(U8).rearrange("p g (x t) -> p g t x", t=PACK),
+        )
+        plane1 = at(31.5, "plane1", [P, (PLANE_LEAD + S + 3 * K_PASS) // 4], I32)[:, PLANE_LEAD // 4 :]
         nc.vector.memset(plane1[:], 0)
         move_plane(plane1, 1)
 
@@ -174,8 +186,8 @@ def tile_list_supplier_shortage_cost_kernel(
 
         def ws_views(a, raw, xs):
             return (
-                ws_bf[a][:, :, xs, :].rearrange("p t x j -> p x t j"),
-                raw[:].rearrange("p j (x t) -> p x t j", t=PACK),
+                ws_bf[a][:, :, xs, :].rearrange("p t x j -> p x j t"),
+                raw[:].rearrange("p j (x t) -> p x j t", t=PACK),
             )
 
         def quantize_ws(a):
@@ -200,11 +212,11 @@ def tile_list_supplier_shortage_cost_kernel(
         plane_bytes = [plane0[:].bitcast(U8), plane1[:].bitcast(U8)]
 
         def demand_pass(acc, g, a, t, h, start, stop):
-            first = S + (a * PACK + t) * P
+            first = S + a * (1 + g) * K_PASS + t * P
             nc.tensor.matmul_mx(
                 out=acc[:],
                 lhsT=wd_codes[a][:, g, t, :].bitcast(U8).bitcast(FP4X4),
-                lhsT_scale=plane_bytes[g][:, first : first + P],
+                lhsT_scale=plane_bytes[max(g, a)][:, first : first + P],
                 rhs=v_codes[g][h][:].bitcast(FP8X4),
                 rhs_scale=plane_bytes[g][:, h * HALF : (h + 1) * HALF],
                 start=start,

@@ -29,6 +29,7 @@ SPREAD2 = 7
 STOCK_ROW = 4
 COST_ROW = 8
 KIB = 1024
+WS_SPLIT = 384
 
 PLANE_LEAD = 64
 STATIONARY_LEAD = 128
@@ -60,12 +61,13 @@ def tile_list_supplier_shortage_cost_kernel(
         v_scale_table = held("v_scale_table", [P, T // 4], I32)
         wd_scale_raw = held("wd_scale_raw", [P, K_PASS // 4], I32)
         wd_scale_late = held("wd_scale_late", [P, 2, K_PASS // 4], I32)
-        stage = [held("stage%d" % g, [P, (S + (1 + 2 * g) * K_PASS) // 4], I32) for g in range(2)]
+        stage = [held("stage0", [P, (S + K_PASS) // 4], I32)]
         plane0 = shifted("plane0", (S + K_PASS) // 4, I32, PLANE_LEAD // 4)
+        plane1 = shifted("plane1", (S + 3 * K_PASS) // 4, I32, PLANE_LEAD // 4)
         v2_plane = shifted("v2_plane", S // 4, I32, PLANE_LEAD // 4)
         warm = held("warm", [P, 2], F32)
 
-        v_scale_picked = at(8, "v_scale_picked", [P, S], U8)
+        v_scale_picked = at(7.5, "v_scale_picked", [P, S], U8)
         v2_scale_table = at(31, "v2_scale_table", [P, T2 // 4], I32)
         v2_scale_picked = at(35, "v2_scale_picked", [P, 16 * KIB], U8)
 
@@ -101,13 +103,12 @@ def tile_list_supplier_shortage_cost_kernel(
             wd_scale_words[:, :, K_PASS // 4 :].rearrange("g q w -> q g w"),
         )
         nc.sync.dma_start(v_table0[:], words(tab_words[0]))
-        v2_table = at(0, "v2_table", [P, T2], I32)
-        nc.sync.dma_start(v2_table[:], words(tab2_words[0]))
 
         nc.vector.memset(warm[:, 0:1], 0.0)
         nc.scalar.activation(warm[:, 1:2], warm[:, 0:1], ACT.Relu)
         nc.vector.memset(plane0[:], 0)
         nc.vector.memset(v2_plane[:], 0)
+        nc.vector.memset(plane1[:], 0)
 
         nc.vector.tensor_copy(v_scale_picked[:], v_scale_table[:].bitcast(U8).indirect(idx[:]))
         nc.vector.tensor_copy(
@@ -122,6 +123,8 @@ def tile_list_supplier_shortage_cost_kernel(
                 nc.sync.dma_start(plane[r:P:QUADRANT, :], stage[g][first : SPREAD * BLOCKS * (g + 1) : 4 * SPREAD, :])
 
         move_plane(plane0, 0)
+        v2_table = at(0, "v2_table", [P, T2], I32)
+        nc.sync.dma_start(v2_table[:], words(tab2_words[0]))
 
         nc.vector.tensor_copy(v2_scale_picked[:, :S], v2_scale_table[:].bitcast(U8).indirect(idx2[:]))
         v_table = [v_table0, at(8, "v_table1", [P, T], I32)]
@@ -132,20 +135,24 @@ def tile_list_supplier_shortage_cost_kernel(
                 v2_scale_picked[4 + SPREAD2 * r : 4 + SPREAD2 * BLOCKS : 4 * SPREAD2, :S].bitcast(I32),
             )
         nc.sync.dma_start(v_table[1][:, T // 2 :], words(tab_words[1])[:, T // 2 :])
+
         safety_sb = at(31, "safety_sb", [P, 2, PACK], F32)
         nc.sync.dma_start(safety_sb[:], safety.rearrange("(a p t) -> p a t", a=2, t=PACK))
 
+        stage.append(at(75, "stage1", [P, (S + 3 * K_PASS) // 4], I32))
         nc.vector.tensor_copy(stage[1][:, : (S + K_PASS) // 4], stage[0][:])
         nc.vector.tensor_copy(
             stage[1][:, (S + K_PASS) // 4 :].bitcast(U8).rearrange("p (g t x) -> p g t x", g=2, t=PACK),
             wd_scale_late[:].bitcast(U8).rearrange("p g (x t) -> p g t x", t=PACK),
         )
-        plane1 = at(31.5, "plane1", [P, (PLANE_LEAD + S + 3 * K_PASS) // 4], I32)[:, PLANE_LEAD // 4 :]
-        nc.vector.memset(plane1[:], 0)
         move_plane(plane1, 1)
 
         wd_raw1 = at(35, "wd_raw1", [P, 2, K_PASS // 2], I32)
-        ws_raw1 = [at(37 + 4 * c, "ws_raw1_%d" % c, [P, PACK, K_PASS // 2], F32) for c in range(2)]
+        ws_cols1 = [slice(0, WS_SPLIT), slice(WS_SPLIT, K_PASS)]
+        ws_raw1 = [
+            at(37 + cols.start / 64, "ws_raw1_%d" % c, [P, PACK, cols.stop - cols.start], F32)
+            for c, cols in enumerate(ws_cols1)
+        ]
         wc_codes = at(45, "wc_codes", [P, STATIONARY_LEAD // 4 + 2 * N], I32)[:, STATIONARY_LEAD // 4 :]
         wc_codes = wc_codes.rearrange("p (a n) -> p a n", a=2)
         wc_planes = at(49.25, "wc_planes", [P, 2, N // 4], I32)
@@ -153,7 +160,7 @@ def tile_list_supplier_shortage_cost_kernel(
         wd_raw = [wd_raw0, wd_raw1]
         nc.sync.dma_start(wd_raw1[:], wd_half(1))
         for c in range(2):
-            nc.sync.dma_start(ws_raw1[c][:], ws_half(1)[:, :, c * K_PASS // 2 : (c + 1) * K_PASS // 2])
+            nc.sync.dma_start(ws_raw1[c][:], ws_half(1)[:, :, ws_cols1[c]])
         nc.sync.dma_start(wc_codes[:], wc_words.rearrange("a p c i -> p a (c i)").bitcast(I32))
         with nc.allow_non_contiguous_dma(reason="one value of base for each partition"):
             nc.sync.dma_start(base_sb[:], base.rearrange("(i p) -> p i", p=P))
@@ -177,11 +184,16 @@ def tile_list_supplier_shortage_cost_kernel(
                 wd_raw[a][:].bitcast(U16).rearrange("p g (x t) -> p g t x", t=PACK),
             )
 
+        ws_codes0 = at(71, "ws_codes0", [P, STATIONARY_LEAD // 4 + K_PASS], U32)[:, STATIONARY_LEAD // 4 :]
+        ws_plane0 = held("ws_plane0", [P, K_PASS], U8)
         ws_codes = [
-            at(71, "ws_codes0", [P, STATIONARY_LEAD // 4 + K_PASS], U32)[:, STATIONARY_LEAD // 4 :],
-            shifted("ws_codes1", K_PASS, U32, STATIONARY_LEAD // 4),
+            [ws_codes0[:, : 2 * P], ws_codes0[:, 2 * P :]],
+            [shifted("ws_codes1_%d" % u, 2 * P, U32, STATIONARY_LEAD // 4) for u in range(2)],
         ]
-        ws_planes = [held("ws_plane%d" % a, [P, K_PASS], U8) for a in range(2)]
+        ws_planes = [
+            [ws_plane0[:, : 2 * P], ws_plane0[:, 2 * P :]],
+            [held("ws_plane1_%d" % u, [P, 2 * P], U8)[:] for u in range(2)],
+        ]
         ws_bf = [held("ws_bf0", [P, PACK, P, PACK], BF16), at(51, "ws_bf1", [P, PACK, P, PACK], BF16)]
 
         def ws_views(a, raw, xs):
@@ -190,11 +202,9 @@ def tile_list_supplier_shortage_cost_kernel(
                 raw[:].rearrange("p j (x t) -> p x j t", t=PACK),
             )
 
-        def quantize_ws(a):
+        def quantize_ws(codes, plane, values):
             nc.vector.quantize_mx(
-                out=ws_codes[a][:].bitcast(FP8X4),
-                scales=ws_planes[a][:],
-                in_=ws_bf[a][:].rearrange("p t x j -> p (t x j)"),
+                out=codes.bitcast(FP8X4), scales=plane, in_=values.rearrange("p t x j -> p (t x j)")
             )
 
         def list_cols(h):
@@ -226,8 +236,8 @@ def tile_list_supplier_shortage_cost_kernel(
         def stock_pass(acc, a, t, h, start, stop):
             nc.tensor.matmul_mx(
                 out=acc[:],
-                lhsT=ws_codes[a][:, t * P : (t + 1) * P].bitcast(FP8X4),
-                lhsT_scale=ws_planes[a][:, t * P : (t + 1) * P],
+                lhsT=ws_codes[a][t // 2][:, t % 2 * P : (t % 2 + 1) * P].bitcast(FP8X4),
+                lhsT_scale=ws_planes[a][t // 2][:, t % 2 * P : (t % 2 + 1) * P],
                 rhs=v2_codes[h][:].bitcast(FP8X4),
                 rhs_scale=v2_plane[STOCK_ROW:P, :].bitcast(U8)[:, h * HALF : (h + 1) * HALF],
                 start=start,
@@ -306,7 +316,7 @@ def tile_list_supplier_shortage_cost_kernel(
             for t in range(PACK):
                 demand_pass(accs[h][t], 0, 0, t, h, True, False)
         gather_v2(0)
-        quantize_ws(0)
+        quantize_ws(ws_codes0, ws_plane0[:], ws_bf[0][:])
         gather_v2(1)
         for h in range(2):
             for t in range(PACK):
@@ -319,9 +329,10 @@ def tile_list_supplier_shortage_cost_kernel(
 
         sort_wd(1)
         for c in range(2):
-            dst, src = ws_views(1, ws_raw1[c], slice(c * P // 2, (c + 1) * P // 2))
+            dst, src = ws_views(1, ws_raw1[c], slice(ws_cols1[c].start // PACK, ws_cols1[c].stop // PACK))
             nc.vector.tensor_scalar(dst, src, -1.0, None, ALU.mult)
-        quantize_ws(1)
+        for u in range(2):
+            quantize_ws(ws_codes[1][u], ws_planes[1][u], ws_bf[1][:, 2 * u : 2 * u + 2, :, :])
         accs = [bank(0, t) for t in range(PACK)]
         for t in range(PACK):
             for g in range(2):
@@ -374,9 +385,9 @@ def tile_list_supplier_shortage_cost_kernel(
             target = out[first_row : first_row + 2 * P, HALF + cols.start : HALF + cols.stop]
             for e in range(2):
                 add_base(result[:, parts[e]], accs[b][:, parts[e]], 2 * (b % 2) + e, b % 2 == 1)
-                if b == 0:
+                if b in (0, PACK - 1):
                     nc.sync.dma_start(target[e * P : (e + 1) * P, :], result[:, parts[e]])
-            if b > 0:
+            if 0 < b < PACK - 1:
                 nc.sync.dma_start(
                     target.rearrange("(e p) c -> p e c", e=2), result[:].rearrange("p (e c) -> p e c", e=2)
                 )

@@ -383,11 +383,12 @@ def tile_list_supplier_shortage_cost_kernel(
             first_row = 2 * (b % 2) * P
             cols = parts[b // 2]
             target = out[first_row : first_row + 2 * P, HALF + cols.start : HALF + cols.stop]
+            queue = nc.sync if b % 2 == 1 else nc.scalar
             for e in range(2):
                 add_base(result[:, parts[e]], accs[b][:, parts[e]], 2 * (b % 2) + e, b % 2 == 1)
                 if b in (0, PACK - 1):
-                    nc.sync.dma_start(target[e * P : (e + 1) * P, :], result[:, parts[e]])
+                    queue.dma_start(target[e * P : (e + 1) * P, :], result[:, parts[e]])
             if 0 < b < PACK - 1:
-                nc.sync.dma_start(
+                queue.dma_start(
                     target.rearrange("(e p) c -> p e c", e=2), result[:].rearrange("p (e c) -> p e c", e=2)
                 )

@@ -25,7 +25,7 @@ LIST_ROWS = 16
 BLOCKS = 16
 QUADRANT = 32
 SPREAD = 4
-SPREAD2 = 7
+SPREAD2, FIRST2 = 7, 4
 STOCK_ROW = 4
 COST_ROW = 8
 KIB = 1024
@@ -96,7 +96,7 @@ def tile_list_supplier_shortage_cost_kernel(
         nc.sync.dma_start(wd_scale_raw[0:P:SPREAD, :], wd_scale_words.rearrange("g q w -> (g q) w")[:, : K_PASS // 4])
         nc.sync.dma_start(wd_raw0[:], wd_half(0))
         nc.sync.dma_start(ws_raw0[:, 2:, :], ws_half(0)[:, 2:, :])
-        nc.sync.dma_start(v2_scale_table[4 : 4 + SPREAD2 * BLOCKS : SPREAD2, :], tab2_scales[0].bitcast(I32))
+        nc.sync.dma_start(v2_scale_table[FIRST2 : FIRST2 + SPREAD2 * BLOCKS : SPREAD2, :], tab2_scales[0].bitcast(I32))
         nc.sync.dma_start(idx2[:], offs2)
         nc.sync.dma_start(
             wd_scale_late[SPREAD * BLOCKS : P : SPREAD, :, :],
@@ -132,7 +132,7 @@ def tile_list_supplier_shortage_cost_kernel(
         for r in range(4):
             nc.sync.dma_start(
                 v2_plane[STOCK_ROW + r : P : QUADRANT, :],
-                v2_scale_picked[4 + SPREAD2 * r : 4 + SPREAD2 * BLOCKS : 4 * SPREAD2, :S].bitcast(I32),
+                v2_scale_picked[FIRST2 + SPREAD2 * r : FIRST2 + SPREAD2 * BLOCKS : 4 * SPREAD2, :S].bitcast(I32),
             )
         nc.sync.dma_start(v_table[1][:, T // 2 :], words(tab_words[1])[:, T // 2 :])
 
@@ -150,7 +150,7 @@ def tile_list_supplier_shortage_cost_kernel(
         wd_raw1 = at(35, "wd_raw1", [P, 2, K_PASS // 2], I32)
         ws_cols1 = [slice(0, WS_SPLIT), slice(WS_SPLIT, K_PASS)]
         ws_raw1 = [
-            at(37 + cols.start / 64, "ws_raw1_%d" % c, [P, PACK, cols.stop - cols.start], F32)
+            at(37 + cols.start * PACK * 4 / KIB, "ws_raw1_%d" % c, [P, PACK, cols.stop - cols.start], F32)
             for c, cols in enumerate(ws_cols1)
         ]
         wc_codes = at(45, "wc_codes", [P, STATIONARY_LEAD // 4 + 2 * N], I32)[:, STATIONARY_LEAD // 4 :]
@@ -351,8 +351,7 @@ def tile_list_supplier_shortage_cost_kernel(
         for cols in parts:
             quantize_h(1, 0, cols)
         interleave(0, 1, parts[1])
-        for cols in parts:
-            quantize_h(0, 1, cols)
+        quantize_h(0, 1, parts[0])
 
         for t in range(PACK):
             acc = bank(1, t)
@@ -360,10 +359,11 @@ def tile_list_supplier_shortage_cost_kernel(
                 demand_pass(acc, g, 1, t, 1, g == 0, False)
             stock_pass(acc, 1, t, 1, False, True)
             shortage(1, 1, t, acc)
-        for cols in parts:
-            interleave(1, 1, cols)
-        for cols in parts:
-            quantize_h(1, 1, cols)
+        interleave(1, 1, parts[0])
+        quantize_h(0, 1, parts[1])
+        quantize_h(1, 1, parts[0])
+        interleave(1, 1, parts[1])
+        quantize_h(1, 1, parts[1])
 
         for i in range(N // P):
             acc = bank(0, i)
@@ -383,9 +383,10 @@ def tile_list_supplier_shortage_cost_kernel(
             first_row = 2 * (b % 2) * P
             cols = parts[b // 2]
             target = out[first_row : first_row + 2 * P, HALF + cols.start : HALF + cols.stop]
-            queue = nc.sync if b % 2 == 1 else nc.scalar
+            on_vector = b % 2 == 1
+            queue = nc.sync if on_vector else nc.scalar
             for e in range(2):
-                add_base(result[:, parts[e]], accs[b][:, parts[e]], 2 * (b % 2) + e, b % 2 == 1)
+                add_base(result[:, parts[e]], accs[b][:, parts[e]], 2 * (b % 2) + e, on_vector)
                 if b in (0, PACK - 1):
                     queue.dma_start(target[e * P : (e + 1) * P, :], result[:, parts[e]])
             if 0 < b < PACK - 1:

@@ -370,26 +370,33 @@ def tile_list_supplier_shortage_cost_kernel(
             for a in range(2):
                 cost_pass(acc[:], a, i, 0, whole, a == 0, a == 1)
             result = outs.tile([P, HALF], F32, name="result")
-            add_base(result[:], acc[:], i, False)
-            nc.sync.dma_start(out[i * P : (i + 1) * P, :HALF], result[:])
+            for cols in parts if i == 0 else [whole]:
+                add_base(result[:, cols], acc[:, cols], i, False)
+                nc.sync.dma_start(out[i * P : (i + 1) * P, cols], result[:, cols])
 
-        accs = [bank(1, b) for b in range(PACK)]
-        for b in range(PACK):
+        for b in range(2):
+            acc = bank(1, b)
             for a in range(2):
                 for e in range(2):
                     first, final = (a, e) == (0, 0), (a, e) == (1, 1)
-                    cost_pass(accs[b][:, parts[e]], a, 2 * (b % 2) + e, 1, parts[b // 2], first, final)
+                    cost_pass(acc[:, parts[e]], a, 2 * b + e, 1, parts[0], first, final)
             result = outs.tile([P, HALF], F32, name="result")
-            first_row = 2 * (b % 2) * P
-            cols = parts[b // 2]
-            target = out[first_row : first_row + 2 * P, HALF + cols.start : HALF + cols.stop]
-            on_vector = b % 2 == 1
-            queue = nc.sync if on_vector else nc.scalar
+            target = out[2 * b * P : 2 * (b + 1) * P, HALF : HALF + PART]
             for e in range(2):
-                add_base(result[:, parts[e]], accs[b][:, parts[e]], 2 * (b % 2) + e, on_vector)
-                if b in (0, PACK - 1):
-                    queue.dma_start(target[e * P : (e + 1) * P, :], result[:, parts[e]])
-            if 0 < b < PACK - 1:
-                queue.dma_start(
+                add_base(result[:, parts[e]], acc[:, parts[e]], 2 * b + e, b == 1)
+                if b == 0:
+                    nc.scalar.dma_start(target[e * P : (e + 1) * P, :], result[:, parts[e]])
+            if b == 1:
+                nc.sync.dma_start(
                     target.rearrange("(e p) c -> p e c", e=2), result[:].rearrange("p (e c) -> p e c", e=2)
                 )
+
+        for i in range(N // P):
+            acc = bank(1 - i // 2, 2 + i % 2)
+            for a in range(2):
+                cost_pass(acc[:, :PART], a, i, 1, parts[1], a == 0, a == 1)
+            result = outs.tile([P, PART], F32, name="last_result")
+            on_vector = i % 2 == 1
+            add_base(result[:], acc[:, :PART], i, on_vector)
+            queue = nc.sync if on_vector else nc.scalar
+            queue.dma_start(out[i * P : (i + 1) * P, HALF + PART :], result[:])

@@ -81,7 +81,7 @@ def tile_list_supplier_shortage_cost_kernel(
             pairs = K_PASS // 2
             return wd_words.bitcast(I32)[:, :, a * pairs : (a + 1) * pairs].rearrange("g p w -> p g w")
 
-        wd_raw0 = held("wd_raw0", [P, 2, K_PASS // 2], I32)
+        wd_raw0 = [held("wd_raw0_%d" % g, [P, K_PASS // 2], I32) for g in range(2)]
         v_table0 = at(67, "v_table0", [P, T], I32)
 
         nc.vector.memset(v_scale_table[:], 0)
@@ -94,7 +94,7 @@ def tile_list_supplier_shortage_cost_kernel(
         nc.sync.dma_start(idx[:], offs)
         wd_scale_words = wd_scales.bitcast(I32)
         nc.sync.dma_start(wd_scale_raw[0:P:SPREAD, :], wd_scale_words.rearrange("g q w -> (g q) w")[:, : K_PASS // 4])
-        nc.sync.dma_start(wd_raw0[:], wd_half(0))
+        nc.sync.dma_start(wd_raw0[0][:], wd_half(0)[:, 0, :])
         nc.sync.dma_start(ws_raw0[:, 2:, :], ws_half(0)[:, 2:, :])
         nc.sync.dma_start(v2_scale_table[FIRST2 : FIRST2 + SPREAD2 * BLOCKS : SPREAD2, :], tab2_scales[0].bitcast(I32))
         nc.sync.dma_start(idx2[:], offs2)
@@ -136,6 +136,7 @@ def tile_list_supplier_shortage_cost_kernel(
             )
         nc.sync.dma_start(v_table[1][:, T // 2 :], words(tab_words[1])[:, T // 2 :])
 
+        nc.sync.dma_start(wd_raw0[1][:], wd_half(0)[:, 1, :])
         safety_sb = at(31, "safety_sb", [P, 2, PACK], F32)
         nc.sync.dma_start(safety_sb[:], safety.rearrange("(a p t) -> p a t", a=2, t=PACK))
 
@@ -155,34 +156,34 @@ def tile_list_supplier_shortage_cost_kernel(
         ]
         wc_codes = at(45, "wc_codes", [P, STATIONARY_LEAD // 4 + 2 * N], I32)[:, STATIONARY_LEAD // 4 :]
         wc_codes = wc_codes.rearrange("p (a n) -> p a n", a=2)
-        wc_planes = at(49.25, "wc_planes", [P, 2, N // 4], I32)
+        wc_planes = held("wc_planes", [P, 2, N // 4], I32)
+        nc.gpsimd.memset(wc_planes[:], 0)
         base_sb = at(50.5, "base_sb", [P, N // P], F32)
-        wd_raw = [wd_raw0, wd_raw1]
         nc.sync.dma_start(wd_raw1[:], wd_half(1))
         for c in range(2):
             nc.sync.dma_start(ws_raw1[c][:], ws_half(1)[:, :, ws_cols1[c]])
         nc.sync.dma_start(wc_codes[:], wc_words.rearrange("a p c i -> p a (c i)").bitcast(I32))
         with nc.allow_non_contiguous_dma(reason="one value of base for each partition"):
             nc.sync.dma_start(base_sb[:], base.rearrange("(i p) -> p i", p=P))
-        nc.gpsimd.memset(wc_planes[:], 0)
         for r in range(4):
             nc.sync.dma_start(
                 wc_planes[COST_ROW + r : P : QUADRANT, :, :],
                 wc_scales[:, r:BLOCKS:4, :].bitcast(I32).rearrange("a q w -> q a w"),
             )
 
+        wd_codes1 = shifted("wd_codes1", 2 * K_PASS, U16, STATIONARY_LEAD // 2).rearrange(
+            "p (g t x) -> p g t x", g=2, t=PACK
+        )
         wd_codes = [
-            shifted("wd_codes%d" % a, 2 * K_PASS, U16, STATIONARY_LEAD // 2).rearrange(
-                "p (g t x) -> p g t x", g=2, t=PACK
-            )
-            for a in range(2)
+            [
+                shifted("wd_codes0_%d" % g, K_PASS, U16, STATIONARY_LEAD // 2).rearrange("p (t x) -> p t x", t=PACK)
+                for g in range(2)
+            ],
+            [wd_codes1[:, g, :, :] for g in range(2)],
         ]
 
-        def sort_wd(a):
-            nc.vector.tensor_copy(
-                wd_codes[a][:],
-                wd_raw[a][:].bitcast(U16).rearrange("p g (x t) -> p g t x", t=PACK),
-            )
+        def wd_sorted(g):
+            return wd_codes[0][g], wd_raw0[g][:].bitcast(U16).rearrange("p (x t) -> p t x", t=PACK)
 
         ws_codes0 = at(71, "ws_codes0", [P, STATIONARY_LEAD // 4 + K_PASS], U32)[:, STATIONARY_LEAD // 4 :]
         ws_plane0 = held("ws_plane0", [P, K_PASS], U8)
@@ -225,12 +226,27 @@ def tile_list_supplier_shortage_cost_kernel(
             first = S + a * (1 + g) * K_PASS + t * P
             nc.tensor.matmul_mx(
                 out=acc[:],
-                lhsT=wd_codes[a][:, g, t, :].bitcast(U8).bitcast(FP4X4),
+                lhsT=wd_codes[a][g][:, t, :].bitcast(U8).bitcast(FP4X4),
                 lhsT_scale=plane_bytes[max(g, a)][:, first : first + P],
                 rhs=v_codes[g][h][:].bitcast(FP8X4),
                 rhs_scale=plane_bytes[g][:, h * HALF : (h + 1) * HALF],
                 start=start,
                 stop=stop,
+            )
+
+        def gather_part(h, cols):
+            entries = slice((h * HALF + cols.start) // LIST_ROWS, (h * HALF + cols.stop) // LIST_ROWS)
+            nc.vector.tensor_copy(v_codes[1][h][:, cols], v_table[1][:].bitcast(U32).indirect(idx[:, entries]))
+
+        def closing_pass(acc, t, h, cols):
+            nc.tensor.matmul_mx(
+                out=acc[:, cols],
+                lhsT=wd_codes[0][1][:, t, :].bitcast(U8).bitcast(FP4X4),
+                lhsT_scale=plane_bytes[1][:, S + t * P : S + (t + 1) * P],
+                rhs=v_codes[1][h][:, cols].bitcast(FP8X4),
+                rhs_scale=plane_bytes[1][:, h * HALF + cols.start : h * HALF + cols.stop],
+                start=False,
+                stop=cols.stop == HALF,
             )
 
         def stock_pass(acc, a, t, h, start, stop):
@@ -307,7 +323,7 @@ def tile_list_supplier_shortage_cost_kernel(
             else:
                 nc.scalar.activation(result, acc, ACT.Identity, bias=base_sb[:, i : i + 1])
 
-        sort_wd(0)
+        nc.vector.tensor_copy(*wd_sorted(0))
         dst, src = ws_views(0, ws_raw0, slice(0, P))
         nc.scalar.activation(dst, src, ACT.Copy, scale=-1.0)
         accs = [[bank(h, t) for t in range(PACK)] for h in range(2)]
@@ -321,13 +337,16 @@ def tile_list_supplier_shortage_cost_kernel(
         for h in range(2):
             for t in range(PACK):
                 stock_pass(accs[h][t], 0, t, h, False, False)
+        nc.scalar.copy(*wd_sorted(1))
         for h in range(2):
-            gather_v(1, h)
-            for t in range(PACK):
-                demand_pass(accs[h][t], 1, 0, t, h, False, True)
-                shortage(0, h, t, accs[h][t])
+            for cols in parts:
+                gather_part(h, cols)
+                for t in range(PACK):
+                    closing_pass(accs[h][t], t, h, cols)
+                    if cols == parts[1]:
+                        shortage(0, h, t, accs[h][t])
 
-        sort_wd(1)
+        nc.vector.tensor_copy(wd_codes1, wd_raw1[:].bitcast(U16).rearrange("p g (x t) -> p g t x", t=PACK))
         for c in range(2):
             dst, src = ws_views(1, ws_raw1[c], slice(ws_cols1[c].start // PACK, ws_cols1[c].stop // PACK))
             nc.vector.tensor_scalar(dst, src, -1.0, None, ALU.mult)

@@ -54,7 +54,7 @@ def tile_list_supplier_shortage_cost_kernel(
             return keep.tile([P, lead + width], dtype, name=name, align_bytes=256)[:, lead:]
 
         def at(kib, name, shape, dtype):
-            return placed.tile(shape, dtype, name=name, align_bytes=256, offset=int(kib * KIB))
+            return placed.tile(shape, dtype, name=name, align_bytes=256, offset=kib * KIB)
 
         idx = keep.tile([P, S // LIST_ROWS], U16, name="idx")
         idx2 = keep.tile([P, S // LIST_ROWS], U16, name="idx2")
@@ -67,9 +67,9 @@ def tile_list_supplier_shortage_cost_kernel(
         v2_plane = shifted("v2_plane", S // 4, I32, PLANE_LEAD // 4)
         warm = held("warm", [P, 2], F32)
 
-        v_scale_picked = at(7.5, "v_scale_picked", [P, S], U8)
-        v2_scale_table = at(31, "v2_scale_table", [P, T2 // 4], I32)
-        v2_scale_picked = at(35, "v2_scale_picked", [P, 16 * KIB], U8)
+        v_scale_picked = held("v_scale_picked", [P, S], U8)
+        v2_scale_table = held("v2_scale_table", [P, T2 // 4], I32)
+        v2_scale_picked = held("v2_scale_picked", [P, S], U8)
 
         def words(ap):
             return ap.rearrange("p t i -> p (t i)").bitcast(I32)
@@ -82,7 +82,7 @@ def tile_list_supplier_shortage_cost_kernel(
             return wd_words.bitcast(I32)[:, :, a * pairs : (a + 1) * pairs].rearrange("g p w -> p g w")
 
         wd_raw0 = [held("wd_raw0_%d" % g, [P, K_PASS // 2], I32) for g in range(2)]
-        v_table0 = at(67, "v_table0", [P, T], I32)
+        v_table0 = at(16, "v_table0", [P, T], I32)
 
         nc.vector.memset(v_scale_table[:], 0)
         nc.vector.memset(wd_scale_raw[:], 0)
@@ -123,11 +123,11 @@ def tile_list_supplier_shortage_cost_kernel(
                 nc.sync.dma_start(plane[r:P:QUADRANT, :], stage[g][first : SPREAD * BLOCKS * (g + 1) : 4 * SPREAD, :])
 
         move_plane(plane0, 0)
-        v2_table = at(0, "v2_table", [P, T2], I32)
+        v2_table = held("v2_table", [P, T2], I32)
         nc.sync.dma_start(v2_table[:], words(tab2_words[0]))
 
         nc.vector.tensor_copy(v2_scale_picked[:, :S], v2_scale_table[:].bitcast(U8).indirect(idx2[:]))
-        v_table = [v_table0, at(8, "v_table1", [P, T], I32)]
+        v_table = [v_table0, held("v_table1", [P, T], I32)]
         nc.sync.dma_start(v_table[1][:, : T // 2], words(tab_words[1])[:, : T // 2])
         for r in range(4):
             nc.sync.dma_start(
@@ -137,10 +137,10 @@ def tile_list_supplier_shortage_cost_kernel(
         nc.sync.dma_start(v_table[1][:, T // 2 :], words(tab_words[1])[:, T // 2 :])
 
         nc.sync.dma_start(wd_raw0[1][:], wd_half(0)[:, 1, :])
-        safety_sb = at(31, "safety_sb", [P, 2, PACK], F32)
+        safety_sb = held("safety_sb", [P, 2, PACK], F32)
         nc.sync.dma_start(safety_sb[:], safety.rearrange("(a p t) -> p a t", a=2, t=PACK))
 
-        stage.append(at(75, "stage1", [P, (S + 3 * K_PASS) // 4], I32))
+        stage.append(at(24, "stage1", [P, (S + 3 * K_PASS) // 4], I32))
         nc.vector.tensor_copy(stage[1][:, : (S + K_PASS) // 4], stage[0][:])
         nc.vector.tensor_copy(
             stage[1][:, (S + K_PASS) // 4 :].bitcast(U8).rearrange("p (g t x) -> p g t x", g=2, t=PACK),
@@ -148,17 +148,16 @@ def tile_list_supplier_shortage_cost_kernel(
         )
         move_plane(plane1, 1)
 
-        wd_raw1 = at(35, "wd_raw1", [P, 2, K_PASS // 2], I32)
+        wd_raw1 = held("wd_raw1", [P, 2, K_PASS // 2], I32)
         ws_cols1 = [slice(0, WS_SPLIT), slice(WS_SPLIT, K_PASS)]
         ws_raw1 = [
-            at(37 + cols.start * PACK * 4 / KIB, "ws_raw1_%d" % c, [P, PACK, cols.stop - cols.start], F32)
+            held("ws_raw1_%d" % c, [P, PACK, cols.stop - cols.start], F32)
             for c, cols in enumerate(ws_cols1)
         ]
-        wc_codes = at(45, "wc_codes", [P, STATIONARY_LEAD // 4 + 2 * N], I32)[:, STATIONARY_LEAD // 4 :]
-        wc_codes = wc_codes.rearrange("p (a n) -> p a n", a=2)
+        wc_codes = shifted("wc_codes", 2 * N, I32, STATIONARY_LEAD // 4).rearrange("p (a n) -> p a n", a=2)
         wc_planes = held("wc_planes", [P, 2, N // 4], I32)
         nc.gpsimd.memset(wc_planes[:], 0)
-        base_sb = at(50.5, "base_sb", [P, N // P], F32)
+        base_sb = held("base_sb", [P, N // P], F32)
         nc.sync.dma_start(wd_raw1[:], wd_half(1))
         for c in range(2):
             nc.sync.dma_start(ws_raw1[c][:], ws_half(1)[:, :, ws_cols1[c]])
@@ -185,7 +184,7 @@ def tile_list_supplier_shortage_cost_kernel(
         def wd_sorted(g):
             return wd_codes[0][g], wd_raw0[g][:].bitcast(U16).rearrange("p (x t) -> p t x", t=PACK)
 
-        ws_codes0 = at(71, "ws_codes0", [P, STATIONARY_LEAD // 4 + K_PASS], U32)[:, STATIONARY_LEAD // 4 :]
+        ws_codes0 = at(20, "ws_codes0", [P, STATIONARY_LEAD // 4 + K_PASS], U32)[:, STATIONARY_LEAD // 4 :]
         ws_plane0 = held("ws_plane0", [P, K_PASS], U8)
         ws_codes = [
             [ws_codes0[:, : 2 * P], ws_codes0[:, 2 * P :]],
@@ -195,7 +194,7 @@ def tile_list_supplier_shortage_cost_kernel(
             [ws_plane0[:, : 2 * P], ws_plane0[:, 2 * P :]],
             [held("ws_plane1_%d" % u, [P, 2 * P], U8)[:] for u in range(2)],
         ]
-        ws_bf = [held("ws_bf0", [P, PACK, P, PACK], BF16), at(51, "ws_bf1", [P, PACK, P, PACK], BF16)]
+        ws_bf = [held("ws_bf0", [P, PACK, P, PACK], BF16), at(0, "ws_bf1", [P, PACK, P, PACK], BF16)]
 
         def ws_views(a, raw, xs):
             return (
@@ -208,45 +207,36 @@ def tile_list_supplier_shortage_cost_kernel(
                 out=codes.bitcast(FP8X4), scales=plane, in_=values.rearrange("p t x j -> p (t x j)")
             )
 
-        def list_cols(h):
-            return slice(h * HALF // LIST_ROWS, (h + 1) * HALF // LIST_ROWS)
+        whole = slice(0, HALF)
+        parts = [slice(0, PART), slice(PART, HALF)]
+
+        def queries(h, cols):
+            return slice(h * HALF + cols.start, h * HALF + cols.stop)
+
+        def list_cols(h, cols):
+            return slice(queries(h, cols).start // LIST_ROWS, queries(h, cols).stop // LIST_ROWS)
 
         v_codes = [[held("v_codes%d_%d" % (g, h), [P, HALF], U32) for h in range(2)] for g in range(2)]
-        v2_codes = [at(67 + 2 * h, "v2_codes%d" % h, [P, HALF], U32) for h in range(2)]
+        v2_codes = [at(16 + 2 * h, "v2_codes%d" % h, [P, HALF], U32) for h in range(2)]
 
-        def gather_v(g, h):
-            nc.vector.tensor_copy(v_codes[g][h][:], v_table[g][:].bitcast(U32).indirect(idx[:, list_cols(h)]))
+        def gather_v(g, h, cols):
+            nc.vector.tensor_copy(v_codes[g][h][:, cols], v_table[g][:].bitcast(U32).indirect(idx[:, list_cols(h, cols)]))
 
         def gather_v2(h):
-            nc.vector.tensor_copy(v2_codes[h][:], v2_table[:].bitcast(U32).indirect(idx2[:, list_cols(h)]))
+            nc.vector.tensor_copy(v2_codes[h][:], v2_table[:].bitcast(U32).indirect(idx2[:, list_cols(h, whole)]))
 
         plane_bytes = [plane0[:].bitcast(U8), plane1[:].bitcast(U8)]
 
-        def demand_pass(acc, g, a, t, h, start, stop):
+        def demand_pass(acc, g, a, t, h, cols, start, stop):
             first = S + a * (1 + g) * K_PASS + t * P
             nc.tensor.matmul_mx(
-                out=acc[:],
+                out=acc[:, cols],
                 lhsT=wd_codes[a][g][:, t, :].bitcast(U8).bitcast(FP4X4),
                 lhsT_scale=plane_bytes[max(g, a)][:, first : first + P],
-                rhs=v_codes[g][h][:].bitcast(FP8X4),
-                rhs_scale=plane_bytes[g][:, h * HALF : (h + 1) * HALF],
+                rhs=v_codes[g][h][:, cols].bitcast(FP8X4),
+                rhs_scale=plane_bytes[g][:, queries(h, cols)],
                 start=start,
                 stop=stop,
-            )
-
-        def gather_part(h, cols):
-            entries = slice((h * HALF + cols.start) // LIST_ROWS, (h * HALF + cols.stop) // LIST_ROWS)
-            nc.vector.tensor_copy(v_codes[1][h][:, cols], v_table[1][:].bitcast(U32).indirect(idx[:, entries]))
-
-        def closing_pass(acc, t, h, cols):
-            nc.tensor.matmul_mx(
-                out=acc[:, cols],
-                lhsT=wd_codes[0][1][:, t, :].bitcast(U8).bitcast(FP4X4),
-                lhsT_scale=plane_bytes[1][:, S + t * P : S + (t + 1) * P],
-                rhs=v_codes[1][h][:, cols].bitcast(FP8X4),
-                rhs_scale=plane_bytes[1][:, h * HALF + cols.start : h * HALF + cols.stop],
-                start=False,
-                stop=cols.stop == HALF,
             )
 
         def stock_pass(acc, a, t, h, start, stop):
@@ -255,7 +245,7 @@ def tile_list_supplier_shortage_cost_kernel(
                 lhsT=ws_codes[a][t // 2][:, t % 2 * P : (t % 2 + 1) * P].bitcast(FP8X4),
                 lhsT_scale=ws_planes[a][t // 2][:, t % 2 * P : (t % 2 + 1) * P],
                 rhs=v2_codes[h][:].bitcast(FP8X4),
-                rhs_scale=v2_plane[STOCK_ROW:P, :].bitcast(U8)[:, h * HALF : (h + 1) * HALF],
+                rhs_scale=v2_plane[STOCK_ROW:P, :].bitcast(U8)[:, queries(h, whole)],
                 start=start,
                 stop=stop,
             )
@@ -273,20 +263,18 @@ def tile_list_supplier_shortage_cost_kernel(
             else:
                 nc.scalar.activation(rows[a][h][:, t, :], acc[:], ACT.Relu, bias=bias)
 
-        rows = [[new_rows(), new_rows()], [at(83, "h_rows1_0", [P, PACK, HALF], BF16), new_rows()]]
+        rows = [[new_rows(), new_rows()], [at(32, "h_rows1_0", [P, PACK, HALF], BF16), new_rows()]]
         h_codes = [
-            [held("h_codes0_0", [P, HALF], U32), at(83, "h_codes0_1", [P, HALF], U32)],
+            [held("h_codes0_0", [P, HALF], U32), at(32, "h_codes0_1", [P, HALF], U32)],
             [held("h_codes1_0", [P, HALF], U32), held("h_codes1_1", [P, HALF], U32)],
         ]
         h_planes = [[shifted("h_plane%d_%d" % (a, h), HALF, U8, PLANE_LEAD) for h in range(2)] for a in range(2)]
 
-        whole = slice(0, HALF)
-        parts = [slice(0, PART), slice(PART, HALF)]
         grouped = {
-            (a, h): at(51 + 4 * (2 * a + h), "h_grouped%d_%d" % (a, h), [P, HALF * PACK], BF16)
+            (a, h): at(4 * (2 * a + h), "h_grouped%d_%d" % (a, h), [P, HALF * PACK], BF16)
             for a, h in ((0, 0), (1, 0), (1, 1))
         }
-        grouped_01 = [at(kib, "h_grouped0_1_at%d" % kib, [P, PART * PACK], BF16) for kib in (55, 85)]
+        grouped_01 = [at(kib, "h_grouped0_1_at%d" % kib, [P, PART * PACK], BF16) for kib in (4, 34)]
 
         def grouped_cols(a, h, cols):
             if (a, h) == (0, 1):
@@ -328,9 +316,9 @@ def tile_list_supplier_shortage_cost_kernel(
         nc.scalar.activation(dst, src, ACT.Copy, scale=-1.0)
         accs = [[bank(h, t) for t in range(PACK)] for h in range(2)]
         for h in range(2):
-            gather_v(0, h)
+            gather_v(0, h, whole)
             for t in range(PACK):
-                demand_pass(accs[h][t], 0, 0, t, h, True, False)
+                demand_pass(accs[h][t], 0, 0, t, h, whole, True, False)
         gather_v2(0)
         quantize_ws(ws_codes0, ws_plane0[:], ws_bf[0][:])
         gather_v2(1)
@@ -340,9 +328,9 @@ def tile_list_supplier_shortage_cost_kernel(
         nc.scalar.copy(*wd_sorted(1))
         for h in range(2):
             for cols in parts:
-                gather_part(h, cols)
+                gather_v(1, h, cols)
                 for t in range(PACK):
-                    closing_pass(accs[h][t], t, h, cols)
+                    demand_pass(accs[h][t], 1, 0, t, h, cols, False, cols == parts[1])
                     if cols == parts[1]:
                         shortage(0, h, t, accs[h][t])
 
@@ -355,7 +343,7 @@ def tile_list_supplier_shortage_cost_kernel(
         accs = [bank(0, t) for t in range(PACK)]
         for t in range(PACK):
             for g in range(2):
-                demand_pass(accs[t], g, 1, t, 0, g == 0, False)
+                demand_pass(accs[t], g, 1, t, 0, whole, g == 0, False)
         last = PACK - 1
         for t in range(last):
             stock_pass(accs[t], 1, t, 0, False, True)
@@ -375,7 +363,7 @@ def tile_list_supplier_shortage_cost_kernel(
         for t in range(PACK):
             acc = bank(1, t)
             for g in range(2):
-                demand_pass(acc, g, 1, t, 1, g == 0, False)
+                demand_pass(acc, g, 1, t, 1, whole, g == 0, False)
             stock_pass(acc, 1, t, 1, False, True)
             shortage(1, 1, t, acc)
         interleave(1, 1, parts[0])

@@ -109,6 +109,8 @@ def tile_list_supplier_shortage_cost_kernel(
         nc.vector.memset(plane0[:], 0)
         nc.vector.memset(v2_plane[:], 0)
         nc.vector.memset(plane1[:], 0)
+        wc_planes = held("wc_planes", [P, 2, N // 4], I32)
+        nc.vector.memset(wc_planes[:], 0)
 
         nc.vector.tensor_copy(v_scale_picked[:], v_scale_table[:].bitcast(U8).indirect(idx[:]))
         nc.vector.tensor_copy(
@@ -118,9 +120,9 @@ def tile_list_supplier_shortage_cost_kernel(
         nc.vector.tensor_copy(stage[0][:, : S // 4], v_scale_picked[:].bitcast(I32))
 
         def move_plane(plane, g):
-            for r in range(4):
-                first = SPREAD * (BLOCKS * g + r)
-                nc.sync.dma_start(plane[r:P:QUADRANT, :], stage[g][first : SPREAD * BLOCKS * (g + 1) : 4 * SPREAD, :])
+            for s in range(4):
+                sources = slice(SPREAD * (BLOCKS * g + s), SPREAD * BLOCKS * (g + 1), 4 * SPREAD)
+                nc.sync.dma_start(plane[s:P:QUADRANT, :], stage[g][sources, :])
 
         move_plane(plane0, 0)
         v2_table = held("v2_table", [P, T2], I32)
@@ -129,10 +131,10 @@ def tile_list_supplier_shortage_cost_kernel(
         nc.vector.tensor_copy(v2_scale_picked[:, :S], v2_scale_table[:].bitcast(U8).indirect(idx2[:]))
         v_table = [v_table0, held("v_table1", [P, T], I32)]
         nc.sync.dma_start(v_table[1][:, : T // 2], words(tab_words[1])[:, : T // 2])
-        for r in range(4):
+        for s in range(4):
             nc.sync.dma_start(
-                v2_plane[STOCK_ROW + r : P : QUADRANT, :],
-                v2_scale_picked[FIRST2 + SPREAD2 * r : FIRST2 + SPREAD2 * BLOCKS : 4 * SPREAD2, :S].bitcast(I32),
+                v2_plane[STOCK_ROW + s : P : QUADRANT, :],
+                v2_scale_picked[FIRST2 + SPREAD2 * s : FIRST2 + SPREAD2 * BLOCKS : 4 * SPREAD2, :S].bitcast(I32),
             )
         nc.sync.dma_start(v_table[1][:, T // 2 :], words(tab_words[1])[:, T // 2 :])
 
@@ -155,8 +157,6 @@ def tile_list_supplier_shortage_cost_kernel(
             for c, cols in enumerate(ws_cols1)
         ]
         wc_codes = shifted("wc_codes", 2 * N, I32, STATIONARY_LEAD // 4).rearrange("p (a n) -> p a n", a=2)
-        wc_planes = held("wc_planes", [P, 2, N // 4], I32)
-        nc.gpsimd.memset(wc_planes[:], 0)
         base_sb = held("base_sb", [P, N // P], F32)
         nc.sync.dma_start(wd_raw1[:], wd_half(1))
         for c in range(2):
@@ -164,10 +164,10 @@ def tile_list_supplier_shortage_cost_kernel(
         nc.sync.dma_start(wc_codes[:], wc_words.rearrange("a p c i -> p a (c i)").bitcast(I32))
         with nc.allow_non_contiguous_dma(reason="one value of base for each partition"):
             nc.sync.dma_start(base_sb[:], base.rearrange("(i p) -> p i", p=P))
-        for r in range(4):
+        for s in range(4):
             nc.sync.dma_start(
-                wc_planes[COST_ROW + r : P : QUADRANT, :, :],
-                wc_scales[:, r:BLOCKS:4, :].bitcast(I32).rearrange("a q w -> q a w"),
+                wc_planes[COST_ROW + s : P : QUADRANT, :, :],
+                wc_scales[:, s:BLOCKS:4, :].bitcast(I32).rearrange("a q w -> q a w"),
             )
 
         wd_codes1 = shifted("wd_codes1", 2 * K_PASS, U16, STATIONARY_LEAD // 2).rearrange(
@@ -210,97 +210,97 @@ def tile_list_supplier_shortage_cost_kernel(
         whole = slice(0, HALF)
         parts = [slice(0, PART), slice(PART, HALF)]
 
-        def queries(h, cols):
-            return slice(h * HALF + cols.start, h * HALF + cols.stop)
+        def queries(qh, cols):
+            return slice(qh * HALF + cols.start, qh * HALF + cols.stop)
 
-        def list_cols(h, cols):
-            return slice(queries(h, cols).start // LIST_ROWS, queries(h, cols).stop // LIST_ROWS)
+        def list_cols(qh, cols):
+            return slice(queries(qh, cols).start // LIST_ROWS, queries(qh, cols).stop // LIST_ROWS)
 
-        v_codes = [[held("v_codes%d_%d" % (g, h), [P, HALF], U32) for h in range(2)] for g in range(2)]
-        v2_codes = [at(16 + 2 * h, "v2_codes%d" % h, [P, HALF], U32) for h in range(2)]
+        v_codes = [[held("v_codes%d_%d" % (g, qh), [P, HALF], U32) for qh in range(2)] for g in range(2)]
+        v2_codes = [at(16 + 2 * qh, "v2_codes%d" % qh, [P, HALF], U32) for qh in range(2)]
 
-        def gather_v(g, h, cols):
-            nc.vector.tensor_copy(v_codes[g][h][:, cols], v_table[g][:].bitcast(U32).indirect(idx[:, list_cols(h, cols)]))
+        def gather_v(g, qh, cols):
+            nc.vector.tensor_copy(v_codes[g][qh][:, cols], v_table[g][:].bitcast(U32).indirect(idx[:, list_cols(qh, cols)]))
 
-        def gather_v2(h):
-            nc.vector.tensor_copy(v2_codes[h][:], v2_table[:].bitcast(U32).indirect(idx2[:, list_cols(h, whole)]))
+        def gather_v2(qh):
+            nc.vector.tensor_copy(v2_codes[qh][:], v2_table[:].bitcast(U32).indirect(idx2[:, list_cols(qh, whole)]))
 
         plane_bytes = [plane0[:].bitcast(U8), plane1[:].bitcast(U8)]
 
-        def demand_pass(acc, g, a, t, h, cols, start, stop):
-            first = S + a * (1 + g) * K_PASS + t * P
+        def demand_pass(acc, g, a, t, qh, cols, start, stop):
+            wd_col = S + a * (1 + g) * K_PASS + t * P
             nc.tensor.matmul_mx(
                 out=acc[:, cols],
                 lhsT=wd_codes[a][g][:, t, :].bitcast(U8).bitcast(FP4X4),
-                lhsT_scale=plane_bytes[max(g, a)][:, first : first + P],
-                rhs=v_codes[g][h][:, cols].bitcast(FP8X4),
-                rhs_scale=plane_bytes[g][:, queries(h, cols)],
+                lhsT_scale=plane_bytes[max(g, a)][:, wd_col : wd_col + P],
+                rhs=v_codes[g][qh][:, cols].bitcast(FP8X4),
+                rhs_scale=plane_bytes[g][:, queries(qh, cols)],
                 start=start,
                 stop=stop,
             )
 
-        def stock_pass(acc, a, t, h, start, stop):
+        def stock_pass(acc, a, t, qh, start, stop):
             nc.tensor.matmul_mx(
                 out=acc[:],
                 lhsT=ws_codes[a][t // 2][:, t % 2 * P : (t % 2 + 1) * P].bitcast(FP8X4),
                 lhsT_scale=ws_planes[a][t // 2][:, t % 2 * P : (t % 2 + 1) * P],
-                rhs=v2_codes[h][:].bitcast(FP8X4),
-                rhs_scale=v2_plane[STOCK_ROW:P, :].bitcast(U8)[:, queries(h, whole)],
+                rhs=v2_codes[qh][:].bitcast(FP8X4),
+                rhs_scale=v2_plane[STOCK_ROW:P, :].bitcast(U8)[:, queries(qh, whole)],
                 start=start,
                 stop=stop,
             )
 
-        def bank(h, b):
-            return psum.tile([P, HALF], F32, name="bank%d" % (PACK * h + b))
+        def bank(qh, b):
+            return psum.tile([P, HALF], F32, name="bank%d" % (PACK * qh + b))
 
         def new_rows():
             return ring.tile([P, PACK, HALF], BF16, name="h_rows", align_bytes=256)
 
-        def shortage(a, h, t, acc, on_vector=False):
+        def shortage(a, qh, t, acc, on_vector=False):
             bias = safety_sb[:, a, t : t + 1]
             if on_vector:
-                nc.vector.tensor_scalar(rows[a][h][:, t, :], acc[:], bias, 0.0, ALU.add, ALU.max)
+                nc.vector.tensor_scalar(rows[a][qh][:, t, :], acc[:], bias, 0.0, ALU.add, ALU.max)
             else:
-                nc.scalar.activation(rows[a][h][:, t, :], acc[:], ACT.Relu, bias=bias)
+                nc.scalar.activation(rows[a][qh][:, t, :], acc[:], ACT.Relu, bias=bias)
 
         rows = [[new_rows(), new_rows()], [at(32, "h_rows1_0", [P, PACK, HALF], BF16), new_rows()]]
         h_codes = [
             [held("h_codes0_0", [P, HALF], U32), at(32, "h_codes0_1", [P, HALF], U32)],
             [held("h_codes1_0", [P, HALF], U32), held("h_codes1_1", [P, HALF], U32)],
         ]
-        h_planes = [[shifted("h_plane%d_%d" % (a, h), HALF, U8, PLANE_LEAD) for h in range(2)] for a in range(2)]
+        h_planes = [[shifted("h_plane%d_%d" % (a, qh), HALF, U8, PLANE_LEAD) for qh in range(2)] for a in range(2)]
 
         grouped = {
-            (a, h): at(4 * (2 * a + h), "h_grouped%d_%d" % (a, h), [P, HALF * PACK], BF16)
-            for a, h in ((0, 0), (1, 0), (1, 1))
+            (a, qh): at(4 * (2 * a + qh), "h_grouped%d_%d" % (a, qh), [P, HALF * PACK], BF16)
+            for a, qh in ((0, 0), (1, 0), (1, 1))
         }
         grouped_01 = [at(kib, "h_grouped0_1_at%d" % kib, [P, PART * PACK], BF16) for kib in (4, 34)]
 
-        def grouped_cols(a, h, cols):
-            if (a, h) == (0, 1):
+        def grouped_cols(a, qh, cols):
+            if (a, qh) == (0, 1):
                 return grouped_01[cols.start // PART][:]
-            return grouped[a, h][:, PACK * cols.start : PACK * cols.stop]
+            return grouped[a, qh][:, PACK * cols.start : PACK * cols.stop]
 
-        def interleave(a, h, cols):
+        def interleave(a, qh, cols):
             nc.vector.tensor_copy(
-                grouped_cols(a, h, cols).rearrange("p (c i t) -> p c t i", i=4, t=PACK),
-                rows[a][h][:, :, cols].rearrange("p t (c i) -> p c t i", i=4),
+                grouped_cols(a, qh, cols).rearrange("p (c i t) -> p c t i", i=4, t=PACK),
+                rows[a][qh][:, :, cols].rearrange("p t (c i) -> p c t i", i=4),
             )
 
-        def quantize_h(a, h, cols):
+        def quantize_h(a, qh, cols):
             nc.vector.quantize_mx(
-                out=h_codes[a][h][:, cols].bitcast(FP8X4),
-                scales=h_planes[a][h][:, cols],
-                in_=grouped_cols(a, h, cols),
+                out=h_codes[a][qh][:, cols].bitcast(FP8X4),
+                scales=h_planes[a][qh][:, cols],
+                in_=grouped_cols(a, qh, cols),
             )
 
-        def cost_pass(acc, a, i, h, cols, start, stop):
+        def cost_pass(acc, a, i, qh, cols, start, stop):
             nc.tensor.matmul_mx(
                 out=acc,
                 lhsT=wc_codes[:, a, i * P : (i + 1) * P].bitcast(FP8X4),
                 lhsT_scale=wc_planes[COST_ROW:P, a, :].bitcast(U8)[:, i * P : (i + 1) * P],
-                rhs=h_codes[a][h][:, cols].bitcast(FP8X4),
-                rhs_scale=h_planes[a][h][:, cols],
+                rhs=h_codes[a][qh][:, cols].bitcast(FP8X4),
+                rhs_scale=h_planes[a][qh][:, cols],
                 start=start,
                 stop=stop,
             )
@@ -314,25 +314,25 @@ def tile_list_supplier_shortage_cost_kernel(
         nc.vector.tensor_copy(*wd_sorted(0))
         dst, src = ws_views(0, ws_raw0, slice(0, P))
         nc.scalar.activation(dst, src, ACT.Copy, scale=-1.0)
-        accs = [[bank(h, t) for t in range(PACK)] for h in range(2)]
-        for h in range(2):
-            gather_v(0, h, whole)
+        accs = [[bank(qh, t) for t in range(PACK)] for qh in range(2)]
+        for qh in range(2):
+            gather_v(0, qh, whole)
             for t in range(PACK):
-                demand_pass(accs[h][t], 0, 0, t, h, whole, True, False)
+                demand_pass(accs[qh][t], 0, 0, t, qh, whole, True, False)
         gather_v2(0)
         quantize_ws(ws_codes0, ws_plane0[:], ws_bf[0][:])
         gather_v2(1)
-        for h in range(2):
+        for qh in range(2):
             for t in range(PACK):
-                stock_pass(accs[h][t], 0, t, h, False, False)
+                stock_pass(accs[qh][t], 0, t, qh, False, False)
         nc.scalar.copy(*wd_sorted(1))
-        for h in range(2):
+        for qh in range(2):
             for cols in parts:
-                gather_v(1, h, cols)
+                gather_v(1, qh, cols)
                 for t in range(PACK):
-                    demand_pass(accs[h][t], 1, 0, t, h, cols, False, cols == parts[1])
+                    demand_pass(accs[qh][t], 1, 0, t, qh, cols, False, cols == parts[1])
                     if cols == parts[1]:
-                        shortage(0, h, t, accs[h][t])
+                        shortage(0, qh, t, accs[qh][t])
 
         nc.vector.tensor_copy(wd_codes1, wd_raw1[:].bitcast(U16).rearrange("p g (x t) -> p g t x", t=PACK))
         for c in range(2):
@@ -385,8 +385,8 @@ def tile_list_supplier_shortage_cost_kernel(
             acc = bank(1, b)
             for a in range(2):
                 for e in range(2):
-                    first, final = (a, e) == (0, 0), (a, e) == (1, 1)
-                    cost_pass(acc[:, parts[e]], a, 2 * b + e, 1, parts[0], first, final)
+                    opens, closes = (a, e) == (0, 0), (a, e) == (1, 1)
+                    cost_pass(acc[:, parts[e]], a, 2 * b + e, 1, parts[0], opens, closes)
             result = outs.tile([P, HALF], F32, name="result")
             target = out[2 * b * P : 2 * (b + 1) * P, HALF : HALF + PART]
             for e in range(2):

@@ -24,12 +24,12 @@ PART = HALF // 2
 LIST_ROWS = 16
 BLOCKS = 16
 QUADRANT = 32
-SPREAD = 4
+FIRST = 96
 SPREAD2, FIRST2 = 7, 4
 STOCK_ROW = 4
 COST_ROW = 8
+WS_CUTS = (256, 384)
 KIB = 1024
-WS_SPLIT = 384
 
 PLANE_LEAD = 64
 STATIONARY_LEAD = 128
@@ -43,7 +43,6 @@ def tile_list_supplier_shortage_cost_kernel(
     with ExitStack() as ctx:
         keep = ctx.enter_context(tc.tile_pool(name="keep", bufs=1))
         placed = ctx.enter_context(tc.tile_pool(name="placed", bufs=1))
-        ring = ctx.enter_context(tc.tile_pool(name="ring", bufs=3))
         outs = ctx.enter_context(tc.tile_pool(name="outs", bufs=8))
         psum = ctx.enter_context(tc.psum_pool(name="psum", bufs=1))
 
@@ -59,153 +58,109 @@ def tile_list_supplier_shortage_cost_kernel(
         idx = keep.tile([P, S // LIST_ROWS], U16, name="idx")
         idx2 = keep.tile([P, S // LIST_ROWS], U16, name="idx2")
         v_scale_table = held("v_scale_table", [P, T // 4], I32)
-        wd_scale_raw = held("wd_scale_raw", [P, K_PASS // 4], I32)
-        wd_scale_late = held("wd_scale_late", [P, 2, K_PASS // 4], I32)
-        stage = [held("stage0", [P, (S + K_PASS) // 4], I32)]
-        plane0 = shifted("plane0", (S + K_PASS) // 4, I32, PLANE_LEAD // 4)
-        plane1 = shifted("plane1", (S + 3 * K_PASS) // 4, I32, PLANE_LEAD // 4)
+        wd_scale_raw = held("wd_scale_raw", [P, H // 4], I32)
+        v2_scale_table = held("v2_scale_table", [P, T2 // 4], I32)
+        v_scale_picked = held("v_scale_picked", [P, S], U8)
+        v2_scale_picked = held("v2_scale_picked", [P, S], U8)
+        planes = [shifted("plane%d" % g, (S + H) // 4, I32, PLANE_LEAD // 4) for g in range(2)]
+        stage = planes[1]
         v2_plane = shifted("v2_plane", S // 4, I32, PLANE_LEAD // 4)
         warm = held("warm", [P, 2], F32)
-
-        v_scale_picked = held("v_scale_picked", [P, S], U8)
-        v2_scale_table = held("v2_scale_table", [P, T2 // 4], I32)
-        v2_scale_picked = held("v2_scale_picked", [P, S], U8)
 
         def words(ap):
             return ap.rearrange("p t i -> p (t i)").bitcast(I32)
 
-        def ws_half(a):
-            return ws[:, a * K_PASS : (a + 1) * K_PASS].rearrange("(p j) c -> p j c", j=PACK)
-
-        def wd_half(a):
-            pairs = K_PASS // 2
-            return wd_words.bitcast(I32)[:, :, a * pairs : (a + 1) * pairs].rearrange("g p w -> p g w")
-
-        wd_raw0 = [held("wd_raw0_%d" % g, [P, K_PASS // 2], I32) for g in range(2)]
-        v_table0 = at(16, "v_table0", [P, T], I32)
-
-        nc.vector.memset(v_scale_table[:], 0)
-        nc.vector.memset(wd_scale_raw[:], 0)
-        nc.vector.memset(wd_scale_late[:], 0)
         nc.vector.memset(v2_scale_table[:], 0)
-        ws_raw0 = held("ws_raw0", [P, PACK, K_PASS], F32)
-        nc.sync.dma_start(ws_raw0[:, :2, :], ws_half(0)[:, :2, :])
-        nc.sync.dma_start(v_scale_table[0:P:SPREAD, :], tab_scales.bitcast(I32).rearrange("g q w -> (g q) w"))
+        nc.vector.memset(v_scale_table[:FIRST, :], 0)
+        nc.vector.memset(wd_scale_raw[:FIRST, :], 0)
+        wd_raw = [held("wd_raw%d" % g, [P, H // 2], I32) for g in range(2)]
+        nc.sync.dma_start(v_scale_table[FIRST:, :], tab_scales.bitcast(I32).rearrange("g q w -> (g q) w"))
         nc.sync.dma_start(idx[:], offs)
-        wd_scale_words = wd_scales.bitcast(I32)
-        nc.sync.dma_start(wd_scale_raw[0:P:SPREAD, :], wd_scale_words.rearrange("g q w -> (g q) w")[:, : K_PASS // 4])
-        nc.sync.dma_start(wd_raw0[0][:], wd_half(0)[:, 0, :])
-        nc.sync.dma_start(ws_raw0[:, 2:, :], ws_half(0)[:, 2:, :])
+        nc.sync.dma_start(wd_scale_raw[FIRST:, :], wd_scales.bitcast(I32).rearrange("g q w -> (g q) w"))
+        nc.sync.dma_start(wd_raw[0][:], wd_words[0].bitcast(I32))
         nc.sync.dma_start(v2_scale_table[FIRST2 : FIRST2 + SPREAD2 * BLOCKS : SPREAD2, :], tab2_scales[0].bitcast(I32))
         nc.sync.dma_start(idx2[:], offs2)
-        nc.sync.dma_start(
-            wd_scale_late[SPREAD * BLOCKS : P : SPREAD, :, :],
-            wd_scale_words[:, :, K_PASS // 4 :].rearrange("g q w -> q g w"),
-        )
-        nc.sync.dma_start(v_table0[:], words(tab_words[0]))
+        safety_sb = held("safety_sb", [P, 2, PACK], F32)
+        nc.sync.dma_start(safety_sb[:], safety.rearrange("(a p t) -> p a t", a=2, t=PACK))
+        v_table = [at(0, "v_table0", [P, T], I32), held("v_table1", [P, T], I32)]
+        nc.sync.dma_start(v_table[0][:], words(tab_words[0]))
 
         nc.vector.memset(warm[:, 0:1], 0.0)
         nc.scalar.activation(warm[:, 1:2], warm[:, 0:1], ACT.Relu)
-        nc.vector.memset(plane0[:], 0)
-        nc.vector.memset(v2_plane[:], 0)
-        nc.vector.memset(plane1[:], 0)
-        wc_planes = held("wc_planes", [P, 2, N // 4], I32)
-        nc.vector.memset(wc_planes[:], 0)
+        nc.vector.memset(planes[0], 0)
+        nc.vector.memset(v2_plane, 0)
 
         nc.vector.tensor_copy(v_scale_picked[:], v_scale_table[:].bitcast(U8).indirect(idx[:]))
         nc.vector.tensor_copy(
-            stage[0][:, S // 4 :].bitcast(U8).rearrange("p (t x) -> p t x", t=PACK),
-            wd_scale_raw[:].bitcast(U8).rearrange("p (x t) -> p t x", t=PACK),
+            stage[:, S // 4 :].bitcast(U8).rearrange("p (a t x) -> p a t x", a=2, t=PACK),
+            wd_scale_raw[:].bitcast(U8).rearrange("p (a x t) -> p a t x", a=2, t=PACK),
         )
-        nc.vector.tensor_copy(stage[0][:, : S // 4], v_scale_picked[:].bitcast(I32))
+        nc.vector.tensor_copy(stage[:, : S // 4], v_scale_picked[:].bitcast(I32))
+        nc.vector.tensor_copy(v2_scale_picked[:], v2_scale_table[:].bitcast(U8).indirect(idx2[:]))
 
-        def move_plane(plane, g):
+        def move_plane(g):
             for s in range(4):
-                sources = slice(SPREAD * (BLOCKS * g + s), SPREAD * BLOCKS * (g + 1), 4 * SPREAD)
-                nc.sync.dma_start(plane[s:P:QUADRANT, :], stage[g][sources, :])
+                sources = slice(FIRST + BLOCKS * g + s, FIRST + BLOCKS * (g + 1), 4)
+                nc.sync.dma_start(planes[g][s:P:QUADRANT, :], stage[sources, :])
 
-        move_plane(plane0, 0)
+        nc.sync.dma_start(v_table[1][:, : T // 2], words(tab_words[1])[:, : T // 2])
+        move_plane(0)
+        nc.sync.dma_start(v_table[1][:, T // 2 :], words(tab_words[1])[:, T // 2 :])
+        nc.sync.dma_start(wd_raw[1][:], wd_words[1].bitcast(I32))
+        move_plane(1)
         v2_table = held("v2_table", [P, T2], I32)
         nc.sync.dma_start(v2_table[:], words(tab2_words[0]))
-
-        nc.vector.tensor_copy(v2_scale_picked[:, :S], v2_scale_table[:].bitcast(U8).indirect(idx2[:]))
-        v_table = [v_table0, held("v_table1", [P, T], I32)]
-        nc.sync.dma_start(v_table[1][:, : T // 2], words(tab_words[1])[:, : T // 2])
         for s in range(4):
             nc.sync.dma_start(
                 v2_plane[STOCK_ROW + s : P : QUADRANT, :],
-                v2_scale_picked[FIRST2 + SPREAD2 * s : FIRST2 + SPREAD2 * BLOCKS : 4 * SPREAD2, :S].bitcast(I32),
+                v2_scale_picked[FIRST2 + SPREAD2 * s : FIRST2 + SPREAD2 * BLOCKS : 4 * SPREAD2, :].bitcast(I32),
             )
-        nc.sync.dma_start(v_table[1][:, T // 2 :], words(tab_words[1])[:, T // 2 :])
-
-        nc.sync.dma_start(wd_raw0[1][:], wd_half(0)[:, 1, :])
-        safety_sb = held("safety_sb", [P, 2, PACK], F32)
-        nc.sync.dma_start(safety_sb[:], safety.rearrange("(a p t) -> p a t", a=2, t=PACK))
-
-        stage.append(at(24, "stage1", [P, (S + 3 * K_PASS) // 4], I32))
-        nc.vector.tensor_copy(stage[1][:, : (S + K_PASS) // 4], stage[0][:])
-        nc.vector.tensor_copy(
-            stage[1][:, (S + K_PASS) // 4 :].bitcast(U8).rearrange("p (g t x) -> p g t x", g=2, t=PACK),
-            wd_scale_late[:].bitcast(U8).rearrange("p g (x t) -> p g t x", t=PACK),
-        )
-        move_plane(plane1, 1)
-
-        wd_raw1 = held("wd_raw1", [P, 2, K_PASS // 2], I32)
-        ws_cols1 = [slice(0, WS_SPLIT), slice(WS_SPLIT, K_PASS)]
-        ws_raw1 = [
-            held("ws_raw1_%d" % c, [P, PACK, cols.stop - cols.start], F32)
-            for c, cols in enumerate(ws_cols1)
+        ws_cols = [[slice(0, cut), slice(cut, K_PASS)] for cut in WS_CUTS]
+        ws_raw = [
+            [held("ws_raw%d_%d" % (a, c), [P, PACK, cols.stop - cols.start], F32) for c, cols in enumerate(ws_cols[a])]
+            for a in range(2)
         ]
+        for a in range(2):
+            half = ws[:, a * K_PASS : (a + 1) * K_PASS].rearrange("(p j) c -> p j c", j=PACK)
+            for c in range(2):
+                nc.sync.dma_start(ws_raw[a][c][:], half[:, :, ws_cols[a][c]])
         wc_codes = shifted("wc_codes", 2 * N, I32, STATIONARY_LEAD // 4).rearrange("p (a n) -> p a n", a=2)
         base_sb = held("base_sb", [P, N // P], F32)
-        nc.sync.dma_start(wd_raw1[:], wd_half(1))
-        for c in range(2):
-            nc.sync.dma_start(ws_raw1[c][:], ws_half(1)[:, :, ws_cols1[c]])
-        nc.sync.dma_start(wc_codes[:], wc_words.rearrange("a p c i -> p a (c i)").bitcast(I32))
+        nc.sync.dma_start(wc_codes, wc_words.rearrange("a p c i -> p a (c i)").bitcast(I32))
         with nc.allow_non_contiguous_dma(reason="one value of base for each partition"):
             nc.sync.dma_start(base_sb[:], base.rearrange("(i p) -> p i", p=P))
-        for s in range(4):
-            nc.sync.dma_start(
-                wc_planes[COST_ROW + s : P : QUADRANT, :, :],
-                wc_scales[:, s:BLOCKS:4, :].bitcast(I32).rearrange("a q w -> q a w"),
-            )
 
-        wd_codes1 = shifted("wd_codes1", 2 * K_PASS, U16, STATIONARY_LEAD // 2).rearrange(
-            "p (g t x) -> p g t x", g=2, t=PACK
-        )
         wd_codes = [
-            [
-                shifted("wd_codes0_%d" % g, K_PASS, U16, STATIONARY_LEAD // 2).rearrange("p (t x) -> p t x", t=PACK)
-                for g in range(2)
-            ],
-            [wd_codes1[:, g, :, :] for g in range(2)],
+            shifted("wd_codes%d" % g, H, U16, STATIONARY_LEAD // 2).rearrange("p (a t x) -> p a t x", a=2, t=PACK)
+            for g in range(2)
         ]
+        wd_cols = [wd_raw[g][:].bitcast(U16).rearrange("p (a x t) -> p a t x", a=2, t=PACK) for g in range(2)]
+        nc.scalar.copy(wd_codes[0], wd_cols[0])
+        for a in (1, 0):
+            nc.scalar.copy(wd_codes[1][:, a, :, :], wd_cols[1][:, a, :, :])
 
-        def wd_sorted(g):
-            return wd_codes[0][g], wd_raw0[g][:].bitcast(U16).rearrange("p (x t) -> p t x", t=PACK)
-
-        ws_codes0 = at(20, "ws_codes0", [P, STATIONARY_LEAD // 4 + K_PASS], U32)[:, STATIONARY_LEAD // 4 :]
-        ws_plane0 = held("ws_plane0", [P, K_PASS], U8)
         ws_codes = [
-            [ws_codes0[:, : 2 * P], ws_codes0[:, 2 * P :]],
-            [shifted("ws_codes1_%d" % u, 2 * P, U32, STATIONARY_LEAD // 4) for u in range(2)],
+            [shifted("ws_codes%d_%d" % (a, u), 2 * P, U32, STATIONARY_LEAD // 4) for u in range(2)] for a in range(2)
         ]
-        ws_planes = [
-            [ws_plane0[:, : 2 * P], ws_plane0[:, 2 * P :]],
-            [held("ws_plane1_%d" % u, [P, 2 * P], U8)[:] for u in range(2)],
-        ]
-        ws_bf = [held("ws_bf0", [P, PACK, P, PACK], BF16), at(0, "ws_bf1", [P, PACK, P, PACK], BF16)]
+        ws_planes = [[held("ws_plane%d_%d" % (a, u), [P, 2 * P], U8)[:] for u in range(2)] for a in range(2)]
+        ws_bf = [held("ws_bf%d" % a, [P, PACK, P, PACK], BF16) for a in range(2)]
 
-        def ws_views(a, raw, xs):
-            return (
-                ws_bf[a][:, :, xs, :].rearrange("p t x j -> p x j t"),
-                raw[:].rearrange("p j (x t) -> p x j t", t=PACK),
-            )
+        def round_ws(a, c, on_vector):
+            xs = slice(ws_cols[a][c].start // PACK, ws_cols[a][c].stop // PACK)
+            dst = ws_bf[a][:, :, xs, :].rearrange("p t x j -> p x j t")
+            src = ws_raw[a][c][:].rearrange("p j (x t) -> p x j t", t=PACK)
+            if on_vector:
+                nc.vector.tensor_scalar(dst, src, -1.0, None, ALU.mult)
+            else:
+                nc.scalar.activation(dst, src, ACT.Copy, scale=-1.0)
 
-        def quantize_ws(codes, plane, values):
-            nc.vector.quantize_mx(
-                out=codes.bitcast(FP8X4), scales=plane, in_=values.rearrange("p t x j -> p (t x j)")
-            )
+        def quantize_ws(a):
+            for u in range(2):
+                nc.vector.quantize_mx(
+                    out=ws_codes[a][u].bitcast(FP8X4),
+                    scales=ws_planes[a][u],
+                    in_=ws_bf[a][:, 2 * u : 2 * u + 2, :, :].rearrange("p t x j -> p (t x j)"),
+                )
 
         whole = slice(0, HALF)
         parts = [slice(0, PART), slice(PART, HALF)]
@@ -217,7 +172,7 @@ def tile_list_supplier_shortage_cost_kernel(
             return slice(queries(qh, cols).start // LIST_ROWS, queries(qh, cols).stop // LIST_ROWS)
 
         v_codes = [[held("v_codes%d_%d" % (g, qh), [P, HALF], U32) for qh in range(2)] for g in range(2)]
-        v2_codes = [at(16 + 2 * qh, "v2_codes%d" % qh, [P, HALF], U32) for qh in range(2)]
+        v2_codes = [held("v2_codes%d" % qh, [P, HALF], U32) for qh in range(2)]
 
         def gather_v(g, qh, cols):
             nc.vector.tensor_copy(v_codes[g][qh][:, cols], v_table[g][:].bitcast(U32).indirect(idx[:, list_cols(qh, cols)]))
@@ -225,72 +180,75 @@ def tile_list_supplier_shortage_cost_kernel(
         def gather_v2(qh):
             nc.vector.tensor_copy(v2_codes[qh][:], v2_table[:].bitcast(U32).indirect(idx2[:, list_cols(qh, whole)]))
 
-        plane_bytes = [plane0[:].bitcast(U8), plane1[:].bitcast(U8)]
+        plane_bytes = [planes[g].bitcast(U8) for g in range(2)]
 
         def demand_pass(acc, g, a, t, qh, cols, start, stop):
-            wd_col = S + a * (1 + g) * K_PASS + t * P
+            wd_col = S + a * K_PASS + t * P
             nc.tensor.matmul_mx(
                 out=acc[:, cols],
-                lhsT=wd_codes[a][g][:, t, :].bitcast(U8).bitcast(FP4X4),
-                lhsT_scale=plane_bytes[max(g, a)][:, wd_col : wd_col + P],
+                lhsT=wd_codes[g][:, a, t, :].bitcast(U8).bitcast(FP4X4),
+                lhsT_scale=plane_bytes[g][:, wd_col : wd_col + P],
                 rhs=v_codes[g][qh][:, cols].bitcast(FP8X4),
                 rhs_scale=plane_bytes[g][:, queries(qh, cols)],
                 start=start,
                 stop=stop,
             )
 
-        def stock_pass(acc, a, t, qh, start, stop):
+        def stock_pass(acc, a, t, qh, cols, start, stop):
             nc.tensor.matmul_mx(
-                out=acc[:],
+                out=acc,
                 lhsT=ws_codes[a][t // 2][:, t % 2 * P : (t % 2 + 1) * P].bitcast(FP8X4),
                 lhsT_scale=ws_planes[a][t // 2][:, t % 2 * P : (t % 2 + 1) * P],
-                rhs=v2_codes[qh][:].bitcast(FP8X4),
-                rhs_scale=v2_plane[STOCK_ROW:P, :].bitcast(U8)[:, queries(qh, whole)],
+                rhs=v2_codes[qh][:, cols].bitcast(FP8X4),
+                rhs_scale=v2_plane[STOCK_ROW:P, :].bitcast(U8)[:, queries(qh, cols)],
                 start=start,
                 stop=stop,
             )
 
-        def bank(qh, b):
-            return psum.tile([P, HALF], F32, name="bank%d" % (PACK * qh + b))
+        def bank(b):
+            return psum.tile([P, HALF], F32, name="bank%d" % b)
 
-        def new_rows():
-            return ring.tile([P, PACK, HALF], BF16, name="h_rows", align_bytes=256)
+        rows = {key: held("h_rows%d_%d" % key, [P, PACK, HALF], BF16) for key in ((0, 0), (0, 1), (1, 1))}
+        parked = held("parked", [P, PACK, HALF], F32)
+        pairs = held("pairs", [P, 2, HALF, 2], BF16)
+        tiles = ((0, 0), (0, 1), (1, 0), (1, 1))
+        grouped = {key: held("h_grouped%d_%d" % key, [P, HALF * PACK], BF16) for key in tiles}
+        h_codes = {key: held("h_codes%d_%d" % key, [P, HALF], U32) for key in tiles}
+        h_planes = {key: shifted("h_plane%d_%d" % key, HALF, U8, PLANE_LEAD) for key in tiles}
 
-        def shortage(a, qh, t, acc, on_vector=False):
-            bias = safety_sb[:, a, t : t + 1]
-            if on_vector:
-                nc.vector.tensor_scalar(rows[a][qh][:, t, :], acc[:], bias, 0.0, ALU.add, ALU.max)
-            else:
-                nc.scalar.activation(rows[a][qh][:, t, :], acc[:], ACT.Relu, bias=bias)
-
-        rows = [[new_rows(), new_rows()], [at(32, "h_rows1_0", [P, PACK, HALF], BF16), new_rows()]]
-        h_codes = [
-            [held("h_codes0_0", [P, HALF], U32), at(32, "h_codes0_1", [P, HALF], U32)],
-            [held("h_codes1_0", [P, HALF], U32), held("h_codes1_1", [P, HALF], U32)],
-        ]
-        h_planes = [[shifted("h_plane%d_%d" % (a, qh), HALF, U8, PLANE_LEAD) for qh in range(2)] for a in range(2)]
-
-        grouped = {
-            (a, qh): at(4 * (2 * a + qh), "h_grouped%d_%d" % (a, qh), [P, HALF * PACK], BF16)
-            for a, qh in ((0, 0), (1, 0), (1, 1))
-        }
-        grouped_01 = [at(kib, "h_grouped0_1_at%d" % kib, [P, PART * PACK], BF16) for kib in (4, 34)]
+        def shortage(a, qh, t, acc):
+            nc.scalar.activation(rows[a, qh][:, t, :], acc[:], ACT.Relu, bias=safety_sb[:, a, t : t + 1])
 
         def grouped_cols(a, qh, cols):
-            if (a, qh) == (0, 1):
-                return grouped_01[cols.start // PART][:]
             return grouped[a, qh][:, PACK * cols.start : PACK * cols.stop]
 
         def interleave(a, qh, cols):
             nc.vector.tensor_copy(
                 grouped_cols(a, qh, cols).rearrange("p (c i t) -> p c t i", i=4, t=PACK),
-                rows[a][qh][:, :, cols].rearrange("p t (c i) -> p c t i", i=4),
+                rows[a, qh][:, :, cols].rearrange("p t (c i) -> p c t i", i=4),
+            )
+
+        def add_parked(acc, u, cols):
+            nc.vector.tensor_tensor(
+                pairs[:, u, cols, :].rearrange("p (c i) e -> p c e i", i=4),
+                acc[:].rearrange("p (e c i) -> p c e i", e=2, i=4),
+                parked[:, 2 * u : 2 * u + 2, cols].rearrange("p e (c i) -> p c e i", i=4),
+                ALU.add,
+            )
+
+        def join_pairs(cols):
+            nc.vector.tensor_scalar(
+                grouped_cols(1, 0, cols).rearrange("p (c u e) -> p c u e", u=2, e=2),
+                pairs[:, :, cols, :].rearrange("p u c e -> p c u e"),
+                0.0,
+                None,
+                ALU.max,
             )
 
         def quantize_h(a, qh, cols):
             nc.vector.quantize_mx(
-                out=h_codes[a][qh][:, cols].bitcast(FP8X4),
-                scales=h_planes[a][qh][:, cols],
+                out=h_codes[a, qh][:, cols].bitcast(FP8X4),
+                scales=h_planes[a, qh][:, cols],
                 in_=grouped_cols(a, qh, cols),
             )
 
@@ -299,8 +257,8 @@ def tile_list_supplier_shortage_cost_kernel(
                 out=acc,
                 lhsT=wc_codes[:, a, i * P : (i + 1) * P].bitcast(FP8X4),
                 lhsT_scale=wc_planes[COST_ROW:P, a, :].bitcast(U8)[:, i * P : (i + 1) * P],
-                rhs=h_codes[a][qh][:, cols].bitcast(FP8X4),
-                rhs_scale=h_planes[a][qh][:, cols],
+                rhs=h_codes[a, qh][:, cols].bitcast(FP8X4),
+                rhs_scale=h_planes[a, qh][:, cols],
                 start=start,
                 stop=stop,
             )
@@ -311,95 +269,96 @@ def tile_list_supplier_shortage_cost_kernel(
             else:
                 nc.scalar.activation(result, acc, ACT.Identity, bias=base_sb[:, i : i + 1])
 
-        nc.vector.tensor_copy(*wd_sorted(0))
-        dst, src = ws_views(0, ws_raw0, slice(0, P))
-        nc.scalar.activation(dst, src, ACT.Copy, scale=-1.0)
-        accs = [[bank(qh, t) for t in range(PACK)] for qh in range(2)]
-        for qh in range(2):
-            gather_v(0, qh, whole)
+        early = [bank(PACK + t) for t in range(PACK)]
+        accs = {(0, 0): [bank(t) for t in range(PACK)]}
+        gather_v(0, 0, whole)
+        for t in range(PACK):
+            demand_pass(early[t], 0, 1, t, 0, whole, True, False)
+        for t in range(PACK):
+            demand_pass(accs[0, 0][t], 0, 0, t, 0, whole, True, False)
+        gather_v(0, 1, whole)
+        wc_planes = at(0, "wc_planes", [P, 2, N // 4], I32)
+        nc.vector.memset(wc_planes[:], 0)
+        for s in range(4):
+            nc.sync.dma_start(
+                wc_planes[COST_ROW + s : P : QUADRANT, :, :],
+                wc_scales[:, s:BLOCKS:4, :].bitcast(I32).rearrange("a q w -> q a w"),
+            )
+        for cols in parts:
+            gather_v(1, 0, cols)
             for t in range(PACK):
-                demand_pass(accs[qh][t], 0, 0, t, qh, whole, True, False)
-        gather_v2(0)
-        quantize_ws(ws_codes0, ws_plane0[:], ws_bf[0][:])
-        gather_v2(1)
-        for qh in range(2):
-            for t in range(PACK):
-                stock_pass(accs[qh][t], 0, t, qh, False, False)
-        nc.scalar.copy(*wd_sorted(1))
-        for qh in range(2):
-            for cols in parts:
-                gather_v(1, qh, cols)
-                for t in range(PACK):
-                    demand_pass(accs[qh][t], 1, 0, t, qh, cols, False, cols == parts[1])
-                    if cols == parts[1]:
-                        shortage(0, qh, t, accs[qh][t])
-
-        nc.vector.tensor_copy(wd_codes1, wd_raw1[:].bitcast(U16).rearrange("p g (x t) -> p g t x", t=PACK))
-        for c in range(2):
-            dst, src = ws_views(1, ws_raw1[c], slice(ws_cols1[c].start // PACK, ws_cols1[c].stop // PACK))
-            nc.vector.tensor_scalar(dst, src, -1.0, None, ALU.mult)
-        for u in range(2):
-            quantize_ws(ws_codes[1][u], ws_planes[1][u], ws_bf[1][:, 2 * u : 2 * u + 2, :, :])
-        accs = [bank(0, t) for t in range(PACK)]
+                demand_pass(early[t], 1, 1, t, 0, cols, False, cols == parts[1])
+                if cols == parts[1]:
+                    nc.scalar.activation(parked[:, t, :], early[t][:], ACT.Identity, bias=safety_sb[:, 1, t : t + 1])
+        gather_v(1, 1, whole)
+        for t in range(PACK):
+            demand_pass(accs[0, 0][t], 1, 0, t, 0, whole, False, False)
+        accs[0, 1] = [bank(PACK + t) for t in range(PACK)]
         for t in range(PACK):
             for g in range(2):
-                demand_pass(accs[t], g, 1, t, 0, whole, g == 0, False)
-        last = PACK - 1
-        for t in range(last):
-            stock_pass(accs[t], 1, t, 0, False, True)
-            shortage(1, 0, t, accs[t])
-        stock_pass(accs[last], 1, last, 0, False, True)
-        interleave(0, 0, whole)
-        shortage(1, 0, last, accs[last], on_vector=True)
-        interleave(0, 1, parts[0])
-        quantize_h(0, 0, whole)
-        for cols in parts:
-            interleave(1, 0, cols)
-        for cols in parts:
-            quantize_h(1, 0, cols)
-        interleave(0, 1, parts[1])
-        quantize_h(0, 1, parts[0])
+                demand_pass(accs[0, 1][t], g, 0, t, 1, whole, g == 0, False)
+        for qh in range(2):
+            gather_v2(qh)
 
+        round_ws(0, 0, False)
+        round_ws(0, 1, True)
+        quantize_ws(0)
+        for qh in range(2):
+            for t in range(PACK):
+                stock_pass(accs[0, qh][t][:], 0, t, qh, whole, False, True)
+                shortage(0, qh, t, accs[0, qh][t])
+        for c in range(2):
+            round_ws(1, c, True)
+        quantize_ws(1)
+
+        stock = {}
+        for n, cols in enumerate(parts):
+            for u in range(2):
+                stock[n, u] = bank(2 * n + u)
+                for e in range(2):
+                    stock_pass(stock[n, u][:, parts[e]], 1, 2 * u + e, 0, cols, e == 0, e == 1)
         for t in range(PACK):
-            acc = bank(1, t)
+            acc = bank(PACK + t)
             for g in range(2):
                 demand_pass(acc, g, 1, t, 1, whole, g == 0, False)
-            stock_pass(acc, 1, t, 1, False, True)
+            stock_pass(acc[:], 1, t, 1, whole, False, True)
             shortage(1, 1, t, acc)
+        add_parked(stock[0, 0], 0, parts[0])
+        add_parked(stock[0, 1], 1, parts[0])
+        interleave(0, 0, whole)
+        join_pairs(parts[0])
+        quantize_h(0, 0, whole)
+        quantize_h(1, 0, parts[0])
+        add_parked(stock[1, 0], 0, parts[1])
+        add_parked(stock[1, 1], 1, parts[1])
+        interleave(0, 1, parts[0])
+        join_pairs(parts[1])
+        quantize_h(0, 1, parts[0])
+        quantize_h(1, 0, parts[1])
         interleave(1, 1, parts[0])
-        quantize_h(0, 1, parts[1])
+        interleave(0, 1, parts[1])
         quantize_h(1, 1, parts[0])
         interleave(1, 1, parts[1])
+        quantize_h(0, 1, parts[1])
         quantize_h(1, 1, parts[1])
 
-        for i in range(N // P):
-            acc = bank(0, i)
-            for a in range(2):
-                cost_pass(acc[:], a, i, 0, whole, a == 0, a == 1)
-            result = outs.tile([P, HALF], F32, name="result")
-            for cols in parts if i == 0 else [whole]:
-                add_base(result[:, cols], acc[:, cols], i, False)
-                nc.sync.dma_start(out[i * P : (i + 1) * P, cols], result[:, cols])
-
-        for b in range(2):
-            acc = bank(1, b)
-            for a in range(2):
+        for n, (qh, cols) in enumerate(((0, parts[0]), (0, parts[1]), (1, parts[0]))):
+            for b in range(2):
+                acc = bank(2 * n + b)
+                for a in range(2):
+                    for e in range(2):
+                        opens, closes = (a, e) == (0, 0), (a, e) == (1, 1)
+                        cost_pass(acc[:, parts[e]], a, 2 * b + e, qh, cols, opens, closes)
+                result = outs.tile([P, HALF], F32, name="result")
                 for e in range(2):
-                    opens, closes = (a, e) == (0, 0), (a, e) == (1, 1)
-                    cost_pass(acc[:, parts[e]], a, 2 * b + e, 1, parts[0], opens, closes)
-            result = outs.tile([P, HALF], F32, name="result")
-            target = out[2 * b * P : 2 * (b + 1) * P, HALF : HALF + PART]
-            for e in range(2):
-                add_base(result[:, parts[e]], acc[:, parts[e]], 2 * b + e, b == 1)
-                if b == 0:
-                    nc.scalar.dma_start(target[e * P : (e + 1) * P, :], result[:, parts[e]])
-            if b == 1:
+                    add_base(result[:, parts[e]], acc[:, parts[e]], 2 * b + e, False)
+                target = out[2 * b * P : 2 * (b + 1) * P, queries(qh, cols)]
                 nc.sync.dma_start(
                     target.rearrange("(e p) c -> p e c", e=2), result[:].rearrange("p (e c) -> p e c", e=2)
                 )
 
         for i in range(N // P):
-            acc = bank(1 - i // 2, 2 + i % 2)
+            acc = bank((6 + i) % 8)
             for a in range(2):
                 cost_pass(acc[:, :PART], a, i, 1, parts[1], a == 0, a == 1)
             result = outs.tile([P, PART], F32, name="last_result")

@@ -63,7 +63,7 @@ def tile_list_supplier_shortage_cost_kernel(
         v_scale_picked = held("v_scale_picked", [P, S], U8)
         v2_scale_picked = held("v2_scale_picked", [P, S], U8)
         planes = [shifted("plane%d" % g, (S + H) // 4, I32, PLANE_LEAD // 4) for g in range(2)]
-        stage = planes[1]
+        stage = held("stage", [P, (S + H) // 4], I32)
         v2_plane = shifted("v2_plane", S // 4, I32, PLANE_LEAD // 4)
         warm = held("warm", [P, 2], F32)
 
@@ -87,7 +87,8 @@ def tile_list_supplier_shortage_cost_kernel(
 
         nc.vector.memset(warm[:, 0:1], 0.0)
         nc.scalar.activation(warm[:, 1:2], warm[:, 0:1], ACT.Relu)
-        nc.vector.memset(planes[0], 0)
+        for g in range(2):
+            nc.vector.memset(planes[g], 0)
         nc.vector.memset(v2_plane, 0)
 
         nc.vector.tensor_copy(v_scale_picked[:], v_scale_table[:].bitcast(U8).indirect(idx[:]))
@@ -230,9 +231,9 @@ def tile_list_supplier_shortage_cost_kernel(
 
         def add_parked(acc, u, cols):
             nc.vector.tensor_tensor(
-                pairs[:, u, cols, :].rearrange("p (c i) e -> p c e i", i=4),
-                acc[:].rearrange("p (e c i) -> p c e i", e=2, i=4),
-                parked[:, 2 * u : 2 * u + 2, cols].rearrange("p e (c i) -> p c e i", i=4),
+                pairs[:, u, cols, :],
+                acc[:].rearrange("p (e c) -> p c e", e=2),
+                parked[:, 2 * u : 2 * u + 2, cols].rearrange("p e c -> p c e"),
                 ALU.add,
             )
 

@@ -28,7 +28,7 @@ FIRST = 96
 SPREAD2, FIRST2 = 7, 4
 STOCK_ROW = 4
 COST_ROW = 8
-WS_CUTS = (256, 384)
+WS_CUT = 384
 KIB = 1024
 
 PLANE_LEAD = 64
@@ -73,11 +73,12 @@ def tile_list_supplier_shortage_cost_kernel(
         nc.vector.memset(v2_scale_table[:], 0)
         nc.vector.memset(v_scale_table[:FIRST, :], 0)
         nc.vector.memset(wd_scale_raw[:FIRST, :], 0)
-        wd_raw = [held("wd_raw%d" % g, [P, H // 2], I32) for g in range(2)]
+        wd_raw0 = held("wd_raw0", [P, H // 2], I32)
+        wd_raw1 = [held("wd_raw1_%d" % a, [P, K_PASS // 2], I32) for a in range(2)]
         nc.sync.dma_start(v_scale_table[FIRST:, :], tab_scales.bitcast(I32).rearrange("g q w -> (g q) w"))
         nc.sync.dma_start(idx[:], offs)
         nc.sync.dma_start(wd_scale_raw[FIRST:, :], wd_scales.bitcast(I32).rearrange("g q w -> (g q) w"))
-        nc.sync.dma_start(wd_raw[0][:], wd_words[0].bitcast(I32))
+        nc.sync.dma_start(wd_raw0[:], wd_words[0].bitcast(I32))
         nc.sync.dma_start(v2_scale_table[FIRST2 : FIRST2 + SPREAD2 * BLOCKS : SPREAD2, :], tab2_scales[0].bitcast(I32))
         nc.sync.dma_start(idx2[:], offs2)
         safety_sb = held("safety_sb", [P, 2, PACK], F32)
@@ -104,27 +105,35 @@ def tile_list_supplier_shortage_cost_kernel(
                 sources = slice(FIRST + BLOCKS * g + s, FIRST + BLOCKS * (g + 1), 4)
                 nc.sync.dma_start(planes[g][s:P:QUADRANT, :], stage[sources, :])
 
-        nc.sync.dma_start(v_table[1][:, : T // 2], words(tab_words[1])[:, : T // 2])
+        ws_cols = [[slice(0, K_PASS)], [slice(0, WS_CUT), slice(WS_CUT, K_PASS)]]
+        ws_raw = [
+            [held("ws_raw%d_%d" % (a, c), [P, PACK, cols.stop - cols.start], F32) for c, cols in enumerate(ws_cols[a])]
+            for a in range(2)
+        ]
+
+        def load_ws(a):
+            half = ws[:, a * K_PASS : (a + 1) * K_PASS].rearrange("(p j) c -> p j c", j=PACK)
+            for c, cols in enumerate(ws_cols[a]):
+                nc.sync.dma_start(ws_raw[a][c][:], half[:, :, cols])
+
+        def load_wd1(a):
+            nc.sync.dma_start(wd_raw1[a][:], wd_words[1].bitcast(I32)[:, a * K_PASS // 2 : (a + 1) * K_PASS // 2])
+
+        load_ws(0)
         move_plane(0)
-        nc.sync.dma_start(v_table[1][:, T // 2 :], words(tab_words[1])[:, T // 2 :])
-        nc.sync.dma_start(wd_raw[1][:], wd_words[1].bitcast(I32))
-        move_plane(1)
         v2_table = held("v2_table", [P, T2], I32)
         nc.sync.dma_start(v2_table[:], words(tab2_words[0]))
+        nc.sync.dma_start(v_table[1][:, : T // 2], words(tab_words[1])[:, : T // 2])
         for s in range(4):
             nc.sync.dma_start(
                 v2_plane[STOCK_ROW + s : P : QUADRANT, :],
                 v2_scale_picked[FIRST2 + SPREAD2 * s : FIRST2 + SPREAD2 * BLOCKS : 4 * SPREAD2, :].bitcast(I32),
             )
-        ws_cols = [[slice(0, cut), slice(cut, K_PASS)] for cut in WS_CUTS]
-        ws_raw = [
-            [held("ws_raw%d_%d" % (a, c), [P, PACK, cols.stop - cols.start], F32) for c, cols in enumerate(ws_cols[a])]
-            for a in range(2)
-        ]
-        for a in range(2):
-            half = ws[:, a * K_PASS : (a + 1) * K_PASS].rearrange("(p j) c -> p j c", j=PACK)
-            for c in range(2):
-                nc.sync.dma_start(ws_raw[a][c][:], half[:, :, ws_cols[a][c]])
+        nc.sync.dma_start(v_table[1][:, T // 2 :], words(tab_words[1])[:, T // 2 :])
+        load_wd1(0)
+        move_plane(1)
+        load_wd1(1)
+        load_ws(1)
         wc_codes = shifted("wc_codes", 2 * N, I32, STATIONARY_LEAD // 4).rearrange("p (a n) -> p a n", a=2)
         base_sb = held("base_sb", [P, N // P], F32)
         nc.sync.dma_start(wc_codes, wc_words.rearrange("a p c i -> p a (c i)").bitcast(I32))
@@ -135,16 +144,16 @@ def tile_list_supplier_shortage_cost_kernel(
             shifted("wd_codes%d" % g, H, U16, STATIONARY_LEAD // 2).rearrange("p (a t x) -> p a t x", a=2, t=PACK)
             for g in range(2)
         ]
-        wd_cols = [wd_raw[g][:].bitcast(U16).rearrange("p (a x t) -> p a t x", a=2, t=PACK) for g in range(2)]
-        nc.scalar.copy(wd_codes[0], wd_cols[0])
-        for a in (1, 0):
-            nc.scalar.copy(wd_codes[1][:, a, :, :], wd_cols[1][:, a, :, :])
+        nc.scalar.copy(wd_codes[0], wd_raw0[:].bitcast(U16).rearrange("p (a x t) -> p a t x", a=2, t=PACK))
+
+        def wd1_sorted(a):
+            return wd_codes[1][:, a, :, :], wd_raw1[a][:].bitcast(U16).rearrange("p (x t) -> p t x", t=PACK)
 
         ws_codes = [
             [shifted("ws_codes%d_%d" % (a, u), 2 * P, U32, STATIONARY_LEAD // 4) for u in range(2)] for a in range(2)
         ]
         ws_planes = [[held("ws_plane%d_%d" % (a, u), [P, 2 * P], U8)[:] for u in range(2)] for a in range(2)]
-        ws_bf = [held("ws_bf%d" % a, [P, PACK, P, PACK], BF16) for a in range(2)]
+        ws_bf = [held("ws_bf0", [P, PACK, P, PACK], BF16), at(16, "ws_bf1", [P, PACK, P, PACK], BF16)]
 
         def round_ws(a, c, on_vector):
             xs = slice(ws_cols[a][c].start // PACK, ws_cols[a][c].stop // PACK)
@@ -186,7 +195,7 @@ def tile_list_supplier_shortage_cost_kernel(
         def demand_pass(acc, g, a, t, qh, cols, start, stop):
             wd_col = S + a * K_PASS + t * P
             nc.tensor.matmul_mx(
-                out=acc[:, cols],
+                out=acc,
                 lhsT=wd_codes[g][:, a, t, :].bitcast(U8).bitcast(FP4X4),
                 lhsT_scale=plane_bytes[g][:, wd_col : wd_col + P],
                 rhs=v_codes[g][qh][:, cols].bitcast(FP8X4),
@@ -213,7 +222,11 @@ def tile_list_supplier_shortage_cost_kernel(
         parked = held("parked", [P, PACK, HALF], F32)
         pairs = held("pairs", [P, 2, HALF, 2], BF16)
         tiles = ((0, 0), (0, 1), (1, 0), (1, 1))
-        grouped = {key: held("h_grouped%d_%d" % key, [P, HALF * PACK], BF16) for key in tiles}
+        grouped = {
+            (a, qh, n): at(16 + 2 * (4 * a + 2 * qh + n), "h_grouped%d_%d_%d" % (a, qh, n), [P, PART * PACK], BF16)
+            for a, qh in tiles
+            for n in range(2)
+        }
         h_codes = {key: held("h_codes%d_%d" % key, [P, HALF], U32) for key in tiles}
         h_planes = {key: shifted("h_plane%d_%d" % key, HALF, U8, PLANE_LEAD) for key in tiles}
 
@@ -221,10 +234,10 @@ def tile_list_supplier_shortage_cost_kernel(
             nc.scalar.activation(rows[a, qh][:, t, :], acc[:], ACT.Relu, bias=safety_sb[:, a, t : t + 1])
 
         def grouped_cols(a, qh, cols):
-            return grouped[a, qh][:, PACK * cols.start : PACK * cols.stop]
+            return grouped[a, qh, cols.start // PART][:]
 
-        def interleave(a, qh, cols):
-            nc.vector.tensor_copy(
+        def interleave(a, qh, cols, copy=nc.vector.tensor_copy):
+            copy(
                 grouped_cols(a, qh, cols).rearrange("p (c i t) -> p c t i", i=4, t=PACK),
                 rows[a, qh][:, :, cols].rearrange("p t (c i) -> p c t i", i=4),
             )
@@ -273,11 +286,19 @@ def tile_list_supplier_shortage_cost_kernel(
         early = [bank(PACK + t) for t in range(PACK)]
         accs = {(0, 0): [bank(t) for t in range(PACK)]}
         gather_v(0, 0, whole)
+        round_ws(0, 0, False)
         for t in range(PACK):
-            demand_pass(early[t], 0, 1, t, 0, whole, True, False)
+            demand_pass(early[t][:], 0, 1, t, 0, whole, True, True)
+            nc.scalar.activation(parked[:, t, :], early[t][:], ACT.Identity, bias=safety_sb[:, 1, t : t + 1])
         for t in range(PACK):
-            demand_pass(accs[0, 0][t], 0, 0, t, 0, whole, True, False)
+            demand_pass(accs[0, 0][t][:], 0, 0, t, 0, whole, True, False)
         gather_v(0, 1, whole)
+        accs[0, 1] = [bank(PACK + t) for t in range(PACK)]
+        for t in range(PACK):
+            demand_pass(accs[0, 1][t][:], 0, 0, t, 1, whole, True, False)
+        gather_v2(0)
+        quantize_ws(0)
+        gather_v2(1)
         wc_planes = at(0, "wc_planes", [P, 2, N // 4], I32)
         nc.vector.memset(wc_planes[:], 0)
         for s in range(4):
@@ -285,78 +306,78 @@ def tile_list_supplier_shortage_cost_kernel(
                 wc_planes[COST_ROW + s : P : QUADRANT, :, :],
                 wc_scales[:, s:BLOCKS:4, :].bitcast(I32).rearrange("a q w -> q a w"),
             )
-        for cols in parts:
-            gather_v(1, 0, cols)
-            for t in range(PACK):
-                demand_pass(early[t], 1, 1, t, 0, cols, False, cols == parts[1])
-                if cols == parts[1]:
-                    nc.scalar.activation(parked[:, t, :], early[t][:], ACT.Identity, bias=safety_sb[:, 1, t : t + 1])
-        gather_v(1, 1, whole)
-        for t in range(PACK):
-            demand_pass(accs[0, 0][t], 1, 0, t, 0, whole, False, False)
-        accs[0, 1] = [bank(PACK + t) for t in range(PACK)]
-        for t in range(PACK):
-            for g in range(2):
-                demand_pass(accs[0, 1][t], g, 0, t, 1, whole, g == 0, False)
-        for qh in range(2):
-            gather_v2(qh)
-
-        round_ws(0, 0, False)
-        round_ws(0, 1, True)
-        quantize_ws(0)
         for qh in range(2):
             for t in range(PACK):
-                stock_pass(accs[0, qh][t][:], 0, t, qh, whole, False, True)
-                shortage(0, qh, t, accs[0, qh][t])
+                stock_pass(accs[0, qh][t][:], 0, t, qh, whole, False, False)
+        nc.scalar.copy(*wd1_sorted(0))
+        for qh in range(2):
+            for cols in parts:
+                gather_v(1, qh, cols)
+                for t in range(PACK):
+                    demand_pass(accs[0, qh][t][:, cols], 1, 0, t, qh, cols, False, cols == parts[1])
+                    if cols == parts[1]:
+                        shortage(0, qh, t, accs[0, qh][t])
+        nc.vector.tensor_copy(*wd1_sorted(1))
         for c in range(2):
             round_ws(1, c, True)
         quantize_ws(1)
 
-        stock = {}
-        for n, cols in enumerate(parts):
-            for u in range(2):
-                stock[n, u] = bank(2 * n + u)
-                for e in range(2):
-                    stock_pass(stock[n, u][:, parts[e]], 1, 2 * u + e, 0, cols, e == 0, e == 1)
-        for t in range(PACK):
+        rest = {(n, u): bank(2 * n + u) for n in range(2) for u in range(2)}
+        for (n, u), acc in rest.items():
+            for e in range(2):
+                demand_pass(acc[:, parts[e]], 1, 1, 2 * u + e, 0, parts[n], e == 0, False)
+        for (n, u), acc in rest.items():
+            for e in range(2):
+                stock_pass(acc[:, parts[e]], 1, 2 * u + e, 0, parts[n], False, e == 1)
+        interleave(0, 1, parts[1], nc.scalar.copy)
+
+        def last_tile(t):
             acc = bank(PACK + t)
+            stock_pass(acc[:], 1, t, 1, whole, True, False)
             for g in range(2):
-                demand_pass(acc, g, 1, t, 1, whole, g == 0, False)
-            stock_pass(acc[:], 1, t, 1, whole, False, True)
+                demand_pass(acc[:], g, 1, t, 1, whole, False, g == 1)
             shortage(1, 1, t, acc)
-        add_parked(stock[0, 0], 0, parts[0])
-        add_parked(stock[0, 1], 1, parts[0])
-        interleave(0, 0, whole)
+
+        def costs(n, b, apart, on_vector):
+            qh, cols = n // 2, parts[n % 2]
+            acc = bank(2 * n + b)
+            for a in range(2):
+                for e in range(2):
+                    cost_pass(acc[:, parts[e]], a, 2 * b + e, qh, cols, (a, e) == (0, 0), (a, e) == (1, 1))
+            result = outs.tile([P, 2, PART], F32, name="result")
+            target = out[2 * b * P : 2 * (b + 1) * P, queries(qh, cols)].rearrange("(e p) c -> p e c", e=2)
+            for e in range(2):
+                add_base(result[:, e, :], acc[:, parts[e]], 2 * b + e, on_vector)
+                if apart:
+                    nc.sync.dma_start(target[:, e, :], result[:, e, :])
+            if not apart:
+                nc.sync.dma_start(target, result[:])
+
+        for t in range(PACK):
+            last_tile(t)
+        interleave(0, 0, parts[0])
+        add_parked(rest[0, 0], 0, parts[0])
+        add_parked(rest[0, 1], 1, parts[0])
+        quantize_h(0, 0, parts[0])
         join_pairs(parts[0])
-        quantize_h(0, 0, whole)
+        interleave(0, 0, parts[1])
         quantize_h(1, 0, parts[0])
-        add_parked(stock[1, 0], 0, parts[1])
-        add_parked(stock[1, 1], 1, parts[1])
-        interleave(0, 1, parts[0])
+        add_parked(rest[1, 0], 0, parts[1])
+        add_parked(rest[1, 1], 1, parts[1])
+        quantize_h(0, 0, parts[1])
         join_pairs(parts[1])
-        quantize_h(0, 1, parts[0])
+        interleave(0, 1, parts[0])
         quantize_h(1, 0, parts[1])
         interleave(1, 1, parts[0])
-        interleave(0, 1, parts[1])
+        quantize_h(0, 1, parts[0])
         quantize_h(1, 1, parts[0])
         interleave(1, 1, parts[1])
         quantize_h(0, 1, parts[1])
         quantize_h(1, 1, parts[1])
 
-        for n, (qh, cols) in enumerate(((0, parts[0]), (0, parts[1]), (1, parts[0]))):
+        for n in range(3):
             for b in range(2):
-                acc = bank(2 * n + b)
-                for a in range(2):
-                    for e in range(2):
-                        opens, closes = (a, e) == (0, 0), (a, e) == (1, 1)
-                        cost_pass(acc[:, parts[e]], a, 2 * b + e, qh, cols, opens, closes)
-                result = outs.tile([P, HALF], F32, name="result")
-                for e in range(2):
-                    add_base(result[:, parts[e]], acc[:, parts[e]], 2 * b + e, False)
-                target = out[2 * b * P : 2 * (b + 1) * P, queries(qh, cols)]
-                nc.sync.dma_start(
-                    target.rearrange("(e p) c -> p e c", e=2), result[:].rearrange("p (e c) -> p e c", e=2)
-                )
+                costs(n, b, (n, b) == (0, 0), (n, b) == (2, 1))
 
         for i in range(N // P):
             acc = bank((6 + i) % 8)

@@ -24,7 +24,7 @@ PART = HALF // 2
 LIST_ROWS = 16
 BLOCKS = 16
 QUADRANT = 32
-FIRST = 96
+SPREAD = 4
 SPREAD2, FIRST2 = 7, 4
 STOCK_ROW = 4
 COST_ROW = 8
@@ -70,21 +70,24 @@ def tile_list_supplier_shortage_cost_kernel(
         def words(ap):
             return ap.rearrange("p t i -> p (t i)").bitcast(I32)
 
+        nc.vector.memset(v_scale_table[:], 0)
+        nc.vector.memset(wd_scale_raw[:], 0)
         nc.vector.memset(v2_scale_table[:], 0)
-        nc.vector.memset(v_scale_table[:FIRST, :], 0)
-        nc.vector.memset(wd_scale_raw[:FIRST, :], 0)
+        ws_raw0 = held("ws_raw0", [P, PACK, K_PASS], F32)
+        ws_half0 = ws[:, :K_PASS].rearrange("(p j) c -> p j c", j=PACK)
+        nc.sync.dma_start(ws_raw0[:, :2, :], ws_half0[:, :2, :])
         wd_raw0 = held("wd_raw0", [P, H // 2], I32)
         wd_raw1 = [held("wd_raw1_%d" % a, [P, K_PASS // 2], I32) for a in range(2)]
-        nc.sync.dma_start(v_scale_table[FIRST:, :], tab_scales.bitcast(I32).rearrange("g q w -> (g q) w"))
+        nc.sync.dma_start(v_scale_table[0:P:SPREAD, :], tab_scales.bitcast(I32).rearrange("g q w -> (g q) w"))
         nc.sync.dma_start(idx[:], offs)
-        nc.sync.dma_start(wd_scale_raw[FIRST:, :], wd_scales.bitcast(I32).rearrange("g q w -> (g q) w"))
+        nc.sync.dma_start(wd_scale_raw[0:P:SPREAD, :], wd_scales.bitcast(I32).rearrange("g q w -> (g q) w"))
         nc.sync.dma_start(wd_raw0[:], wd_words[0].bitcast(I32))
         nc.sync.dma_start(v2_scale_table[FIRST2 : FIRST2 + SPREAD2 * BLOCKS : SPREAD2, :], tab2_scales[0].bitcast(I32))
         nc.sync.dma_start(idx2[:], offs2)
-        safety_sb = held("safety_sb", [P, 2, PACK], F32)
-        nc.sync.dma_start(safety_sb[:], safety.rearrange("(a p t) -> p a t", a=2, t=PACK))
         v_table = [at(0, "v_table0", [P, T], I32), held("v_table1", [P, T], I32)]
         nc.sync.dma_start(v_table[0][:], words(tab_words[0]))
+        safety_sb = held("safety_sb", [P, 2, PACK], F32)
+        nc.sync.dma_start(safety_sb[:], safety.rearrange("(a p t) -> p a t", a=2, t=PACK))
 
         nc.vector.memset(warm[:, 0:1], 0.0)
         nc.scalar.activation(warm[:, 1:2], warm[:, 0:1], ACT.Relu)
@@ -102,13 +105,13 @@ def tile_list_supplier_shortage_cost_kernel(
 
         def move_plane(g):
             for s in range(4):
-                sources = slice(FIRST + BLOCKS * g + s, FIRST + BLOCKS * (g + 1), 4)
+                sources = slice(SPREAD * (BLOCKS * g + s), SPREAD * BLOCKS * (g + 1), 4 * SPREAD)
                 nc.sync.dma_start(planes[g][s:P:QUADRANT, :], stage[sources, :])
 
         ws_cols = [[slice(0, K_PASS)], [slice(0, WS_CUT), slice(WS_CUT, K_PASS)]]
         ws_raw = [
-            [held("ws_raw%d_%d" % (a, c), [P, PACK, cols.stop - cols.start], F32) for c, cols in enumerate(ws_cols[a])]
-            for a in range(2)
+            [ws_raw0],
+            [held("ws_raw1_%d" % c, [P, PACK, cols.stop - cols.start], F32) for c, cols in enumerate(ws_cols[1])],
         ]
 
         def load_ws(a):
@@ -119,7 +122,7 @@ def tile_list_supplier_shortage_cost_kernel(
         def load_wd1(a):
             nc.sync.dma_start(wd_raw1[a][:], wd_words[1].bitcast(I32)[:, a * K_PASS // 2 : (a + 1) * K_PASS // 2])
 
-        load_ws(0)
+        nc.sync.dma_start(ws_raw0[:, 2:, :], ws_half0[:, 2:, :])
         move_plane(0)
         v2_table = held("v2_table", [P, T2], I32)
         nc.sync.dma_start(v2_table[:], words(tab2_words[0]))
@@ -222,11 +225,7 @@ def tile_list_supplier_shortage_cost_kernel(
         parked = held("parked", [P, PACK, HALF], F32)
         pairs = held("pairs", [P, 2, HALF, 2], BF16)
         tiles = ((0, 0), (0, 1), (1, 0), (1, 1))
-        grouped = {
-            (a, qh, n): at(16 + 2 * (4 * a + 2 * qh + n), "h_grouped%d_%d_%d" % (a, qh, n), [P, PART * PACK], BF16)
-            for a, qh in tiles
-            for n in range(2)
-        }
+        grouped = {key: at(16 + 4 * n, "h_grouped%d_%d" % key, [P, HALF * PACK], BF16) for n, key in enumerate(tiles)}
         h_codes = {key: held("h_codes%d_%d" % key, [P, HALF], U32) for key in tiles}
         h_planes = {key: shifted("h_plane%d_%d" % key, HALF, U8, PLANE_LEAD) for key in tiles}
 
@@ -234,7 +233,7 @@ def tile_list_supplier_shortage_cost_kernel(
             nc.scalar.activation(rows[a, qh][:, t, :], acc[:], ACT.Relu, bias=safety_sb[:, a, t : t + 1])
 
         def grouped_cols(a, qh, cols):
-            return grouped[a, qh, cols.start // PART][:]
+            return grouped[a, qh][:, PACK * cols.start : PACK * cols.stop]
 
         def interleave(a, qh, cols, copy=nc.vector.tensor_copy):
             copy(
@@ -355,16 +354,14 @@ def tile_list_supplier_shortage_cost_kernel(
 
         for t in range(PACK):
             last_tile(t)
-        interleave(0, 0, parts[0])
+        interleave(0, 0, whole)
         add_parked(rest[0, 0], 0, parts[0])
         add_parked(rest[0, 1], 1, parts[0])
-        quantize_h(0, 0, parts[0])
+        quantize_h(0, 0, whole)
         join_pairs(parts[0])
-        interleave(0, 0, parts[1])
-        quantize_h(1, 0, parts[0])
         add_parked(rest[1, 0], 0, parts[1])
         add_parked(rest[1, 1], 1, parts[1])
-        quantize_h(0, 0, parts[1])
+        quantize_h(1, 0, parts[0])
         join_pairs(parts[1])
         interleave(0, 1, parts[0])
         quantize_h(1, 0, parts[1])

@@ -24,8 +24,9 @@ PART = HALF // 2
 LIST_ROWS = 16
 BLOCKS = 16
 QUADRANT = 32
-SPREAD = 4
-SPREAD2, FIRST2 = 7, 4
+FIRST = 32
+SPREAD = 2
+SPREAD2 = 4
 STOCK_ROW = 4
 COST_ROW = 8
 WS_CUT = 384
@@ -78,16 +79,16 @@ def tile_list_supplier_shortage_cost_kernel(
         nc.sync.dma_start(ws_raw0[:, :2, :], ws_half0[:, :2, :])
         wd_raw0 = held("wd_raw0", [P, H // 2], I32)
         wd_raw1 = [held("wd_raw1_%d" % a, [P, K_PASS // 2], I32) for a in range(2)]
-        nc.sync.dma_start(v_scale_table[0:P:SPREAD, :], tab_scales.bitcast(I32).rearrange("g q w -> (g q) w"))
+        nc.sync.dma_start(v_scale_table[FIRST : FIRST + 64 : SPREAD, :], tab_scales.bitcast(I32).rearrange("g q w -> (g q) w"))
         nc.sync.dma_start(idx[:], offs)
-        nc.sync.dma_start(wd_scale_raw[0:P:SPREAD, :], wd_scales.bitcast(I32).rearrange("g q w -> (g q) w"))
+        nc.sync.dma_start(wd_scale_raw[FIRST : FIRST + 64 : SPREAD, :], wd_scales.bitcast(I32).rearrange("g q w -> (g q) w"))
         nc.sync.dma_start(wd_raw0[:], wd_words[0].bitcast(I32))
-        nc.sync.dma_start(v2_scale_table[FIRST2 : FIRST2 + SPREAD2 * BLOCKS : SPREAD2, :], tab2_scales[0].bitcast(I32))
+        nc.sync.dma_start(v2_scale_table[FIRST : FIRST + 64 : SPREAD2, :], tab2_scales[0].bitcast(I32))
         nc.sync.dma_start(idx2[:], offs2)
         v_table = [at(0, "v_table0", [P, T], I32), held("v_table1", [P, T], I32)]
         nc.sync.dma_start(v_table[0][:], words(tab_words[0]))
-        safety_sb = held("safety_sb", [P, 2, PACK], F32)
-        nc.sync.dma_start(safety_sb[:], safety.rearrange("(a p t) -> p a t", a=2, t=PACK))
+        safety_sb = held("safety_sb", [P, 2, 2 * PACK], F32)[:, :, :PACK]
+        nc.sync.dma_start(safety_sb, safety.rearrange("(a p t) -> p a t", a=2, t=PACK))
 
         nc.vector.memset(warm[:, 0:1], 0.0)
         nc.scalar.activation(warm[:, 1:2], warm[:, 0:1], ACT.Relu)
@@ -105,7 +106,7 @@ def tile_list_supplier_shortage_cost_kernel(
 
         def move_plane(g):
             for s in range(4):
-                sources = slice(SPREAD * (BLOCKS * g + s), SPREAD * BLOCKS * (g + 1), 4 * SPREAD)
+                sources = slice(FIRST + SPREAD * (BLOCKS * g + s), FIRST + SPREAD * BLOCKS * (g + 1), 4 * SPREAD)
                 nc.sync.dma_start(planes[g][s:P:QUADRANT, :], stage[sources, :])
 
         ws_cols = [[slice(0, K_PASS)], [slice(0, WS_CUT), slice(WS_CUT, K_PASS)]]
@@ -130,7 +131,7 @@ def tile_list_supplier_shortage_cost_kernel(
         for s in range(4):
             nc.sync.dma_start(
                 v2_plane[STOCK_ROW + s : P : QUADRANT, :],
-                v2_scale_picked[FIRST2 + SPREAD2 * s : FIRST2 + SPREAD2 * BLOCKS : 4 * SPREAD2, :].bitcast(I32),
+                v2_scale_picked[FIRST + SPREAD2 * s : FIRST + SPREAD2 * BLOCKS : 4 * SPREAD2, :].bitcast(I32),
             )
         nc.sync.dma_start(v_table[1][:, T // 2 :], words(tab_words[1])[:, T // 2 :])
         load_wd1(0)

@@ -31,6 +31,7 @@ STOCK_ROW = 4
 COST_ROW = 8
 WS_CUT = 384
 KIB = 1024
+TAB_CUT = 5 * T // 8
 
 PLANE_LEAD = 64
 STATIONARY_LEAD = 128
@@ -127,13 +128,13 @@ def tile_list_supplier_shortage_cost_kernel(
         move_plane(0)
         v2_table = held("v2_table", [P, T2], I32)
         nc.sync.dma_start(v2_table[:], words(tab2_words[0]))
-        nc.sync.dma_start(v_table[1][:, : T // 2], words(tab_words[1])[:, : T // 2])
+        nc.sync.dma_start(v_table[1][:, :TAB_CUT], words(tab_words[1])[:, :TAB_CUT])
         for s in range(4):
             nc.sync.dma_start(
                 v2_plane[STOCK_ROW + s : P : QUADRANT, :],
                 v2_scale_picked[FIRST + SPREAD2 * s : FIRST + SPREAD2 * BLOCKS : 4 * SPREAD2, :].bitcast(I32),
             )
-        nc.sync.dma_start(v_table[1][:, T // 2 :], words(tab_words[1])[:, T // 2 :])
+        nc.sync.dma_start(v_table[1][:, TAB_CUT:], words(tab_words[1])[:, TAB_CUT:])
         load_wd1(0)
         move_plane(1)
         load_wd1(1)

from contextlib import ExitStack

import concourse.mybir as mybir

K, K2, H, N, T, T2, S = 1024, 512, 1024, 512, 4096, 2048, 1024
FLOPS = 2 * S * (K * H + K2 * H + H * N)

F32 = mybir.dt.float32
BF16 = mybir.dt.bfloat16
I32 = mybir.dt.int32
U32 = mybir.dt.uint32
U16 = mybir.dt.uint16
U8 = mybir.dt.uint8
FP8X4 = mybir.dt.float8_e4m3fn_x4
FP4X4 = mybir.dt.float4_e2m1fn_x4
ALU = mybir.AluOpType
ACT = mybir.ActivationFunctionType

P = 128
PACK = 4
K_PASS = P * PACK
HALF = 512
PART = HALF // 2
LIST_ROWS = 16
BLOCKS = 16
QUADRANT = 32
FIRST = 32
SPREAD = 2
SPREAD2 = 4
STOCK_ROW = 4
COST_ROW = 8
WS_CUT = 384
KIB = 1024
TAB_CUT = 5 * T // 8

PLANE_LEAD = 64
STATIONARY_LEAD = 128


def tile_list_supplier_shortage_cost_kernel(
    tc, tab_words, tab_scales, tab2_words, tab2_scales, offs, offs2,
    wd_words, wd_scales, ws, safety, wc_words, wc_scales, base, out,
):
    nc = tc.nc
    with ExitStack() as ctx:
        keep = ctx.enter_context(tc.tile_pool(name="keep", bufs=1))
        placed = ctx.enter_context(tc.tile_pool(name="placed", bufs=1))
        outs = ctx.enter_context(tc.tile_pool(name="outs", bufs=8))
        psum = ctx.enter_context(tc.psum_pool(name="psum", bufs=1))

        def held(name, shape, dtype):
            return keep.tile(shape, dtype, name=name, align_bytes=256)

        def shifted(name, width, dtype, lead):
            return keep.tile([P, lead + width], dtype, name=name, align_bytes=256)[:, lead:]

        def at(kib, name, shape, dtype):
            return placed.tile(shape, dtype, name=name, align_bytes=256, offset=kib * KIB)

        idx = keep.tile([P, S // LIST_ROWS], U16, name="idx")
        idx2 = keep.tile([P, S // LIST_ROWS], U16, name="idx2")
        v_scale_table = held("v_scale_table", [P, T // 4], I32)
        wd_scale_raw = held("wd_scale_raw", [P, H // 4], I32)
        v2_scale_table = held("v2_scale_table", [P, T2 // 4], I32)
        v_scale_picked = held("v_scale_picked", [P, S], U8)
        v2_scale_picked = held("v2_scale_picked", [P, S], U8)
        planes = [shifted("plane%d" % g, (S + H) // 4, I32, PLANE_LEAD // 4) for g in range(2)]
        stage = held("stage", [P, (S + H) // 4], I32)
        v2_plane = shifted("v2_plane", S // 4, I32, PLANE_LEAD // 4)
        warm = held("warm", [P, 2], F32)

        def words(ap):
            return ap.rearrange("p t i -> p (t i)").bitcast(I32)

        nc.vector.memset(v_scale_table[:], 0)
        nc.vector.memset(wd_scale_raw[:], 0)
        nc.vector.memset(v2_scale_table[:], 0)
        ws_raw0 = held("ws_raw0", [P, PACK, K_PASS], F32)
        ws_half0 = ws[:, :K_PASS].rearrange("(p j) c -> p j c", j=PACK)
        nc.sync.dma_start(ws_raw0[:, :2, :], ws_half0[:, :2, :])
        wd_raw0 = held("wd_raw0", [P, H // 2], I32)
        wd_raw1 = [held("wd_raw1_%d" % a, [P, K_PASS // 2], I32) for a in range(2)]
        nc.sync.dma_start(v_scale_table[FIRST : FIRST + 64 : SPREAD, :], tab_scales.bitcast(I32).rearrange("g q w -> (g q) w"))
        nc.sync.dma_start(idx[:], offs)
        nc.sync.dma_start(wd_scale_raw[FIRST : FIRST + 64 : SPREAD, :], wd_scales.bitcast(I32).rearrange("g q w -> (g q) w"))
        nc.sync.dma_start(wd_raw0[:], wd_words[0].bitcast(I32))
        nc.sync.dma_start(v2_scale_table[FIRST : FIRST + 64 : SPREAD2, :], tab2_scales[0].bitcast(I32))
        nc.sync.dma_start(idx2[:], offs2)
        v_table = [at(0, "v_table0", [P, T], I32), held("v_table1", [P, T], I32)]
        nc.sync.dma_start(v_table[0][:], words(tab_words[0]))
        safety_sb = held("safety_sb", [P, 2, 2 * PACK], F32)[:, :, :PACK]
        nc.sync.dma_start(safety_sb, safety.rearrange("(a p t) -> p a t", a=2, t=PACK))

        nc.vector.memset(warm[:, 0:1], 0.0)
        nc.scalar.activation(warm[:, 1:2], warm[:, 0:1], ACT.Relu)
        for g in range(2):
            nc.vector.memset(planes[g], 0)
        nc.vector.memset(v2_plane, 0)

        nc.vector.tensor_copy(v_scale_picked[:], v_scale_table[:].bitcast(U8).indirect(idx[:]))
        nc.vector.tensor_copy(
            stage[:, S // 4 :].bitcast(U8).rearrange("p (a t x) -> p a t x", a=2, t=PACK),
            wd_scale_raw[:].bitcast(U8).rearrange("p (a x t) -> p a t x", a=2, t=PACK),
        )
        nc.vector.tensor_copy(stage[:, : S // 4], v_scale_picked[:].bitcast(I32))
        nc.vector.tensor_copy(v2_scale_picked[:], v2_scale_table[:].bitcast(U8).indirect(idx2[:]))

        def move_plane(g):
            for s in range(4):
                sources = slice(FIRST + SPREAD * (BLOCKS * g + s), FIRST + SPREAD * BLOCKS * (g + 1), 4 * SPREAD)
                nc.sync.dma_start(planes[g][s:P:QUADRANT, :], stage[sources, :])

        ws_cols = [[slice(0, K_PASS)], [slice(0, WS_CUT), slice(WS_CUT, K_PASS)]]
        ws_raw = [
            [ws_raw0],
            [held("ws_raw1_%d" % c, [P, PACK, cols.stop - cols.start], F32) for c, cols in enumerate(ws_cols[1])],
        ]

        def load_ws(a):
            half = ws[:, a * K_PASS : (a + 1) * K_PASS].rearrange("(p j) c -> p j c", j=PACK)
            for c, cols in enumerate(ws_cols[a]):
                nc.sync.dma_start(ws_raw[a][c][:], half[:, :, cols])

        def load_wd1(a):
            nc.sync.dma_start(wd_raw1[a][:], wd_words[1].bitcast(I32)[:, a * K_PASS // 2 : (a + 1) * K_PASS // 2])

        nc.sync.dma_start(ws_raw0[:, 2:, :], ws_half0[:, 2:, :])
        move_plane(0)
        v2_table = held("v2_table", [P, T2], I32)
        nc.sync.dma_start(v2_table[:], words(tab2_words[0]))
        nc.sync.dma_start(v_table[1][:, :TAB_CUT], words(tab_words[1])[:, :TAB_CUT])
        for s in range(4):
            nc.sync.dma_start(
                v2_plane[STOCK_ROW + s : P : QUADRANT, :],
                v2_scale_picked[FIRST + SPREAD2 * s : FIRST + SPREAD2 * BLOCKS : 4 * SPREAD2, :].bitcast(I32),
            )
        nc.sync.dma_start(v_table[1][:, TAB_CUT:], words(tab_words[1])[:, TAB_CUT:])
        load_wd1(0)
        move_plane(1)
        load_wd1(1)
        load_ws(1)
        wc_codes = shifted("wc_codes", 2 * N, I32, STATIONARY_LEAD // 4).rearrange("p (a n) -> p a n", a=2)
        base_sb = held("base_sb", [P, N // P], F32)
        nc.sync.dma_start(wc_codes, wc_words.rearrange("a p c i -> p a (c i)").bitcast(I32))
        with nc.allow_non_contiguous_dma(reason="one value of base for each partition"):
            nc.sync.dma_start(base_sb[:], base.rearrange("(i p) -> p i", p=P))

        wd_codes = [
            shifted("wd_codes%d" % g, H, U16, STATIONARY_LEAD // 2).rearrange("p (a t x) -> p a t x", a=2, t=PACK)
            for g in range(2)
        ]
        nc.scalar.copy(wd_codes[0], wd_raw0[:].bitcast(U16).rearrange("p (a x t) -> p a t x", a=2, t=PACK))

        def wd1_sorted(a):
            return wd_codes[1][:, a, :, :], wd_raw1[a][:].bitcast(U16).rearrange("p (x t) -> p t x", t=PACK)

        ws_codes = [
            [shifted("ws_codes%d_%d" % (a, u), 2 * P, U32, STATIONARY_LEAD // 4) for u in range(2)] for a in range(2)
        ]
        ws_planes = [[held("ws_plane%d_%d" % (a, u), [P, 2 * P], U8)[:] for u in range(2)] for a in range(2)]
        ws_bf = [held("ws_bf0", [P, PACK, P, PACK], BF16), at(16, "ws_bf1", [P, PACK, P, PACK], BF16)]

        def round_ws(a, c, on_vector):
            xs = slice(ws_cols[a][c].start // PACK, ws_cols[a][c].stop // PACK)
            dst = ws_bf[a][:, :, xs, :].rearrange("p t x j -> p x j t")
            src = ws_raw[a][c][:].rearrange("p j (x t) -> p x j t", t=PACK)
            if on_vector:
                nc.vector.tensor_scalar(dst, src, -1.0, None, ALU.mult)
            else:
                nc.scalar.activation(dst, src, ACT.Copy, scale=-1.0)

        def quantize_ws(a):
            for u in range(2):
                nc.vector.quantize_mx(
                    out=ws_codes[a][u].bitcast(FP8X4),
                    scales=ws_planes[a][u],
                    in_=ws_bf[a][:, 2 * u : 2 * u + 2, :, :].rearrange("p t x j -> p (t x j)"),
                )

        whole = slice(0, HALF)
        parts = [slice(0, PART), slice(PART, HALF)]

        def queries(qh, cols):
            return slice(qh * HALF + cols.start, qh * HALF + cols.stop)

        def list_cols(qh, cols):
            return slice(queries(qh, cols).start // LIST_ROWS, queries(qh, cols).stop // LIST_ROWS)

        v_codes = [[held("v_codes%d_%d" % (g, qh), [P, HALF], U32) for qh in range(2)] for g in range(2)]
        v2_codes = [held("v2_codes%d" % qh, [P, HALF], U32) for qh in range(2)]

        def gather_v(g, qh, cols):
            nc.vector.tensor_copy(v_codes[g][qh][:, cols], v_table[g][:].bitcast(U32).indirect(idx[:, list_cols(qh, cols)]))

        def gather_v2(qh):
            nc.vector.tensor_copy(v2_codes[qh][:], v2_table[:].bitcast(U32).indirect(idx2[:, list_cols(qh, whole)]))

        plane_bytes = [planes[g].bitcast(U8) for g in range(2)]

        def demand_pass(acc, g, a, t, qh, cols, start, stop):
            wd_col = S + a * K_PASS + t * P
            nc.tensor.matmul_mx(
                out=acc,
                lhsT=wd_codes[g][:, a, t, :].bitcast(U8).bitcast(FP4X4),
                lhsT_scale=plane_bytes[g][:, wd_col : wd_col + P],
                rhs=v_codes[g][qh][:, cols].bitcast(FP8X4),
                rhs_scale=plane_bytes[g][:, queries(qh, cols)],
                start=start,
                stop=stop,
            )

        def stock_pass(acc, a, t, qh, cols, start, stop):
            nc.tensor.matmul_mx(
                out=acc,
                lhsT=ws_codes[a][t // 2][:, t % 2 * P : (t % 2 + 1) * P].bitcast(FP8X4),
                lhsT_scale=ws_planes[a][t // 2][:, t % 2 * P : (t % 2 + 1) * P],
                rhs=v2_codes[qh][:, cols].bitcast(FP8X4),
                rhs_scale=v2_plane[STOCK_ROW:P, :].bitcast(U8)[:, queries(qh, cols)],
                start=start,
                stop=stop,
            )

        def bank(b):
            return psum.tile([P, HALF], F32, name="bank%d" % b)

        rows = {key: held("h_rows%d_%d" % key, [P, PACK, HALF], BF16) for key in ((0, 0), (0, 1), (1, 1))}
        parked = held("parked", [P, PACK, HALF], F32)
        pairs = held("pairs", [P, 2, HALF, 2], BF16)
        tiles = ((0, 0), (0, 1), (1, 0), (1, 1))
        grouped = {key: at(16 + 4 * n, "h_grouped%d_%d" % key, [P, HALF * PACK], BF16) for n, key in enumerate(tiles)}
        h_codes = {key: held("h_codes%d_%d" % key, [P, HALF], U32) for key in tiles}
        h_planes = {key: shifted("h_plane%d_%d" % key, HALF, U8, PLANE_LEAD) for key in tiles}

        def shortage(a, qh, t, acc):
            nc.scalar.activation(rows[a, qh][:, t, :], acc[:], ACT.Relu, bias=safety_sb[:, a, t : t + 1])

        def grouped_cols(a, qh, cols):
            return grouped[a, qh][:, PACK * cols.start : PACK * cols.stop]

        def interleave(a, qh, cols, copy=nc.vector.tensor_copy):
            copy(
                grouped_cols(a, qh, cols).rearrange("p (c i t) -> p c t i", i=4, t=PACK),
                rows[a, qh][:, :, cols].rearrange("p t (c i) -> p c t i", i=4),
            )

        def add_parked(acc, u, cols):
            nc.vector.tensor_tensor(
                pairs[:, u, cols, :],
                acc[:].rearrange("p (e c) -> p c e", e=2),
                parked[:, 2 * u : 2 * u + 2, cols].rearrange("p e c -> p c e"),
                ALU.add,
            )

        def join_pairs(cols):
            nc.vector.tensor_scalar(
                grouped_cols(1, 0, cols).rearrange("p (c u e) -> p c u e", u=2, e=2),
                pairs[:, :, cols, :].rearrange("p u c e -> p c u e"),
                0.0,
                None,
                ALU.max,
            )

        def quantize_h(a, qh, cols):
            nc.vector.quantize_mx(
                out=h_codes[a, qh][:, cols].bitcast(FP8X4),
                scales=h_planes[a, qh][:, cols],
                in_=grouped_cols(a, qh, cols),
            )

        def cost_pass(acc, a, i, qh, cols, start, stop):
            nc.tensor.matmul_mx(
                out=acc,
                lhsT=wc_codes[:, a, i * P : (i + 1) * P].bitcast(FP8X4),
                lhsT_scale=wc_planes[COST_ROW:P, a, :].bitcast(U8)[:, i * P : (i + 1) * P],
                rhs=h_codes[a, qh][:, cols].bitcast(FP8X4),
                rhs_scale=h_planes[a, qh][:, cols],
                start=start,
                stop=stop,
            )

        def add_base(result, acc, i, on_vector):
            if on_vector:
                nc.vector.tensor_scalar(result, acc, base_sb[:, i : i + 1], None, ALU.add)
            else:
                nc.scalar.activation(result, acc, ACT.Identity, bias=base_sb[:, i : i + 1])

        early = [bank(PACK + t) for t in range(PACK)]
        accs = {(0, 0): [bank(t) for t in range(PACK)]}
        gather_v(0, 0, whole)
        round_ws(0, 0, False)
        for t in range(PACK):
            demand_pass(early[t][:], 0, 1, t, 0, whole, True, True)
            nc.scalar.activation(parked[:, t, :], early[t][:], ACT.Identity, bias=safety_sb[:, 1, t : t + 1])
        for t in range(PACK):
            demand_pass(accs[0, 0][t][:], 0, 0, t, 0, whole, True, False)
        gather_v(0, 1, whole)
        accs[0, 1] = [bank(PACK + t) for t in range(PACK)]
        for t in range(PACK):
            demand_pass(accs[0, 1][t][:], 0, 0, t, 1, whole, True, False)
        gather_v2(0)
        quantize_ws(0)
        gather_v2(1)
        wc_planes = at(0, "wc_planes", [P, 2, N // 4], I32)
        nc.vector.memset(wc_planes[:], 0)
        for s in range(4):
            nc.sync.dma_start(
                wc_planes[COST_ROW + s : P : QUADRANT, :, :],
                wc_scales[:, s:BLOCKS:4, :].bitcast(I32).rearrange("a q w -> q a w"),
            )
        for qh in range(2):
            for t in range(PACK):
                stock_pass(accs[0, qh][t][:], 0, t, qh, whole, False, False)
        nc.scalar.copy(*wd1_sorted(0))
        for qh in range(2):
            for cols in parts:
                gather_v(1, qh, cols)
                for t in range(PACK):
                    demand_pass(accs[0, qh][t][:, cols], 1, 0, t, qh, cols, False, cols == parts[1])
                    if cols == parts[1]:
                        shortage(0, qh, t, accs[0, qh][t])
        nc.vector.tensor_copy(*wd1_sorted(1))
        for c in range(2):
            round_ws(1, c, True)
        quantize_ws(1)

        rest = {(n, u): bank(2 * n + u) for n in range(2) for u in range(2)}
        for (n, u), acc in rest.items():
            for e in range(2):
                demand_pass(acc[:, parts[e]], 1, 1, 2 * u + e, 0, parts[n], e == 0, False)
        for (n, u), acc in rest.items():
            for e in range(2):
                stock_pass(acc[:, parts[e]], 1, 2 * u + e, 0, parts[n], False, e == 1)
        interleave(0, 1, parts[1], nc.scalar.copy)

        def last_tile(t):
            acc = bank(PACK + t)
            stock_pass(acc[:], 1, t, 1, whole, True, False)
            for g in range(2):
                demand_pass(acc[:], g, 1, t, 1, whole, False, g == 1)
            shortage(1, 1, t, acc)

        def costs(n, b, apart, on_vector):
            qh, cols = n // 2, parts[n % 2]
            acc = bank(2 * n + b)
            for a in range(2):
                for e in range(2):
                    cost_pass(acc[:, parts[e]], a, 2 * b + e, qh, cols, (a, e) == (0, 0), (a, e) == (1, 1))
            result = outs.tile([P, 2, PART], F32, name="result")
            target = out[2 * b * P : 2 * (b + 1) * P, queries(qh, cols)].rearrange("(e p) c -> p e c", e=2)
            for e in range(2):
                add_base(result[:, e, :], acc[:, parts[e]], 2 * b + e, on_vector)
                if apart:
                    nc.sync.dma_start(target[:, e, :], result[:, e, :])
            if not apart:
                nc.sync.dma_start(target, result[:])

        for t in range(PACK):
            last_tile(t)
        interleave(0, 0, whole)
        add_parked(rest[0, 0], 0, parts[0])
        add_parked(rest[0, 1], 1, parts[0])
        quantize_h(0, 0, whole)
        join_pairs(parts[0])
        add_parked(rest[1, 0], 0, parts[1])
        add_parked(rest[1, 1], 1, parts[1])
        quantize_h(1, 0, parts[0])
        join_pairs(parts[1])
        interleave(0, 1, parts[0])
        quantize_h(1, 0, parts[1])
        interleave(1, 1, parts[0])
        quantize_h(0, 1, parts[0])
        quantize_h(1, 1, parts[0])
        interleave(1, 1, parts[1])
        quantize_h(0, 1, parts[1])
        quantize_h(1, 1, parts[1])

        for n in range(3):
            for b in range(2):
                costs(n, b, (n, b) == (0, 0), (n, b) == (2, 1))

        for i in range(N // P):
            acc = bank((6 + i) % 8)
            for a in range(2):
                cost_pass(acc[:, :PART], a, i, 1, parts[1], a == 0, a == 1)
            result = outs.tile([P, PART], F32, name="last_result")
            on_vector = i % 2 == 1
            add_base(result[:], acc[:, :PART], i, on_vector)
            queue = nc.sync if on_vector else nc.scalar
            queue.dma_start(out[i * P : (i + 1) * P, HALF + PART :], result[:])
